import numpy as np
import ml_dtypes


def mxq(x, axis, fmt="e4m3"):
    dtype, down = {"e4m3": (ml_dtypes.float8_e4m3fn, 7), "e5m2": (ml_dtypes.float8_e5m2, 14)}[fmt]
    v = np.moveaxis(np.asarray(x, np.float32).astype(ml_dtypes.bfloat16).astype(np.float64), axis, -1)
    blocks = v.reshape(v.shape[:-1] + (-1, 32))
    amax = np.abs(blocks).max(-1, keepdims=True)
    byte = np.maximum(np.where(amax > 0, np.frexp(amax)[1] - 1 + 127, 0) - down, 1)
    scale = np.exp2(byte - 127.0)
    codes = (blocks / scale).astype(np.float32).astype(dtype).astype(np.float64)
    return np.moveaxis((codes * scale).reshape(v.shape), -1, axis)


WIDE = False


def mx_kscale(k):
    if not WIDE:
        return np.ones(k)
    levels = np.array([10, -10, 5, -5, 0])
    if k % 512:
        return np.exp2(np.random.permutation(np.resize(levels, k // 32))).repeat(32)
    a = np.empty((k // 512, 16))
    for p in range(k // 512):
        a[p, :8] = np.random.permutation(np.resize(levels, 8))
        for g in range(8):
            far = levels[np.abs(levels - a[p, g]) >= 10]
            a[p, g + 8] = far[np.random.randint(len(far))]
    return np.exp2(a.ravel()).repeat(32)


def f64(x):
    return np.asarray(x).astype(np.float64)


def striped(idx):
    return np.tile(idx.reshape(-1, 16).T, (8, 1)).astype(np.uint16)


def unstriped(offs):
    return offs[:16].T.reshape(-1).astype(np.int64)


def pack_weight(w):
    k, n = w.shape
    w = f64(np.asarray(w, np.float32).astype(ml_dtypes.bfloat16)).reshape(k // 32, 32, n)
    amax = np.abs(w).max(1)
    byte = np.clip(np.where(amax > 0, np.frexp(amax)[1] - 1 + 127 - 7, 1), 1, 254)
    scaled = (w * np.exp2(127.0 - byte)[:, None, :]).reshape(k, n).astype(np.float32)
    words = np.ascontiguousarray(scaled.reshape(k // 512, 128, 4, n).transpose(0, 1, 3, 2)).astype(ml_dtypes.float8_e4m3fn).view(np.uint8)
    return words, np.ascontiguousarray(byte.astype(np.uint8).reshape(k // 512, 16, n))


def unpack_weight(words, scales):
    g, p, n, _ = words.shape
    vals = np.ascontiguousarray(words).view(ml_dtypes.float8_e4m3fn).astype(np.float64) * np.repeat(np.exp2(scales.astype(np.float64) - 127.0), 8, axis=1)[..., None]
    return vals.transpose(0, 1, 3, 2).reshape(g * 512, n)

def planes(y):
    n, m = y.shape
    v = y.astype(np.float32).astype(ml_dtypes.bfloat16).astype(np.float64).reshape(n // 32, 32, m)
    top = np.abs(v).max(1)
    byte = np.clip(np.where(top > 0, np.frexp(top)[1] - 1 + 127 - 7, 1), 1, 254)
    codes = (v * np.exp2(127.0 - byte)[:, None, :]).reshape(n, m).astype(np.float32).astype(ml_dtypes.float8_e4m3fn).view(np.uint8)
    words = codes.reshape(n // 512, 128, 4, m).transpose(0, 1, 3, 2)
    return np.ascontiguousarray(words), np.ascontiguousarray(byte.astype(np.uint8).reshape(n // 512, 16, m))


K, T, N = 512, 512, 512
P = 2 ** 7


def setup_inputs():
    n = np.random.standard_normal
    s = mx_kscale(K)[:, None]
    packed_xT = pack_weight(n((K, T)) * s)
    return {
        "x_words": packed_xT[0],
        "x_scales": packed_xT[1],
        "w1": (n((K, N)) / np.sqrt(K) / s).astype(np.float32),
        "bound": np.tile(np.random.uniform(0.3, 1.2, T), (P, 1)).astype(np.float32),
        "pos1": striped(np.random.permutation(T)),
        "pos2": striped(np.random.permutation(T)),
        "pos3": striped(np.random.permutation(T)),
        "pos4": striped(np.random.permutation(T)),
    }


def reference(x_words, x_scales, w1, bound, pos1, pos2, pos3, pos4):
    xq = unpack_weight(x_words, x_scales)
    y = mxq(f64(w1), 0, "e4m3").T @ xq
    low = -1.0 * f64(bound)[:1]
    out_0 = y + (np.maximum(np.minimum(y[:, unstriped(pos1)] - y, f64(bound)[:1]), low) + np.maximum(np.minimum(y[:, unstriped(pos2)] - y, f64(bound)[:1]), low) + np.maximum(np.minimum(y[:, unstriped(pos3)] - y, f64(bound)[:1]), low) + np.maximum(np.minimum(y[:, unstriped(pos4)] - y, f64(bound)[:1]), low)) / 4
    return (out_0,) + planes(out_0)

@@ -1,0 +1,204 @@
+from contextlib import ExitStack
+
+import concourse.mybir as mybir
+from concourse.masks import make_identity
+
+K, T, N = 512, 512, 512
+D = 4
+P = 128
+PACK = 4
+FLOPS = 2 * K * T * N
+
+F32 = mybir.dt.float32
+BF16 = mybir.dt.bfloat16
+I32 = mybir.dt.int32
+U32 = mybir.dt.uint32
+U16 = mybir.dt.uint16
+U8 = mybir.dt.uint8
+FP8X4 = mybir.dt.float8_e4m3fn_x4
+ALU = mybir.AluOpType
+
+
+def tile_picked_whuber_none_lo_kernel(
+    tc, x_words, x_scales, w1, bound, pos1, pos2, pos3, pos4, out_0, out_1, out_2
+):
+    nc = tc.nc
+    blocks = T // P
+
+    with ExitStack() as ctx:
+        keep = ctx.enter_context(tc.tile_pool(name="keep", bufs=1))
+        psum = ctx.enter_context(tc.psum_pool(name="psum", bufs=1))
+
+        def bank(b, name):
+            return psum.tile([P, 4, P], F32, name=name, tag="bank%d" % b)
+
+        w_raw = keep.tile([P, PACK, N], F32, name="w_raw")
+        nc.sync.dma_start(out=w_raw[:], in_=w1.rearrange("(p j) n -> p j n", j=PACK))
+        x_codes = keep.tile([P, T], U32, name="x_codes", align_bytes=64)
+        nc.sync.dma_start(
+            out=x_codes[:].bitcast(I32),
+            in_=x_words[0].rearrange("p c r -> p (c r)").bitcast(I32),
+        )
+        x_plane = keep.tile([P, T], U8, name="x_plane", align_bytes=64)
+        nc.vector.memset(x_plane[:].bitcast(I32), 0)
+        for q in range(4):
+            nc.scalar.dma_start(
+                out=x_plane[32 * q : 32 * q + 4, :].bitcast(I32),
+                in_=x_scales[0, 4 * q : 4 * q + 4, :].bitcast(I32),
+            )
+        lists = []
+        for d, pos in enumerate((pos1, pos2, pos3, pos4)):
+            tile = keep.tile([P, T // 16], U16, name="list%d" % d)
+            nc.sync.dma_start(tile[:], pos)
+            lists.append(tile)
+            if d == 0:
+                b_rows = keep.tile([P, P], F32, name="b_rows")
+                nc.sync.dma_start(
+                    out=b_rows[:],
+                    in_=bound.rearrange("p (c v) -> (p c) v", c=blocks)[0:P, :],
+                )
+
+        ident = keep.tile([P, P], F32, name="ident")
+        make_identity(nc, ident[:])
+
+        b_ps = bank(4, "b_ps")
+        nc.tensor.transpose(b_ps[:, 0, :], b_rows[:], ident[:])
+        b_hi = keep.tile([P, 8], F32, name="b_hi")
+        nc.scalar.copy(out=b_hi[:], in_=b_ps[:, 0, 0:8])
+        b_lo = keep.tile([P, 8], F32, name="b_lo")
+        nc.gpsimd.tensor_scalar(b_lo[:], b_hi[:], -1.0, 0.0, ALU.mult, ALU.add)
+
+        w_src = w_raw[:].rearrange("p j (m t) -> p t m j", t=PACK)
+        w_codes = keep.tile([P, N], U32, name="w_codes", align_bytes=64)
+        w_plane = keep.tile([P, N], U8, name="w_plane", align_bytes=64)
+        w_first = keep.tile([P, P, PACK], BF16, name="w_first", align_bytes=64)
+        nc.vector.tensor_copy(out=w_first[:], in_=w_src[:, 0])
+        nc.vector.quantize_mx(
+            out=w_codes[:, 0:P].bitcast(FP8X4),
+            scales=w_plane[:, 0:P],
+            in_=w_first[:].rearrange("p m j -> p (m j)"),
+        )
+        w_rest = keep.tile([P, 3, P, PACK], BF16, name="w_rest", align_bytes=64)
+        nc.vector.tensor_copy(
+            out=w_rest[:].rearrange("p t m j -> p m t j"),
+            in_=w_src[:, 1:4].rearrange("p t m j -> p m t j"),
+        )
+        w_flat = w_rest[:].rearrange("p t m j -> p (t m j)")
+        nc.vector.quantize_mx(
+            out=w_codes[:, P : 2 * P].bitcast(FP8X4),
+            scales=w_plane[:, P : 2 * P],
+            in_=w_flat[:, 0:512],
+        )
+        nc.vector.quantize_mx(
+            out=w_codes[:, 2 * P : 4 * P].bitcast(FP8X4),
+            scales=w_plane[:, 2 * P : 4 * P],
+            in_=w_flat[:, 512:1536],
+        )
+
+        y = keep.tile([P, PACK, T], F32, name="y")
+        y_neg = []
+        for t in range(PACK):
+            y_ps = bank(t, "y_ps%d" % t)
+            y_flat = y_ps[:].rearrange("p a b -> p (a b)")
+            nc.tensor.matmul_mx(
+                out=y_flat,
+                lhsT=w_codes[:, t * P : (t + 1) * P].bitcast(FP8X4),
+                lhsT_scale=w_plane[:, t * P : (t + 1) * P],
+                rhs=x_codes[:].bitcast(FP8X4),
+                rhs_scale=x_plane[:],
+                start=True,
+                stop=True,
+            )
+            nc.scalar.copy(out=y[:, t, :], in_=y_flat)
+            neg = keep.tile([P, T], F32, name="y_neg%d" % t)
+            nc.gpsimd.tensor_scalar(neg[:], y[:, t, :], -1.0, 0.0, ALU.mult, ALU.add)
+            y_neg.append(neg)
+
+        o_codes = keep.tile([P, T], U32, name="o_codes", align_bytes=64)
+        o_plane = keep.tile([P, T], U8, name="o_plane", align_bytes=64)
+        out_rows = out_0.rearrange("(p t) v -> p t v", t=PACK)
+        out_words = out_1[0].rearrange("p c r -> p (c r)").bitcast(I32)
+
+        UNITS = [(t, (0, 1), False) for t in range(4)] + [(t, (2, 3), False) for t in range(3)] + [(3, (2,), False), (3, (3,), True)]
+        turn = 0
+        acc = {}
+        for t, vbs, on_vector in UNITS:
+            width = P * len(vbs)
+            c0 = P * vbs[0]
+            pulls = {}
+            for vb in vbs:
+                pull = bank(4 + turn % 4, "pull%d_%d" % (t, vb))
+                turn = turn + 1
+                pulls[vb] = pull
+                for d in range(D):
+                    nc.tensor.matmul(
+                        pull[:, d, :],
+                        lhsT=y_neg[t][:, vb * P : (vb + 1) * P],
+                        rhs=ident[:],
+                        start=(d == 0),
+                        stop=False,
+                        is_transpose=True,
+                    )
+            for d in range(D):
+                picked = keep.tile([P, width], F32, name="picked%d_%d_%d" % (t, vbs[0], d))
+                nc.vector.tensor_copy(
+                    picked[:],
+                    y[:, t, :].indirect(lists[d][:, c0 // 16 : (c0 + width) // 16]),
+                )
+                for i, vb in enumerate(vbs):
+                    nc.tensor.matmul(
+                        pulls[vb][:, d, :],
+                        lhsT=picked[:, i * P : (i + 1) * P],
+                        rhs=ident[:],
+                        start=False,
+                        stop=(d == D - 1),
+                        is_transpose=True,
+                    )
+            for vb in vbs:
+                clipped = keep.tile([P, D, P], F32, name="clipped%d_%d" % (t, vb))
+                if on_vector:
+                    nc.vector.tensor_scalar(
+                        clipped[:], pulls[vb][:], b_hi[:, vb : vb + 1], b_lo[:, vb : vb + 1], ALU.min, ALU.max
+                    )
+                else:
+                    raw = keep.tile([P, D, P], F32, name="raw%d_%d" % (t, vb))
+                    nc.scalar.copy(out=raw[:], in_=pulls[vb][:])
+                    nc.gpsimd.tensor_scalar(
+                        clipped[:], raw[:], b_hi[:, vb : vb + 1], b_lo[:, vb : vb + 1], ALU.min, ALU.max
+                    )
+                if t == 0:
+                    acc[vb] = bank(vb, "acc%d" % vb)
+                for d in range(D):
+                    nc.tensor.matmul(
+                        acc[vb][:, t, :],
+                        lhsT=clipped[:, d, :],
+                        rhs=ident[:],
+                        start=(t == 0 and d == 0),
+                        stop=(t == PACK - 1 and d == D - 1),
+                        is_transpose=True,
+                    )
+                if t == PACK - 1:
+                    cols = slice(vb * P, (vb + 1) * P)
+                    res = keep.tile([P, PACK, P], F32, name="res%d" % vb)
+                    nc.vector.scalar_tensor_tensor(
+                        res[:], acc[vb][:], 1.0 / D, y[:, :, cols], ALU.mult, ALU.add
+                    )
+                    nc.sync.dma_start(out=out_rows[:, :, cols], in_=res[:])
+                    rounded = keep.tile([P, P, PACK], BF16, name="rounded%d" % vb, align_bytes=64)
+                    if vb == blocks - 1:
+                        nc.vector.tensor_copy(out=rounded[:], in_=res[:].rearrange("p t v -> p v t"))
+                    else:
+                        nc.scalar.copy(out=rounded[:], in_=res[:].rearrange("p t v -> p v t"))
+                    nc.vector.quantize_mx(
+                        out=o_codes[:, cols].bitcast(FP8X4),
+                        scales=o_plane[:, cols],
+                        in_=rounded[:].rearrange("p v t -> p (v t)"),
+                    )
+                    nc.scalar.dma_start(out=out_words[:, cols], in_=o_codes[:, cols].bitcast(I32))
+
+        for q in range(4):
+            queue = nc.sync if q % 2 == 0 else nc.scalar
+            queue.dma_start(
+                out=out_2[0, 4 * q : 4 * q + 4, :].bitcast(I32),
+                in_=o_plane[32 * q : 32 * q + 4, :].bitcast(I32),
+            )

@@ -7,6 +7,12 @@ K, T, N = 512, 512, 512
 D = 4
 P = 128
 PACK = 4
+CLIP = "sssssssssssssvvv"
+NEG = "ssss"
+FILL = [4,1,1,1,4,4,4]
+LAG = 4
+ROUND = "sssv"
+LATE = 8
 FLOPS = 2 * K * T * N
 
 F32 = mybir.dt.float32
@@ -17,6 +23,7 @@ U16 = mybir.dt.uint16
 U8 = mybir.dt.uint8
 FP8X4 = mybir.dt.float8_e4m3fn_x4
 ALU = mybir.AluOpType
+ACT = mybir.ActivationFunctionType
 
 
 def tile_picked_whuber_none_lo_kernel(
@@ -40,7 +47,7 @@ def tile_picked_whuber_none_lo_kernel(
             in_=x_words[0].rearrange("p c r -> p (c r)").bitcast(I32),
         )
         x_plane = keep.tile([P, T], U8, name="x_plane", align_bytes=64)
-        nc.vector.memset(x_plane[:].bitcast(I32), 0)
+        nc.gpsimd.memset(x_plane[:].bitcast(I32), 0)
         for q in range(4):
             nc.scalar.dma_start(
                 out=x_plane[32 * q : 32 * q + 4, :].bitcast(I32),
@@ -61,12 +68,12 @@ def tile_picked_whuber_none_lo_kernel(
         ident = keep.tile([P, P], F32, name="ident")
         make_identity(nc, ident[:])
 
-        b_ps = bank(4, "b_ps")
+        b_ps = bank(5, "b_ps")
         nc.tensor.transpose(b_ps[:, 0, :], b_rows[:], ident[:])
-        b_hi = keep.tile([P, 8], F32, name="b_hi")
-        nc.scalar.copy(out=b_hi[:], in_=b_ps[:, 0, 0:8])
-        b_lo = keep.tile([P, 8], F32, name="b_lo")
-        nc.gpsimd.tensor_scalar(b_lo[:], b_hi[:], -1.0, 0.0, ALU.mult, ALU.add)
+        b_cols = keep.tile([P, 4, 8], F32, name="b_cols")
+        for i, factor in enumerate((1.0, -1.0, 2.0, -float(D))):
+            nc.scalar.activation(b_cols[:, i, :], b_ps[:, 0, 0:8], ACT.Copy, scale=factor)
+        b_hi, b_lo, b_two, b_off = (b_cols[:, i, :] for i in range(4))
 
         w_src = w_raw[:].rearrange("p j (m t) -> p t m j", t=PACK)
         w_codes = keep.tile([P, N], U32, name="w_codes", align_bytes=64)
@@ -78,30 +85,30 @@ def tile_picked_whuber_none_lo_kernel(
             scales=w_plane[:, 0:P],
             in_=w_first[:].rearrange("p m j -> p (m j)"),
         )
-        w_rest = keep.tile([P, 3, P, PACK], BF16, name="w_rest", align_bytes=64)
+        w_mid = keep.tile([P, 2, P, PACK], BF16, name="w_mid", align_bytes=64)
         nc.vector.tensor_copy(
-            out=w_rest[:].rearrange("p t m j -> p m t j"),
-            in_=w_src[:, 1:4].rearrange("p t m j -> p m t j"),
-        )
-        w_flat = w_rest[:].rearrange("p t m j -> p (t m j)")
-        nc.vector.quantize_mx(
-            out=w_codes[:, P : 2 * P].bitcast(FP8X4),
-            scales=w_plane[:, P : 2 * P],
-            in_=w_flat[:, 0:512],
+            out=w_mid[:].rearrange("p t m j -> p m t j"),
+            in_=w_src[:, 1:3].rearrange("p t m j -> p m t j"),
         )
         nc.vector.quantize_mx(
-            out=w_codes[:, 2 * P : 4 * P].bitcast(FP8X4),
-            scales=w_plane[:, 2 * P : 4 * P],
-            in_=w_flat[:, 512:1536],
+            out=w_codes[:, P : 3 * P].bitcast(FP8X4),
+            scales=w_plane[:, P : 3 * P],
+            in_=w_mid[:].rearrange("p t m j -> p (t m j)"),
+        )
+        w_last = keep.tile([P, P, PACK], BF16, name="w_last", align_bytes=64)
+        nc.scalar.copy(out=w_last[:], in_=w_src[:, 3])
+        nc.vector.quantize_mx(
+            out=w_codes[:, 3 * P : 4 * P].bitcast(FP8X4),
+            scales=w_plane[:, 3 * P : 4 * P],
+            in_=w_last[:].rearrange("p m j -> p (m j)"),
         )
 
         y = keep.tile([P, PACK, T], F32, name="y")
-        y_neg = []
-        for t in range(PACK):
-            y_ps = bank(t, "y_ps%d" % t)
-            y_flat = y_ps[:].rearrange("p a b -> p (a b)")
+        y_neg = {}
+
+        def product(t, target):
             nc.tensor.matmul_mx(
-                out=y_flat,
+                out=target[:].rearrange("p a b -> p (a b)"),
                 lhsT=w_codes[:, t * P : (t + 1) * P].bitcast(FP8X4),
                 lhsT_scale=w_plane[:, t * P : (t + 1) * P],
                 rhs=x_codes[:].bitcast(FP8X4),
@@ -109,92 +116,132 @@ def tile_picked_whuber_none_lo_kernel(
                 start=True,
                 stop=True,
             )
-            nc.scalar.copy(out=y[:, t, :], in_=y_flat)
-            neg = keep.tile([P, T], F32, name="y_neg%d" % t)
-            nc.gpsimd.tensor_scalar(neg[:], y[:, t, :], -1.0, 0.0, ALU.mult, ALU.add)
-            y_neg.append(neg)
+
+        def bring_out(t, source):
+            nc.scalar.copy(out=y[:, t, :], in_=source[:].rearrange("p a b -> p (a b)"))
+            y_neg[t] = keep.tile([P, T], F32, name="y_neg%d" % t)
+            if NEG[t] == "s":
+                nc.scalar.activation(y_neg[t][:], y[:, t, :], ACT.Copy, scale=-1.0)
+            else:
+                nc.gpsimd.tensor_scalar(y_neg[t][:], y[:, t, :], -1.0, 0.0, ALU.mult, ALU.add)
+
+        def turn_into(target, source, start, stop):
+            nc.tensor.matmul(target, lhsT=source, rhs=ident[:], start=start, stop=stop, is_transpose=True)
+
+        zeros = keep.tile([P, P], F32, name="zeros")
+        nc.gpsimd.memset(zeros[:], 0.0)
 
         o_codes = keep.tile([P, T], U32, name="o_codes", align_bytes=64)
         o_plane = keep.tile([P, T], U8, name="o_plane", align_bytes=64)
         out_rows = out_0.rearrange("(p t) v -> p t v", t=PACK)
         out_words = out_1[0].rearrange("p c r -> p (c r)").bitcast(I32)
 
-        UNITS = [(t, (0, 1), False) for t in range(4)] + [(t, (2, 3), False) for t in range(3)] + [(3, (2,), False), (3, (3,), True)]
-        turn = 0
+        steps = [(t, vb) for t in range(PACK) for vb in range(blocks)]
+        pulls = {}
+        clipped = {}
         acc = {}
-        for t, vbs, on_vector in UNITS:
-            width = P * len(vbs)
-            c0 = P * vbs[0]
-            pulls = {}
-            for vb in vbs:
-                pull = bank(4 + turn % 4, "pull%d_%d" % (t, vb))
-                turn = turn + 1
-                pulls[vb] = pull
-                for d in range(D):
-                    nc.tensor.matmul(
-                        pull[:, d, :],
-                        lhsT=y_neg[t][:, vb * P : (vb + 1) * P],
-                        rhs=ident[:],
-                        start=(d == 0),
-                        stop=False,
-                        is_transpose=True,
-                    )
+
+        def seed(i):
+            if i >= len(steps):
+                return
+            t, vb = steps[i]
+            if i == LATE:
+                product(0, bank(4 + i % 4, "again"))
+            pulls[i] = bank(4 + i % 4, "pull%d" % i)
             for d in range(D):
-                picked = keep.tile([P, width], F32, name="picked%d_%d_%d" % (t, vbs[0], d))
-                nc.vector.tensor_copy(
-                    picked[:],
-                    y[:, t, :].indirect(lists[d][:, c0 // 16 : (c0 + width) // 16]),
+                turn_into(pulls[i][:, d, :], y_neg[t][:, vb * P : (vb + 1) * P], d == 0, False)
+
+        def gather(i, count, d, idle=0):
+            t, vb = steps[i]
+            picked = keep.tile([P, count * P], F32, name="picked%d_%d" % (i, d))
+            nc.vector.tensor_copy(
+                picked[:], y[:, t, :].indirect(lists[d][:, vb * P // 16 : (vb + count) * P // 16])
+            )
+            for e in range(count):
+                turn_into(pulls[i + e][:, d, :], picked[:, e * P : (e + 1) * P], False, d == D - 1)
+            for f in range(idle):
+                turn_into(pulls[i][:, d, :], zeros[:], False, False)
+
+        def clip(i):
+            t, vb = steps[i]
+            clipped[i] = keep.tile([P, D, P], F32, name="clipped%d" % i)
+            if CLIP[i] == "v":
+                nc.vector.tensor_scalar(
+                    clipped[i][:], pulls[i][:], b_hi[:, vb : vb + 1], b_lo[:, vb : vb + 1], ALU.min, ALU.max
                 )
-                for i, vb in enumerate(vbs):
-                    nc.tensor.matmul(
-                        pulls[vb][:, d, :],
-                        lhsT=picked[:, i * P : (i + 1) * P],
-                        rhs=ident[:],
-                        start=False,
-                        stop=(d == D - 1),
-                        is_transpose=True,
-                    )
-            for vb in vbs:
-                clipped = keep.tile([P, D, P], F32, name="clipped%d_%d" % (t, vb))
-                if on_vector:
-                    nc.vector.tensor_scalar(
-                        clipped[:], pulls[vb][:], b_hi[:, vb : vb + 1], b_lo[:, vb : vb + 1], ALU.min, ALU.max
-                    )
+                return
+            raw = keep.tile([P, D, P], F32, name="raw%d" % i)
+            if CLIP[i] == "g":
+                nc.scalar.copy(out=raw[:], in_=pulls[i][:])
+                nc.gpsimd.tensor_scalar(
+                    clipped[i][:], raw[:], b_hi[:, vb : vb + 1], b_lo[:, vb : vb + 1], ALU.min, ALU.max
+                )
+                return
+            nc.scalar.activation(raw[:], pulls[i][:], ACT.Relu, bias=b_hi[:, vb : vb + 1], scale=-1.0)
+            nc.scalar.activation(clipped[i][:], raw[:], ACT.Relu, bias=b_two[:, vb : vb + 1], scale=-1.0)
+
+        def add_up(i):
+            if i < 0:
+                return
+            t, vb = steps[i]
+            if t == 0:
+                acc[vb] = bank(vb, "acc%d" % vb)
+            offset = CLIP[i] == "s"
+            for d in range(D):
+                turn_into(acc[vb][:, t, :], clipped[i][:, d, :], t == 0 and d == 0, t == PACK - 1 and d == D - 1)
+                if offset and d == 0:
+                    turn_into(acc[vb][:, t, :], b_off[:, vb : vb + 1].to_broadcast([P, P]), False, False)
+            if t == PACK - 1:
+                cols = slice(vb * P, (vb + 1) * P)
+                res = keep.tile([P, PACK, P], F32, name="res%d" % vb)
+                nc.vector.scalar_tensor_tensor(res[:], acc[vb][:], 1.0 / D, y[:, :, cols], ALU.mult, ALU.add)
+                nc.sync.dma_start(out=out_rows[:, :, cols], in_=res[:])
+                rounded = keep.tile([P, P, PACK], BF16, name="rounded%d" % vb, align_bytes=64)
+                if ROUND[vb] == "s":
+                    nc.scalar.copy(out=rounded[:], in_=res[:].rearrange("p t v -> p v t"))
                 else:
-                    raw = keep.tile([P, D, P], F32, name="raw%d_%d" % (t, vb))
-                    nc.scalar.copy(out=raw[:], in_=pulls[vb][:])
-                    nc.gpsimd.tensor_scalar(
-                        clipped[:], raw[:], b_hi[:, vb : vb + 1], b_lo[:, vb : vb + 1], ALU.min, ALU.max
-                    )
-                if t == 0:
-                    acc[vb] = bank(vb, "acc%d" % vb)
-                for d in range(D):
-                    nc.tensor.matmul(
-                        acc[vb][:, t, :],
-                        lhsT=clipped[:, d, :],
-                        rhs=ident[:],
-                        start=(t == 0 and d == 0),
-                        stop=(t == PACK - 1 and d == D - 1),
-                        is_transpose=True,
-                    )
-                if t == PACK - 1:
-                    cols = slice(vb * P, (vb + 1) * P)
-                    res = keep.tile([P, PACK, P], F32, name="res%d" % vb)
-                    nc.vector.scalar_tensor_tensor(
-                        res[:], acc[vb][:], 1.0 / D, y[:, :, cols], ALU.mult, ALU.add
-                    )
-                    nc.sync.dma_start(out=out_rows[:, :, cols], in_=res[:])
-                    rounded = keep.tile([P, P, PACK], BF16, name="rounded%d" % vb, align_bytes=64)
-                    if vb == blocks - 1:
-                        nc.vector.tensor_copy(out=rounded[:], in_=res[:].rearrange("p t v -> p v t"))
-                    else:
-                        nc.scalar.copy(out=rounded[:], in_=res[:].rearrange("p t v -> p v t"))
-                    nc.vector.quantize_mx(
-                        out=o_codes[:, cols].bitcast(FP8X4),
-                        scales=o_plane[:, cols],
-                        in_=rounded[:].rearrange("p v t -> p (v t)"),
-                    )
-                    nc.scalar.dma_start(out=out_words[:, cols], in_=o_codes[:, cols].bitcast(I32))
+                    nc.vector.tensor_copy(out=rounded[:], in_=res[:].rearrange("p t v -> p v t"))
+                nc.vector.quantize_mx(
+                    out=o_codes[:, cols].bitcast(FP8X4),
+                    scales=o_plane[:, cols],
+                    in_=rounded[:].rearrange("p v t -> p (v t)"),
+                )
+                nc.sync.dma_start(out=out_words[:, cols], in_=o_codes[:, cols].bitcast(I32))
+
+        y_ps = [bank(t, "y_ps%d" % t) for t in range(PACK)]
+        for t in range(PACK):
+            product(t, y_ps[t])
+            bring_out(t, y_ps[t])
+        early = bank(4, "early")
+        for f in range(FILL[0]):
+            turn_into(early[:, f % 4, :], y[:, 0, 0:P], True, True)
+        seed(0)
+        seed(1)
+        for u in range(7):
+            i = 2 * u
+            idle = FILL[1 + 3 * u : 4 + 3 * u] if u < 2 else (0, 0, 0)
+            add_up(i - LAG)
+            gather(i, 2, 0, idle[0])
+            add_up(i - LAG + 1)
+            gather(i, 2, 1, idle[1])
+            seed(i + 2)
+            gather(i, 2, 2, idle[2])
+            seed(i + 3)
+            gather(i, 2, 3)
+            clip(i)
+            clip(i + 1)
+        add_up(10)
+        for d in range(D):
+            gather(14, 1, d)
+        clip(14)
+        add_up(11)
+        for d in range(D - 1):
+            gather(15, 1, d)
+        add_up(12)
+        gather(15, 1, D - 1)
+        clip(15)
+        for i in (13, 14, 15):
+            add_up(i)
 
         for q in range(4):
             queue = nc.sync if q % 2 == 0 else nc.scalar

@@ -7,12 +7,7 @@ K, T, N = 512, 512, 512
 D = 4
 P = 128
 PACK = 4
-CLIP = "sssssssssssssvvv"
-NEG = "ssss"
-FILL = [4,1,1,1,4,4,4]
-LAG = 4
-ROUND = "sssv"
-LATE = 8
+RING = 4
 FLOPS = 2 * K * T * N
 
 F32 = mybir.dt.float32
@@ -53,195 +48,205 @@ def tile_picked_whuber_none_lo_kernel(
                 out=x_plane[32 * q : 32 * q + 4, :].bitcast(I32),
                 in_=x_scales[0, 4 * q : 4 * q + 4, :].bitcast(I32),
             )
+        b_rows = keep.tile([P, P], F32, name="b_rows")
+        nc.gpsimd.memset(b_rows[:], 0.0)
         lists = []
         for d, pos in enumerate((pos1, pos2, pos3, pos4)):
             tile = keep.tile([P, T // 16], U16, name="list%d" % d)
             nc.sync.dma_start(tile[:], pos)
             lists.append(tile)
-            if d == 0:
-                b_rows = keep.tile([P, P], F32, name="b_rows")
-                nc.sync.dma_start(
-                    out=b_rows[:],
-                    in_=bound.rearrange("p (c v) -> (p c) v", c=blocks)[0:P, :],
-                )
+        nc.sync.dma_start(
+            out=b_rows[0:blocks, :],
+            in_=bound[0:1, :].rearrange("o (c v) -> (o c) v", c=blocks),
+        )
 
         ident = keep.tile([P, P], F32, name="ident")
         make_identity(nc, ident[:])
 
-        b_ps = bank(5, "b_ps")
+        b_ps = bank(7, "b_ps")
         nc.tensor.transpose(b_ps[:, 0, :], b_rows[:], ident[:])
-        b_cols = keep.tile([P, 4, 8], F32, name="b_cols")
-        for i, factor in enumerate((1.0, -1.0, 2.0, -float(D))):
+        b_cols = keep.tile([P, 5, 8], F32, name="b_cols")
+        for i, factor in enumerate((1.0, -1.0, 2.0, -float(D), -2.0)):
             nc.scalar.activation(b_cols[:, i, :], b_ps[:, 0, 0:8], ACT.Copy, scale=factor)
-        b_hi, b_lo, b_two, b_off = (b_cols[:, i, :] for i in range(4))
+        b_hi, b_lo, b_two, b_off, b_half = (b_cols[:, i, :] for i in range(5))
 
         w_src = w_raw[:].rearrange("p j (m t) -> p t m j", t=PACK)
         w_codes = keep.tile([P, N], U32, name="w_codes", align_bytes=64)
         w_plane = keep.tile([P, N], U8, name="w_plane", align_bytes=64)
-        w_first = keep.tile([P, P, PACK], BF16, name="w_first", align_bytes=64)
-        nc.vector.tensor_copy(out=w_first[:], in_=w_src[:, 0])
-        nc.vector.quantize_mx(
-            out=w_codes[:, 0:P].bitcast(FP8X4),
-            scales=w_plane[:, 0:P],
-            in_=w_first[:].rearrange("p m j -> p (m j)"),
+        w_one = keep.tile([P, P, PACK], BF16, name="w_one", align_bytes=64)
+        w_two = keep.tile([P, 2, P, PACK], BF16, name="w_two", align_bytes=64)
+        nc.scalar.copy(
+            out=w_two[:].rearrange("p t m j -> p m t j"),
+            in_=w_src[:, 2:4].rearrange("p t m j -> p m t j"),
         )
-        w_mid = keep.tile([P, 2, P, PACK], BF16, name="w_mid", align_bytes=64)
-        nc.vector.tensor_copy(
-            out=w_mid[:].rearrange("p t m j -> p m t j"),
-            in_=w_src[:, 1:3].rearrange("p t m j -> p m t j"),
-        )
+        for t in range(2):
+            nc.vector.tensor_copy(out=w_one[:], in_=w_src[:, t])
+            nc.vector.quantize_mx(
+                out=w_codes[:, t * P : (t + 1) * P].bitcast(FP8X4),
+                scales=w_plane[:, t * P : (t + 1) * P],
+                in_=w_one[:].rearrange("p m j -> p (m j)"),
+            )
         nc.vector.quantize_mx(
-            out=w_codes[:, P : 3 * P].bitcast(FP8X4),
-            scales=w_plane[:, P : 3 * P],
-            in_=w_mid[:].rearrange("p t m j -> p (t m j)"),
-        )
-        w_last = keep.tile([P, P, PACK], BF16, name="w_last", align_bytes=64)
-        nc.scalar.copy(out=w_last[:], in_=w_src[:, 3])
-        nc.vector.quantize_mx(
-            out=w_codes[:, 3 * P : 4 * P].bitcast(FP8X4),
-            scales=w_plane[:, 3 * P : 4 * P],
-            in_=w_last[:].rearrange("p m j -> p (m j)"),
+            out=w_codes[:, 2 * P : 4 * P].bitcast(FP8X4),
+            scales=w_plane[:, 2 * P : 4 * P],
+            in_=w_two[:].rearrange("p t m j -> p (t m j)"),
         )
 
-        y = keep.tile([P, PACK, T], F32, name="y")
-        y_neg = {}
+        y_win = [keep.tile([P, T], F32, name="y_win%d" % t) for t in range(PACK)]
+        y_own = keep.tile([P, PACK, T], F32, name="y_own")
+        half = T // 2
 
-        def product(t, target):
+        def product(t, target, cols):
             nc.tensor.matmul_mx(
-                out=target[:].rearrange("p a b -> p (a b)"),
+                out=target,
                 lhsT=w_codes[:, t * P : (t + 1) * P].bitcast(FP8X4),
                 lhsT_scale=w_plane[:, t * P : (t + 1) * P],
-                rhs=x_codes[:].bitcast(FP8X4),
-                rhs_scale=x_plane[:],
+                rhs=x_codes[:, cols].bitcast(FP8X4),
+                rhs_scale=x_plane[:, cols],
                 start=True,
                 stop=True,
             )
 
-        def bring_out(t, source):
-            nc.scalar.copy(out=y[:, t, :], in_=source[:].rearrange("p a b -> p (a b)"))
-            y_neg[t] = keep.tile([P, T], F32, name="y_neg%d" % t)
-            if NEG[t] == "s":
-                nc.scalar.activation(y_neg[t][:], y[:, t, :], ACT.Copy, scale=-1.0)
+        for h in range(2):
+            cols = slice(h * half, (h + 1) * half)
+            y_ps = bank(4 * h, "y_half%d" % h)
+            flat = y_ps[:].rearrange("p a b -> p (a b)")[:, 0:half]
+            product(0, flat, cols)
+            nc.scalar.copy(out=y_win[0][:, cols], in_=flat)
+            if h == 0:
+                nc.vector.tensor_copy(out=y_own[:, 0, cols], in_=flat)
+        nc.sync.dma_start(out=y_own[:, 0, half:T], in_=y_win[0][:, half:T])
+        for t in range(1, PACK):
+            y_ps = bank(t, "y_ps%d" % t)
+            flat = y_ps[:].rearrange("p a b -> p (a b)")
+            product(t, flat, slice(0, T))
+            nc.scalar.copy(out=y_win[t][:], in_=flat)
+            if t == 1:
+                nc.scalar.copy(out=y_own[:, t, 0:half], in_=flat[:, 0:half])
+                nc.sync.dma_start(out=y_own[:, t, half:T], in_=y_win[t][:, half:T])
             else:
-                nc.gpsimd.tensor_scalar(y_neg[t][:], y[:, t, :], -1.0, 0.0, ALU.mult, ALU.add)
+                nc.sync.dma_start(out=y_own[:, t, :], in_=y_win[t][:])
 
         def turn_into(target, source, start, stop):
             nc.tensor.matmul(target, lhsT=source, rhs=ident[:], start=start, stop=stop, is_transpose=True)
-
-        zeros = keep.tile([P, P], F32, name="zeros")
-        nc.gpsimd.memset(zeros[:], 0.0)
 
         o_codes = keep.tile([P, T], U32, name="o_codes", align_bytes=64)
         o_plane = keep.tile([P, T], U8, name="o_plane", align_bytes=64)
         out_rows = out_0.rearrange("(p t) v -> p t v", t=PACK)
         out_words = out_1[0].rearrange("p c r -> p (c r)").bitcast(I32)
 
-        steps = [(t, vb) for t in range(PACK) for vb in range(blocks)]
+        ring = [keep.tile([P, 2 * P], F32, name="ring%d" % i) for i in range(RING)]
         pulls = {}
         clipped = {}
         acc = {}
+        res = [keep.tile([P, PACK, P], F32, name="res%d" % vb) for vb in range(blocks)]
+        turns = [0, 0]
 
-        def seed(i):
-            if i >= len(steps):
-                return
-            t, vb = steps[i]
-            if i == LATE:
-                product(0, bank(4 + i % 4, "again"))
-            pulls[i] = bank(4 + i % 4, "pull%d" % i)
-            for d in range(D):
-                turn_into(pulls[i][:, d, :], y_neg[t][:, vb * P : (vb + 1) * P], d == 0, False)
+        def next_bank(name):
+            turns[1] = turns[1] + 1
+            return bank(4 + turns[1] % 4, name)
 
-        def gather(i, count, d, idle=0):
-            t, vb = steps[i]
-            picked = keep.tile([P, count * P], F32, name="picked%d_%d" % (i, d))
-            nc.vector.tensor_copy(
-                picked[:], y[:, t, :].indirect(lists[d][:, vb * P // 16 : (vb + count) * P // 16])
+        def pick(t, vb, count, d):
+            picked = ring[turns[0] % RING]
+            turns[0] = turns[0] + 1
+            nc.vector.tensor_tensor(
+                picked[:, 0 : count * P],
+                y_win[t][:].indirect(lists[d][:, vb * P // 16 : (vb + count) * P // 16]),
+                y_own[:, t, vb * P : (vb + count) * P],
+                ALU.subtract,
             )
+            return picked
+
+        def gather(t, vb, count):
             for e in range(count):
-                turn_into(pulls[i + e][:, d, :], picked[:, e * P : (e + 1) * P], False, d == D - 1)
-            for f in range(idle):
-                turn_into(pulls[i][:, d, :], zeros[:], False, False)
-
-        def clip(i):
-            t, vb = steps[i]
-            clipped[i] = keep.tile([P, D, P], F32, name="clipped%d" % i)
-            if CLIP[i] == "v":
-                nc.vector.tensor_scalar(
-                    clipped[i][:], pulls[i][:], b_hi[:, vb : vb + 1], b_lo[:, vb : vb + 1], ALU.min, ALU.max
-                )
-                return
-            raw = keep.tile([P, D, P], F32, name="raw%d" % i)
-            if CLIP[i] == "g":
-                nc.scalar.copy(out=raw[:], in_=pulls[i][:])
-                nc.gpsimd.tensor_scalar(
-                    clipped[i][:], raw[:], b_hi[:, vb : vb + 1], b_lo[:, vb : vb + 1], ALU.min, ALU.max
-                )
-                return
-            nc.scalar.activation(raw[:], pulls[i][:], ACT.Relu, bias=b_hi[:, vb : vb + 1], scale=-1.0)
-            nc.scalar.activation(clipped[i][:], raw[:], ACT.Relu, bias=b_two[:, vb : vb + 1], scale=-1.0)
-
-        def add_up(i):
-            if i < 0:
-                return
-            t, vb = steps[i]
-            if t == 0:
-                acc[vb] = bank(vb, "acc%d" % vb)
-            offset = CLIP[i] == "s"
+                pulls[t, vb + e] = next_bank("pull%d_%d" % (t, vb + e))
             for d in range(D):
-                turn_into(acc[vb][:, t, :], clipped[i][:, d, :], t == 0 and d == 0, t == PACK - 1 and d == D - 1)
-                if offset and d == 0:
-                    turn_into(acc[vb][:, t, :], b_off[:, vb : vb + 1].to_broadcast([P, P]), False, False)
-            if t == PACK - 1:
-                cols = slice(vb * P, (vb + 1) * P)
-                res = keep.tile([P, PACK, P], F32, name="res%d" % vb)
-                nc.vector.scalar_tensor_tensor(res[:], acc[vb][:], 1.0 / D, y[:, :, cols], ALU.mult, ALU.add)
-                nc.sync.dma_start(out=out_rows[:, :, cols], in_=res[:])
-                rounded = keep.tile([P, P, PACK], BF16, name="rounded%d" % vb, align_bytes=64)
-                if ROUND[vb] == "s":
-                    nc.scalar.copy(out=rounded[:], in_=res[:].rearrange("p t v -> p v t"))
-                else:
-                    nc.vector.tensor_copy(out=rounded[:], in_=res[:].rearrange("p t v -> p v t"))
-                nc.vector.quantize_mx(
-                    out=o_codes[:, cols].bitcast(FP8X4),
-                    scales=o_plane[:, cols],
-                    in_=rounded[:].rearrange("p v t -> p (v t)"),
-                )
-                nc.sync.dma_start(out=out_words[:, cols], in_=o_codes[:, cols].bitcast(I32))
+                picked = pick(t, vb, count, d)
+                for e in range(count):
+                    turn_into(pulls[t, vb + e][:, d, :], picked[:, e * P : (e + 1) * P], True, True)
 
-        y_ps = [bank(t, "y_ps%d" % t) for t in range(PACK)]
-        for t in range(PACK):
-            product(t, y_ps[t])
-            bring_out(t, y_ps[t])
-        early = bank(4, "early")
-        for f in range(FILL[0]):
-            turn_into(early[:, f % 4, :], y[:, 0, 0:P], True, True)
-        seed(0)
-        seed(1)
-        for u in range(7):
-            i = 2 * u
-            idle = FILL[1 + 3 * u : 4 + 3 * u] if u < 2 else (0, 0, 0)
-            add_up(i - LAG)
-            gather(i, 2, 0, idle[0])
-            add_up(i - LAG + 1)
-            gather(i, 2, 1, idle[1])
-            seed(i + 2)
-            gather(i, 2, 2, idle[2])
-            seed(i + 3)
-            gather(i, 2, 3)
-            clip(i)
-            clip(i + 1)
-        add_up(10)
+        def clip_scalar(pieces):
+            raw = []
+            for name, source, vb in pieces:
+                tile = keep.tile(list(source.shape), F32, name="raw" + name)
+                nc.scalar.activation(tile[:], source, ACT.Relu, bias=b_hi[:, vb : vb + 1], scale=-1.0)
+                raw.append(tile)
+            done = []
+            for (name, source, vb), tile in zip(pieces, raw):
+                target = keep.tile(list(source.shape), F32, name="clipped" + name)
+                nc.scalar.activation(target[:], tile[:], ACT.Relu, bias=b_two[:, vb : vb + 1], scale=-1.0)
+                done.append(target)
+            return done
+
+        def clip(t, vb, count):
+            done = clip_scalar([("%d_%d" % (t, vb + e), pulls[t, vb + e][:], vb + e) for e in range(count)])
+            for e in range(count):
+                clipped[t, vb + e] = done[e]
+
+        def add_up(t, vb, count):
+            for v in range(vb, vb + count):
+                if t == 0:
+                    acc[v] = bank(v, "acc%d" % v)
+                closing = t == PACK - 1 or (v == blocks - 1 and t == PACK - 2)
+                turn_into(acc[v][:, t, :], b_off[:, v : v + 1].to_broadcast([P, P]), t == 0, False)
+                for d in range(D):
+                    turn_into(acc[v][:, t, :], clipped[t, v][:, d, :], False, closing and d == D - 1)
+
+        def finish(vb, source, rows):
+            cols = slice(vb * P, (vb + 1) * P)
+            nc.vector.scalar_tensor_tensor(res[vb][:, rows, :], source, 1.0 / D, y_own[:, rows, cols], ALU.mult, ALU.add)
+            nc.sync.dma_start(out=out_rows[:, rows, cols], in_=res[vb][:, rows, :])
+
+        def hand_on(vb, on_scalar):
+            cols = slice(vb * P, (vb + 1) * P)
+            rounded = keep.tile([P, P, PACK], BF16, name="rounded%d" % vb, align_bytes=64)
+            if on_scalar:
+                nc.scalar.copy(out=rounded[:], in_=res[vb][:].rearrange("p t v -> p v t"))
+            else:
+                nc.vector.tensor_copy(out=rounded[:], in_=res[vb][:].rearrange("p t v -> p v t"))
+            nc.vector.quantize_mx(
+                out=o_codes[:, cols].bitcast(FP8X4),
+                scales=o_plane[:, cols],
+                in_=rounded[:].rearrange("p v t -> p (v t)"),
+            )
+            nc.sync.dma_start(out=out_words[:, cols], in_=o_codes[:, cols].bitcast(I32))
+
+        every = slice(0, PACK)
+        units = [(t, 0, 2) for t in range(PACK)] + [(0, 2, 2), (1, 2, 2), (2, 2, 1), (3, 2, 1), (2, 3, 1)]
+        for n, unit in enumerate(units):
+            gather(*unit)
+            clip(*unit)
+            if n > 0:
+                add_up(*units[n - 1])
+            if n == PACK:
+                finish(0, acc[0][:], every)
+                finish(1, acc[1][:], every)
+            if n == PACK + 1:
+                hand_on(0, True)
+            if n == PACK + 2:
+                hand_on(1, True)
+        finish(2, acc[2][:], every)
+
+        t, vb = PACK - 1, blocks - 1
+        early = next_bank("pull_early")
+        late = next_bank("pull_late")
         for d in range(D):
-            gather(14, 1, d)
-        clip(14)
-        add_up(11)
-        for d in range(D - 1):
-            gather(15, 1, d)
-        add_up(12)
-        gather(15, 1, D - 1)
-        clip(15)
-        for i in (13, 14, 15):
-            add_up(i)
+            picked = pick(t, vb, 1, d)
+            turn_into((early if d < 2 else late)[:, d % 2, :], picked[:, 0:P], True, True)
+        (done_early,) = clip_scalar([("_early", early[:, 0:2, :], vb)])
+        add_up(*units[-1])
+        hand_on(2, True)
+        done_late = keep.tile([P, 2, P], F32, name="clipped_late")
+        nc.vector.tensor_scalar(
+            done_late[:], late[:, 0:2, :], b_hi[:, vb : vb + 1], b_lo[:, vb : vb + 1], ALU.min, ALU.max
+        )
+        finish(vb, acc[vb][:, 0 : PACK - 1, :], slice(0, PACK - 1))
+        tail = bank(0, "acc_tail")
+        turn_into(tail[:, 0, :], b_half[:, vb : vb + 1].to_broadcast([P, P]), True, False)
+        for d in range(D):
+            turn_into(tail[:, 0, :], (done_early if d < 2 else done_late)[:, d % 2, :], False, d == D - 1)
+        finish(vb, tail[:, 0:1, :], slice(PACK - 1, PACK))
+        hand_on(vb, False)
 
         for q in range(4):
             queue = nc.sync if q % 2 == 0 else nc.scalar

@@ -7,7 +7,7 @@ K, T, N = 512, 512, 512
 D = 4
 P = 128
 PACK = 4
-RING = 4
+RING = 8
 FLOPS = 2 * K * T * N
 
 F32 = mybir.dt.float32
@@ -42,33 +42,37 @@ def tile_picked_whuber_none_lo_kernel(
             in_=x_words[0].rearrange("p c r -> p (c r)").bitcast(I32),
         )
         x_plane = keep.tile([P, T], U8, name="x_plane", align_bytes=64)
-        nc.gpsimd.memset(x_plane[:].bitcast(I32), 0)
+        nc.vector.memset(x_plane[:].bitcast(I32), 0)
         for q in range(4):
             nc.scalar.dma_start(
                 out=x_plane[32 * q : 32 * q + 4, :].bitcast(I32),
                 in_=x_scales[0, 4 * q : 4 * q + 4, :].bitcast(I32),
             )
-        b_rows = keep.tile([P, P], F32, name="b_rows")
-        nc.gpsimd.memset(b_rows[:], 0.0)
         lists = []
         for d, pos in enumerate((pos1, pos2, pos3, pos4)):
             tile = keep.tile([P, T // 16], U16, name="list%d" % d)
             nc.sync.dma_start(tile[:], pos)
             lists.append(tile)
+        b_rows = keep.tile([P, P], F32, name="b_rows")
+        nc.gpsimd.memset(b_rows[:], 0.0)
         nc.sync.dma_start(
             out=b_rows[0:blocks, :],
             in_=bound[0:1, :].rearrange("o (c v) -> (o c) v", c=blocks),
         )
+        b_last = keep.tile([P, P], F32, name="b_last")
+        nc.sync.dma_start(out=b_last[:], in_=bound[:, T - P : T])
 
         ident = keep.tile([P, P], F32, name="ident")
         make_identity(nc, ident[:])
 
         b_ps = bank(7, "b_ps")
         nc.tensor.transpose(b_ps[:, 0, :], b_rows[:], ident[:])
-        b_cols = keep.tile([P, 5, 8], F32, name="b_cols")
-        for i, factor in enumerate((1.0, -1.0, 2.0, -float(D), -2.0)):
-            nc.scalar.activation(b_cols[:, i, :], b_ps[:, 0, 0:8], ACT.Copy, scale=factor)
-        b_hi, b_lo, b_two, b_off, b_half = (b_cols[:, i, :] for i in range(5))
+        b_cols = keep.tile([P, 3, 8], F32, name="b_cols")
+        b_hi, b_two, b_off = (b_cols[:, i, 0:blocks] for i in range(3))
+        for target, factor in ((b_hi, 1.0), (b_two, 2.0), (b_off, -float(D))):
+            nc.scalar.activation(target, b_ps[:, 0, 0:blocks], ACT.Copy, scale=factor)
+        top_last = keep.tile([P, P], F32, name="top_last")
+        nc.scalar.activation(top_last[:], b_last[:], ACT.Relu, scale=2.0)
 
         w_src = w_raw[:].rearrange("p j (m t) -> p t m j", t=PACK)
         w_codes = keep.tile([P, N], U32, name="w_codes", align_bytes=64)
@@ -77,20 +81,18 @@ def tile_picked_whuber_none_lo_kernel(
         w_two = keep.tile([P, 2, P, PACK], BF16, name="w_two", align_bytes=64)
         nc.scalar.copy(
             out=w_two[:].rearrange("p t m j -> p m t j"),
-            in_=w_src[:, 2:4].rearrange("p t m j -> p m t j"),
+            in_=w_src[:, 1:3].rearrange("p t m j -> p m t j"),
         )
-        for t in range(2):
-            nc.vector.tensor_copy(out=w_one[:], in_=w_src[:, t])
-            nc.vector.quantize_mx(
-                out=w_codes[:, t * P : (t + 1) * P].bitcast(FP8X4),
-                scales=w_plane[:, t * P : (t + 1) * P],
-                in_=w_one[:].rearrange("p m j -> p (m j)"),
-            )
-        nc.vector.quantize_mx(
-            out=w_codes[:, 2 * P : 4 * P].bitcast(FP8X4),
-            scales=w_plane[:, 2 * P : 4 * P],
-            in_=w_two[:].rearrange("p t m j -> p (t m j)"),
-        )
+
+        def quantise(first, count, source):
+            cols = slice(first * P, (first + count) * P)
+            nc.vector.quantize_mx(out=w_codes[:, cols].bitcast(FP8X4), scales=w_plane[:, cols], in_=source)
+
+        nc.vector.tensor_copy(out=w_one[:], in_=w_src[:, 0])
+        quantise(0, 1, w_one[:].rearrange("p m j -> p (m j)"))
+        nc.vector.tensor_copy(out=w_one[:], in_=w_src[:, 3])
+        quantise(1, 2, w_two[:].rearrange("p t m j -> p (t m j)"))
+        quantise(3, 1, w_one[:].rearrange("p m j -> p (m j)"))
 
         y_win = [keep.tile([P, T], F32, name="y_win%d" % t) for t in range(PACK)]
         y_own = keep.tile([P, PACK, T], F32, name="y_own")
@@ -137,6 +139,7 @@ def tile_picked_whuber_none_lo_kernel(
 
         ring = [keep.tile([P, 2 * P], F32, name="ring%d" % i) for i in range(RING)]
         pulls = {}
+        raws = {}
         clipped = {}
         acc = {}
         res = [keep.tile([P, PACK, P], F32, name="res%d" % vb) for vb in range(blocks)]
@@ -146,107 +149,116 @@ def tile_picked_whuber_none_lo_kernel(
             turns[1] = turns[1] + 1
             return bank(4 + turns[1] % 4, name)
 
-        def pick(t, vb, count, d):
-            picked = ring[turns[0] % RING]
+        def next_ring():
             turns[0] = turns[0] + 1
+            return ring[turns[0] % RING]
+
+        def pick(target, t, vb, count, d, own):
             nc.vector.tensor_tensor(
-                picked[:, 0 : count * P],
+                target,
                 y_win[t][:].indirect(lists[d][:, vb * P // 16 : (vb + count) * P // 16]),
-                y_own[:, t, vb * P : (vb + count) * P],
+                own,
                 ALU.subtract,
             )
-            return picked
 
         def gather(t, vb, count):
             for e in range(count):
                 pulls[t, vb + e] = next_bank("pull%d_%d" % (t, vb + e))
             for d in range(D):
-                picked = pick(t, vb, count, d)
+                picked = next_ring()
+                pick(picked[:, 0 : count * P], t, vb, count, d, y_own[:, t, vb * P : (vb + count) * P])
                 for e in range(count):
                     turn_into(pulls[t, vb + e][:, d, :], picked[:, e * P : (e + 1) * P], True, True)
 
-        def clip_scalar(pieces):
-            raw = []
-            for name, source, vb in pieces:
-                tile = keep.tile(list(source.shape), F32, name="raw" + name)
-                nc.scalar.activation(tile[:], source, ACT.Relu, bias=b_hi[:, vb : vb + 1], scale=-1.0)
-                raw.append(tile)
-            done = []
-            for (name, source, vb), tile in zip(pieces, raw):
-                target = keep.tile(list(source.shape), F32, name="clipped" + name)
-                nc.scalar.activation(target[:], tile[:], ACT.Relu, bias=b_two[:, vb : vb + 1], scale=-1.0)
-                done.append(target)
-            return done
+        def col(cols, vb):
+            return cols[:, vb : vb + 1]
 
         def clip(t, vb, count):
-            done = clip_scalar([("%d_%d" % (t, vb + e), pulls[t, vb + e][:], vb + e) for e in range(count)])
-            for e in range(count):
-                clipped[t, vb + e] = done[e]
+            raw = {}
+            for v in range(vb, vb + count):
+                raw[v] = raws[t, v] = keep.tile([P, D, P], F32, name="raw%d_%d" % (t, v), align_bytes=64)
+                nc.scalar.activation(raw[v][:], pulls[t, v][:], ACT.Relu, bias=col(b_hi, v), scale=-1.0)
+            for v in raw:
+                clipped[t, v] = keep.tile([P, D, P], F32, name="clipped%d_%d" % (t, v))
+                nc.scalar.activation(clipped[t, v][:], raw[v][:], ACT.Relu, bias=col(b_two, v), scale=-1.0)
+
+        def turned_rows(v):
+            return PACK - 1 if v == blocks - 1 else PACK
+
+        def open_sums(v):
+            acc[v] = bank(v, "acc%d" % v)
+            for t in range(turned_rows(v)):
+                turn_into(acc[v][:, t, :], col(b_off, v).to_broadcast([P, P]), t == 0, False)
 
         def add_up(t, vb, count):
             for v in range(vb, vb + count):
-                if t == 0:
-                    acc[v] = bank(v, "acc%d" % v)
-                closing = t == PACK - 1 or (v == blocks - 1 and t == PACK - 2)
-                turn_into(acc[v][:, t, :], b_off[:, v : v + 1].to_broadcast([P, P]), t == 0, False)
                 for d in range(D):
-                    turn_into(acc[v][:, t, :], clipped[t, v][:, d, :], False, closing and d == D - 1)
+                    turn_into(acc[v][:, t, :], clipped[t, v][:, d, :], False, t == turned_rows(v) - 1 and d == D - 1)
 
-        def finish(vb, source, rows):
+        def finish(vb, rows):
             cols = slice(vb * P, (vb + 1) * P)
-            nc.vector.scalar_tensor_tensor(res[vb][:, rows, :], source, 1.0 / D, y_own[:, rows, cols], ALU.mult, ALU.add)
-            nc.sync.dma_start(out=out_rows[:, rows, cols], in_=res[vb][:, rows, :])
+            nc.vector.scalar_tensor_tensor(
+                res[vb][:, rows, :], acc[vb][:, rows, :], 1.0 / D, y_own[:, rows, cols], ALU.mult, ALU.add
+            )
 
-        def hand_on(vb, on_scalar):
-            cols = slice(vb * P, (vb + 1) * P)
-            rounded = keep.tile([P, P, PACK], BF16, name="rounded%d" % vb, align_bytes=64)
-            if on_scalar:
-                nc.scalar.copy(out=rounded[:], in_=res[vb][:].rearrange("p t v -> p v t"))
-            else:
-                nc.vector.tensor_copy(out=rounded[:], in_=res[vb][:].rearrange("p t v -> p v t"))
+        def store(vb):
+            nc.sync.dma_start(out=out_rows[:, :, vb * P : (vb + 1) * P], in_=res[vb][:])
+
+        def interleaved(vb):
+            return res[vb][:].rearrange("p t v -> p v t")
+
+        def hand_on(h, rounded):
+            cols = slice(h * half, (h + 1) * half)
             nc.vector.quantize_mx(
                 out=o_codes[:, cols].bitcast(FP8X4),
                 scales=o_plane[:, cols],
-                in_=rounded[:].rearrange("p v t -> p (v t)"),
+                in_=rounded.rearrange("p b v t -> p (b v t)"),
             )
             nc.sync.dma_start(out=out_words[:, cols], in_=o_codes[:, cols].bitcast(I32))
 
-        every = slice(0, PACK)
         units = [(t, 0, 2) for t in range(PACK)] + [(0, 2, 2), (1, 2, 2), (2, 2, 1), (3, 2, 1), (2, 3, 1)]
         for n, unit in enumerate(units):
             gather(*unit)
             clip(*unit)
+            if n < 2:
+                open_sums(2 * n)
+                open_sums(2 * n + 1)
             if n > 0:
                 add_up(*units[n - 1])
             if n == PACK:
-                finish(0, acc[0][:], every)
-                finish(1, acc[1][:], every)
-            if n == PACK + 1:
-                hand_on(0, True)
-            if n == PACK + 2:
-                hand_on(1, True)
-        finish(2, acc[2][:], every)
+                for vb in range(2):
+                    finish(vb, slice(0, PACK))
+                    store(vb)
 
         t, vb = PACK - 1, blocks - 1
-        early = next_bank("pull_early")
-        late = next_bank("pull_late")
-        for d in range(D):
-            picked = pick(t, vb, 1, d)
-            turn_into((early if d < 2 else late)[:, d % 2, :], picked[:, 0:P], True, True)
-        (done_early,) = clip_scalar([("_early", early[:, 0:2, :], vb)])
+        cols = slice(vb * P, (vb + 1) * P)
+        base = keep.tile([P, P], F32, name="base")
+        nc.vector.tensor_tensor(base[:], y_own[:, t, cols], b_last[:], ALU.subtract)
+        lifted = [next_ring()[:, 0:P] for d in range(D)]
+        held = raws[t, vb - 1]
+        sums = clipped[t, vb - 1]
         add_up(*units[-1])
-        hand_on(2, True)
-        done_late = keep.tile([P, 2, P], F32, name="clipped_late")
-        nc.vector.tensor_scalar(
-            done_late[:], late[:, 0:2, :], b_hi[:, vb : vb + 1], b_lo[:, vb : vb + 1], ALU.min, ALU.max
-        )
-        finish(vb, acc[vb][:, 0 : PACK - 1, :], slice(0, PACK - 1))
-        tail = bank(0, "acc_tail")
-        turn_into(tail[:, 0, :], b_half[:, vb : vb + 1].to_broadcast([P, P]), True, False)
         for d in range(D):
-            turn_into(tail[:, 0, :], (done_early if d < 2 else done_late)[:, d % 2, :], False, d == D - 1)
-        finish(vb, tail[:, 0:1, :], slice(PACK - 1, PACK))
-        hand_on(vb, False)
+            pick(lifted[d], t, vb, 1, d, base[:])
+        finish(2, slice(0, PACK))
+        store(2)
+        finish(vb, slice(0, t))
+        for d in range(D):
+            nc.vector.scalar_tensor_tensor(held[:, d, :], lifted[d], 0.0, top_last[:], ALU.max, ALU.min)
+        for d in range(D):
+            nc.vector.scalar_tensor_tensor(
+                sums[:, d, :] if d < D - 1 else res[vb][:, t, :],
+                held[:, d, :], 1.0 / D, sums[:, d - 1, :] if d > 0 else base[:], ALU.mult, ALU.add,
+            )
+        store(vb)
+        first = raws[t - 1, vb][:].rearrange("p d v -> p (d v)").bitcast(BF16).rearrange("p (b v t) -> p b v t", b=2, t=PACK)
+        second = keep.tile([P, 2, P, PACK], BF16, name="second", align_bytes=64)
+        nc.scalar.copy(out=first[:, 0], in_=interleaved(0))
+        nc.scalar.copy(out=first[:, 1], in_=interleaved(1))
+        nc.scalar.copy(out=second[:, 0], in_=interleaved(2))
+        hand_on(0, first)
+        nc.vector.tensor_copy(out=second[:, 1], in_=interleaved(3))
+        hand_on(1, second[:])
 
         for q in range(4):
             queue = nc.sync if q % 2 == 0 else nc.scalar

@@ -8,6 +8,7 @@ D = 4
 P = 128
 PACK = 4
 RING = 8
+SPLIT = 88
 FLOPS = 2 * K * T * N
 
 F32 = mybir.dt.float32
@@ -79,20 +80,20 @@ def tile_picked_whuber_none_lo_kernel(
         w_plane = keep.tile([P, N], U8, name="w_plane", align_bytes=64)
         w_one = keep.tile([P, P, PACK], BF16, name="w_one", align_bytes=64)
         w_two = keep.tile([P, 2, P, PACK], BF16, name="w_two", align_bytes=64)
+        nc.scalar.copy(out=w_one[:, SPLIT:P, :], in_=w_src[:, 0, SPLIT:P, :])
         nc.scalar.copy(
             out=w_two[:].rearrange("p t m j -> p m t j"),
-            in_=w_src[:, 1:3].rearrange("p t m j -> p m t j"),
+            in_=w_src[:, 2:4].rearrange("p t m j -> p m t j"),
         )
 
         def quantise(first, count, source):
             cols = slice(first * P, (first + count) * P)
             nc.vector.quantize_mx(out=w_codes[:, cols].bitcast(FP8X4), scales=w_plane[:, cols], in_=source)
 
-        nc.vector.tensor_copy(out=w_one[:], in_=w_src[:, 0])
+        nc.vector.tensor_copy(out=w_one[:, 0:SPLIT, :], in_=w_src[:, 0, 0:SPLIT, :])
         quantise(0, 1, w_one[:].rearrange("p m j -> p (m j)"))
-        nc.vector.tensor_copy(out=w_one[:], in_=w_src[:, 3])
-        quantise(1, 2, w_two[:].rearrange("p t m j -> p (t m j)"))
-        quantise(3, 1, w_one[:].rearrange("p m j -> p (m j)"))
+        nc.vector.tensor_copy(out=w_one[:], in_=w_src[:, 1])
+        quantise(1, 1, w_one[:].rearrange("p m j -> p (m j)"))
 
         y_win = [keep.tile([P, T], F32, name="y_win%d" % t) for t in range(PACK)]
         y_own = keep.tile([P, PACK, T], F32, name="y_own")
@@ -114,20 +115,20 @@ def tile_picked_whuber_none_lo_kernel(
             y_ps = bank(4 * h, "y_half%d" % h)
             flat = y_ps[:].rearrange("p a b -> p (a b)")[:, 0:half]
             product(0, flat, cols)
-            nc.scalar.copy(out=y_win[0][:, cols], in_=flat)
             if h == 0:
-                nc.vector.tensor_copy(out=y_own[:, 0, cols], in_=flat)
+                nc.scalar.copy(out=y_win[0][:, cols], in_=flat)
+                nc.scalar.copy(out=y_own[:, 0, cols], in_=flat)
+            else:
+                nc.vector.tensor_copy(out=y_win[0][:, cols], in_=flat)
+        quantise(2, 2, w_two[:].rearrange("p t m j -> p (t m j)"))
         nc.sync.dma_start(out=y_own[:, 0, half:T], in_=y_win[0][:, half:T])
         for t in range(1, PACK):
             y_ps = bank(t, "y_ps%d" % t)
             flat = y_ps[:].rearrange("p a b -> p (a b)")
             product(t, flat, slice(0, T))
             nc.scalar.copy(out=y_win[t][:], in_=flat)
-            if t == 1:
-                nc.scalar.copy(out=y_own[:, t, 0:half], in_=flat[:, 0:half])
-                nc.sync.dma_start(out=y_own[:, t, half:T], in_=y_win[t][:, half:T])
-            else:
-                nc.sync.dma_start(out=y_own[:, t, :], in_=y_win[t][:])
+            nc.scalar.copy(out=y_own[:, t, 0:half], in_=flat[:, 0:half])
+            nc.sync.dma_start(out=y_own[:, t, half:T], in_=y_win[t][:, half:T])
 
         def turn_into(target, source, start, stop):
             nc.tensor.matmul(target, lhsT=source, rhs=ident[:], start=start, stop=stop, is_transpose=True)
@@ -137,21 +138,24 @@ def tile_picked_whuber_none_lo_kernel(
         out_rows = out_0.rearrange("(p t) v -> p t v", t=PACK)
         out_words = out_1[0].rearrange("p c r -> p (c r)").bitcast(I32)
 
-        ring = [keep.tile([P, 2 * P], F32, name="ring%d" % i) for i in range(RING)]
+        ring = keep.tile([P, RING * 2 * P], F32, name="ring")
+        shared = keep.tile([P, 6 * P], F32, name="shared", align_bytes=64)
         pulls = {}
         raws = {}
         clipped = {}
         acc = {}
-        res = [keep.tile([P, PACK, P], F32, name="res%d" % vb) for vb in range(blocks)]
+        res = {vb: keep.tile([P, PACK, P], F32, name="res%d" % vb) for vb in (2, 3)}
         turns = [0, 0]
 
         def next_bank(name):
             turns[1] = turns[1] + 1
             return bank(4 + turns[1] % 4, name)
 
-        def next_ring():
+        def next_slot(count):
+            slot = turns[0] % RING
             turns[0] = turns[0] + 1
-            return ring[turns[0] % RING]
+            first = slot * 2 * P + (P if count == 1 and slot % 2 == 0 else 0)
+            return slice(first, first + count * P)
 
         def pick(target, t, vb, count, d, own):
             nc.vector.tensor_tensor(
@@ -165,7 +169,7 @@ def tile_picked_whuber_none_lo_kernel(
             for e in range(count):
                 pulls[t, vb + e] = next_bank("pull%d_%d" % (t, vb + e))
             for d in range(D):
-                picked = next_ring()
+                picked = ring[:, next_slot(count)]
                 pick(picked[:, 0 : count * P], t, vb, count, d, y_own[:, t, vb * P : (vb + count) * P])
                 for e in range(count):
                     turn_into(pulls[t, vb + e][:, d, :], picked[:, e * P : (e + 1) * P], True, True)
@@ -176,7 +180,11 @@ def tile_picked_whuber_none_lo_kernel(
         def clip(t, vb, count):
             raw = {}
             for v in range(vb, vb + count):
-                raw[v] = raws[t, v] = keep.tile([P, D, P], F32, name="raw%d_%d" % (t, v), align_bytes=64)
+                if (t, v) == (PACK - 2, blocks - 1):
+                    raws[t, v] = shared[:, 0 : 4 * P].rearrange("p (d v) -> p d v", d=D)
+                else:
+                    raws[t, v] = keep.tile([P, D, P], F32, name="raw%d_%d" % (t, v))
+                raw[v] = raws[t, v]
                 nc.scalar.activation(raw[v][:], pulls[t, v][:], ACT.Relu, bias=col(b_hi, v), scale=-1.0)
             for v in raw:
                 clipped[t, v] = keep.tile([P, D, P], F32, name="clipped%d_%d" % (t, v))
@@ -207,13 +215,12 @@ def tile_picked_whuber_none_lo_kernel(
         def interleaved(vb):
             return res[vb][:].rearrange("p t v -> p v t")
 
-        def hand_on(h, rounded):
+        def hand_on(vb, count, rounded):
+            cols = slice(vb * P, (vb + count) * P)
+            nc.vector.quantize_mx(out=o_codes[:, cols].bitcast(FP8X4), scales=o_plane[:, cols], in_=rounded)
+
+        def store_words(h):
             cols = slice(h * half, (h + 1) * half)
-            nc.vector.quantize_mx(
-                out=o_codes[:, cols].bitcast(FP8X4),
-                scales=o_plane[:, cols],
-                in_=rounded.rearrange("p b v t -> p (b v t)"),
-            )
             nc.sync.dma_start(out=out_words[:, cols], in_=o_codes[:, cols].bitcast(I32))
 
         units = [(t, 0, 2) for t in range(PACK)] + [(0, 2, 2), (1, 2, 2), (2, 2, 1), (3, 2, 1), (2, 3, 1)]
@@ -225,40 +232,44 @@ def tile_picked_whuber_none_lo_kernel(
                 open_sums(2 * n + 1)
             if n > 0:
                 add_up(*units[n - 1])
-            if n == PACK:
-                for vb in range(2):
-                    finish(vb, slice(0, PACK))
-                    store(vb)
+        for vb in range(2):
+            res[vb] = raws[0, 2 + vb]
+            finish(vb, slice(0, PACK))
+            store(vb)
 
         t, vb = PACK - 1, blocks - 1
         cols = slice(vb * P, (vb + 1) * P)
         base = keep.tile([P, P], F32, name="base")
         nc.vector.tensor_tensor(base[:], y_own[:, t, cols], b_last[:], ALU.subtract)
-        lifted = [next_ring()[:, 0:P] for d in range(D)]
+        lifted = [next_slot(1) for d in range(D)]
         held = raws[t, vb - 1]
         sums = clipped[t, vb - 1]
         add_up(*units[-1])
         for d in range(D):
-            pick(lifted[d], t, vb, 1, d, base[:])
+            pick(ring[:, lifted[d]], t, vb, 1, d, base[:])
         finish(2, slice(0, PACK))
         store(2)
         finish(vb, slice(0, t))
-        for d in range(D):
-            nc.vector.scalar_tensor_tensor(held[:, d, :], lifted[d], 0.0, top_last[:], ALU.max, ALU.min)
-        for d in range(D):
+        top_two = top_last[:].unsqueeze(1).to_broadcast([P, 2, P])
+        for i in range(2):
             nc.vector.scalar_tensor_tensor(
-                sums[:, d, :] if d < D - 1 else res[vb][:, t, :],
-                held[:, d, :], 1.0 / D, sums[:, d - 1, :] if d > 0 else base[:], ALU.mult, ALU.add,
+                held[:, 2 * i : 2 * i + 2, :], ring[:, lifted[2 * i].start : lifted[2 * i + 1].stop].rearrange("p (d v) -> p d v", d=2), 0.0, top_two, ALU.max, ALU.min
             )
+        nc.vector.tensor_tensor(sums[:, 0:2, :], held[:, 0:2, :], held[:, 2:4, :], ALU.add)
+        nc.vector.scalar_tensor_tensor(sums[:, 2, :], sums[:, 0, :], 1.0 / D, base[:], ALU.mult, ALU.add)
+        nc.vector.scalar_tensor_tensor(res[vb][:, t, :], sums[:, 1, :], 1.0 / D, sums[:, 2, :], ALU.mult, ALU.add)
         store(vb)
-        first = raws[t - 1, vb][:].rearrange("p d v -> p (d v)").bitcast(BF16).rearrange("p (b v t) -> p b v t", b=2, t=PACK)
+        first = shared[:, 0 : 4 * P].bitcast(BF16).rearrange("p (b v t) -> p b v t", b=2, t=PACK)
         second = keep.tile([P, 2, P, PACK], BF16, name="second", align_bytes=64)
         nc.scalar.copy(out=first[:, 0], in_=interleaved(0))
         nc.scalar.copy(out=first[:, 1], in_=interleaved(1))
         nc.scalar.copy(out=second[:, 0], in_=interleaved(2))
-        hand_on(0, first)
         nc.vector.tensor_copy(out=second[:, 1], in_=interleaved(3))
-        hand_on(1, second[:])
+        hand_on(0, 2, first.rearrange("p b v t -> p (b v t)"))
+        store_words(0)
+        for i in range(2):
+            hand_on(2 + i, 1, second[:, i].rearrange("p v t -> p (v t)"))
+        store_words(1)
 
         for q in range(4):
             queue = nc.sync if q % 2 == 0 else nc.scalar

@@ -8,6 +8,7 @@ D = 4
 P = 128
 PACK = 4
 RING = 8
+WHOLE = (1,)
 SPLIT = 88
 FLOPS = 2 * K * T * N
 
@@ -95,7 +96,9 @@ def tile_picked_whuber_none_lo_kernel(
         nc.vector.tensor_copy(out=w_one[:], in_=w_src[:, 1])
         quantise(1, 1, w_one[:].rearrange("p m j -> p (m j)"))
 
-        y_win = [keep.tile([P, T], F32, name="y_win%d" % t) for t in range(PACK)]
+        y_win = [keep.tile([P, 2 * T if t in WHOLE else T], F32, name="y_win%d" % t) for t in range(PACK)]
+        for t in WHOLE:
+            nc.gpsimd.memset(y_win[t][:, T : 2 * T], 0.0)
         y_own = keep.tile([P, PACK, T], F32, name="y_own")
         half = T // 2
 
@@ -120,15 +123,14 @@ def tile_picked_whuber_none_lo_kernel(
                 nc.scalar.copy(out=y_own[:, 0, cols], in_=flat)
             else:
                 nc.vector.tensor_copy(out=y_win[0][:, cols], in_=flat)
+                nc.scalar.copy(out=y_own[:, 0, cols], in_=flat)
         quantise(2, 2, w_two[:].rearrange("p t m j -> p (t m j)"))
-        nc.sync.dma_start(out=y_own[:, 0, half:T], in_=y_win[0][:, half:T])
         for t in range(1, PACK):
             y_ps = bank(t, "y_ps%d" % t)
             flat = y_ps[:].rearrange("p a b -> p (a b)")
             product(t, flat, slice(0, T))
-            nc.scalar.copy(out=y_win[t][:], in_=flat)
-            nc.scalar.copy(out=y_own[:, t, 0:half], in_=flat[:, 0:half])
-            nc.sync.dma_start(out=y_own[:, t, half:T], in_=y_win[t][:, half:T])
+            nc.scalar.copy(out=y_win[t][:, 0:T], in_=flat)
+            nc.sync.dma_start(out=y_own[:, t, :], in_=y_win[t][:, 0:T])
 
         def turn_into(target, source, start, stop):
             nc.tensor.matmul(target, lhsT=source, rhs=ident[:], start=start, stop=stop, is_transpose=True)
@@ -139,12 +141,9 @@ def tile_picked_whuber_none_lo_kernel(
         out_words = out_1[0].rearrange("p c r -> p (c r)").bitcast(I32)
 
         ring = keep.tile([P, RING * 2 * P], F32, name="ring")
-        shared = keep.tile([P, 6 * P], F32, name="shared", align_bytes=64)
-        pulls = {}
-        raws = {}
-        clipped = {}
+        shared = keep.tile([P, 8 * P], F32, name="shared", align_bytes=64)
         acc = {}
-        res = {vb: keep.tile([P, PACK, P], F32, name="res%d" % vb) for vb in (2, 3)}
+        res = {vb: keep.tile([P, PACK, P], F32, name="res%d" % vb) for vb in range(blocks)}
         turns = [0, 0]
 
         def next_bank(name):
@@ -153,7 +152,7 @@ def tile_picked_whuber_none_lo_kernel(
 
         def next_slot(count):
             slot = turns[0] % RING
-            turns[0] = turns[0] + 1
+            turns[0] = turns[0] + (count + 1) // 2
             first = slot * 2 * P + (P if count == 1 and slot % 2 == 0 else 0)
             return slice(first, first + count * P)
 
@@ -165,30 +164,36 @@ def tile_picked_whuber_none_lo_kernel(
                 ALU.subtract,
             )
 
-        def gather(t, vb, count):
-            for e in range(count):
-                pulls[t, vb + e] = next_bank("pull%d_%d" % (t, vb + e))
-            for d in range(D):
-                picked = ring[:, next_slot(count)]
-                pick(picked[:, 0 : count * P], t, vb, count, d, y_own[:, t, vb * P : (vb + count) * P])
-                for e in range(count):
-                    turn_into(pulls[t, vb + e][:, d, :], picked[:, e * P : (e + 1) * P], True, True)
-
         def col(cols, vb):
             return cols[:, vb : vb + 1]
 
-        def clip(t, vb, count):
+        def gather(t, vb, count, ds):
+            share = D // len(ds)
+            banks = [next_bank("pull%d_%d_%d_%d" % (t, vb, ds[0], i)) for i in range((count + share - 1) // share)]
+            places = {}
+            for e in range(count):
+                first = (e % share) * len(ds)
+                places[vb + e] = banks[e // share][:, first : first + len(ds), :]
+            for i, d in enumerate(ds):
+                picked = ring[:, next_slot(count)]
+                pick(picked, t, vb, count, d, y_own[:, t, vb * P : (vb + count) * P])
+                for e in range(count):
+                    turn_into(places[vb + e][:, i, :], picked[:, e * P : (e + 1) * P], True, True)
+            return places
+
+        def clip(t, ds, places, last):
             raw = {}
-            for v in range(vb, vb + count):
-                if (t, v) == (PACK - 2, blocks - 1):
-                    raws[t, v] = shared[:, 0 : 4 * P].rearrange("p (d v) -> p d v", d=D)
+            done = {}
+            for v, place in places.items():
+                if last:
+                    raw[v] = shared[:, 3 * P : 7 * P].rearrange("p (d v) -> p d v", d=D)
                 else:
-                    raws[t, v] = keep.tile([P, D, P], F32, name="raw%d_%d" % (t, v))
-                raw[v] = raws[t, v]
-                nc.scalar.activation(raw[v][:], pulls[t, v][:], ACT.Relu, bias=col(b_hi, v), scale=-1.0)
-            for v in raw:
-                clipped[t, v] = keep.tile([P, D, P], F32, name="clipped%d_%d" % (t, v))
-                nc.scalar.activation(clipped[t, v][:], raw[v][:], ACT.Relu, bias=col(b_two, v), scale=-1.0)
+                    raw[v] = keep.tile([P, len(ds), P], F32, name="raw%d_%d_%d" % (t, v, ds[0]))[:]
+                nc.scalar.activation(raw[v], place, ACT.Relu, bias=col(b_hi, v), scale=-1.0)
+            for v in places:
+                done[v] = keep.tile([P, len(ds), P], F32, name="clipped%d_%d_%d" % (t, v, ds[0]))
+                nc.scalar.activation(done[v][:], raw[v], ACT.Relu, bias=col(b_two, v), scale=-1.0)
+            return raw, done
 
         def turned_rows(v):
             return PACK - 1 if v == blocks - 1 else PACK
@@ -198,10 +203,10 @@ def tile_picked_whuber_none_lo_kernel(
             for t in range(turned_rows(v)):
                 turn_into(acc[v][:, t, :], col(b_off, v).to_broadcast([P, P]), t == 0, False)
 
-        def add_up(t, vb, count):
-            for v in range(vb, vb + count):
-                for d in range(D):
-                    turn_into(acc[v][:, t, :], clipped[t, v][:, d, :], False, t == turned_rows(v) - 1 and d == D - 1)
+        def add_up(t, ds, done):
+            for v, tile in done.items():
+                for i, d in enumerate(ds):
+                    turn_into(acc[v][:, t, :], tile[:, i, :], False, t == turned_rows(v) - 1 and d == D - 1)
 
         def finish(vb, rows):
             cols = slice(vb * P, (vb + 1) * P)
@@ -212,8 +217,11 @@ def tile_picked_whuber_none_lo_kernel(
         def store(vb):
             nc.sync.dma_start(out=out_rows[:, :, vb * P : (vb + 1) * P], in_=res[vb][:])
 
-        def interleaved(vb):
-            return res[vb][:].rearrange("p t v -> p v t")
+        def round_into(copy, target, vb):
+            copy(
+                out=target.rearrange("p (c i) t -> p c t i", i=4),
+                in_=res[vb][:].rearrange("p t (c i) -> p c t i", i=4),
+            )
 
         def hand_on(vb, count, rounded):
             cols = slice(vb * P, (vb + count) * P)
@@ -223,28 +231,32 @@ def tile_picked_whuber_none_lo_kernel(
             cols = slice(h * half, (h + 1) * half)
             nc.sync.dma_start(out=out_words[:, cols], in_=o_codes[:, cols].bitcast(I32))
 
-        units = [(t, 0, 2) for t in range(PACK)] + [(0, 2, 2), (1, 2, 2), (2, 2, 1), (3, 2, 1), (2, 3, 1)]
-        for n, unit in enumerate(units):
-            gather(*unit)
-            clip(*unit)
+        every = (0, 1, 2, 3)
+        units = [(0, 0, 2, every), (0, 2, 2, every), (1, 0, 4, (0, 1)), (1, 0, 4, (2, 3))] + [(2, 0, 2, every), (3, 0, 2, every), (2, 2, 1, every), (3, 2, 1, every), (2, 3, 1, every)]
+        raws = []
+        dones = []
+        for n, (t, vb, count, ds) in enumerate(units):
+            raw, done = clip(t, ds, gather(t, vb, count, ds), n == len(units) - 1)
+            raws.append(raw)
+            dones.append(done)
             if n < 2:
                 open_sums(2 * n)
                 open_sums(2 * n + 1)
             if n > 0:
-                add_up(*units[n - 1])
-        for vb in range(2):
-            res[vb] = raws[0, 2 + vb]
-            finish(vb, slice(0, PACK))
-            store(vb)
+                add_up(units[n - 1][0], units[n - 1][3], dones[n - 1])
+
+        for v in range(2):
+            finish(v, slice(0, PACK))
+            store(v)
 
         t, vb = PACK - 1, blocks - 1
         cols = slice(vb * P, (vb + 1) * P)
         base = keep.tile([P, P], F32, name="base")
         nc.vector.tensor_tensor(base[:], y_own[:, t, cols], b_last[:], ALU.subtract)
         lifted = [next_slot(1) for d in range(D)]
-        held = raws[t, vb - 1]
-        sums = clipped[t, vb - 1]
-        add_up(*units[-1])
+        held = raws[-2][2]
+        sums = dones[-2][2]
+        add_up(units[-1][0], every, dones[-1])
         for d in range(D):
             pick(ring[:, lifted[d]], t, vb, 1, d, base[:])
         finish(2, slice(0, PACK))
@@ -253,18 +265,20 @@ def tile_picked_whuber_none_lo_kernel(
         top_two = top_last[:].unsqueeze(1).to_broadcast([P, 2, P])
         for i in range(2):
             nc.vector.scalar_tensor_tensor(
-                held[:, 2 * i : 2 * i + 2, :], ring[:, lifted[2 * i].start : lifted[2 * i + 1].stop].rearrange("p (d v) -> p d v", d=2), 0.0, top_two, ALU.max, ALU.min
+                held[:, 2 * i : 2 * i + 2, :],
+                ring[:, lifted[2 * i].start : lifted[2 * i + 1].stop].rearrange("p (d v) -> p d v", d=2),
+                0.0, top_two, ALU.max, ALU.min,
             )
         nc.vector.tensor_tensor(sums[:, 0:2, :], held[:, 0:2, :], held[:, 2:4, :], ALU.add)
         nc.vector.scalar_tensor_tensor(sums[:, 2, :], sums[:, 0, :], 1.0 / D, base[:], ALU.mult, ALU.add)
         nc.vector.scalar_tensor_tensor(res[vb][:, t, :], sums[:, 1, :], 1.0 / D, sums[:, 2, :], ALU.mult, ALU.add)
         store(vb)
-        first = shared[:, 0 : 4 * P].bitcast(BF16).rearrange("p (b v t) -> p b v t", b=2, t=PACK)
+        first = shared[:, 3 * P : 7 * P].bitcast(BF16).rearrange("p (b v t) -> p b v t", b=2, t=PACK)
         second = keep.tile([P, 2, P, PACK], BF16, name="second", align_bytes=64)
-        nc.scalar.copy(out=first[:, 0], in_=interleaved(0))
-        nc.scalar.copy(out=first[:, 1], in_=interleaved(1))
-        nc.scalar.copy(out=second[:, 0], in_=interleaved(2))
-        nc.vector.tensor_copy(out=second[:, 1], in_=interleaved(3))
+        round_into(nc.scalar.copy, first[:, 0], 0)
+        round_into(nc.scalar.copy, first[:, 1], 1)
+        round_into(nc.scalar.copy, second[:, 0], 2)
+        round_into(nc.vector.tensor_copy, second[:, 1], 3)
         hand_on(0, 2, first.rearrange("p b v t -> p (b v t)"))
         store_words(0)
         for i in range(2):

@@ -7,9 +7,8 @@ K, T, N = 512, 512, 512
 D = 4
 P = 128
 PACK = 4
-RING = 8
-WHOLE = (1,)
 SPLIT = 88
+LAG = 11
 FLOPS = 2 * K * T * N
 
 F32 = mybir.dt.float32
@@ -28,6 +27,7 @@ def tile_picked_whuber_none_lo_kernel(
 ):
     nc = tc.nc
     blocks = T // P
+    half = T // 2
 
     with ExitStack() as ctx:
         keep = ctx.enter_context(tc.tile_pool(name="keep", bufs=1))
@@ -61,46 +61,37 @@ def tile_picked_whuber_none_lo_kernel(
             out=b_rows[0:blocks, :],
             in_=bound[0:1, :].rearrange("o (c v) -> (o c) v", c=blocks),
         )
-        b_last = keep.tile([P, P], F32, name="b_last")
-        nc.sync.dma_start(out=b_last[:], in_=bound[:, T - P : T])
 
         ident = keep.tile([P, P], F32, name="ident")
         make_identity(nc, ident[:])
 
-        b_ps = bank(7, "b_ps")
-        nc.tensor.transpose(b_ps[:, 0, :], b_rows[:], ident[:])
-        b_cols = keep.tile([P, 3, 8], F32, name="b_cols")
-        b_hi, b_two, b_off = (b_cols[:, i, 0:blocks] for i in range(3))
-        for target, factor in ((b_hi, 1.0), (b_two, 2.0), (b_off, -float(D))):
-            nc.scalar.activation(target, b_ps[:, 0, 0:blocks], ACT.Copy, scale=factor)
-        top_last = keep.tile([P, P], F32, name="top_last")
-        nc.scalar.activation(top_last[:], b_last[:], ACT.Relu, scale=2.0)
-
         w_src = w_raw[:].rearrange("p j (m t) -> p t m j", t=PACK)
         w_codes = keep.tile([P, N], U32, name="w_codes", align_bytes=64)
         w_plane = keep.tile([P, N], U8, name="w_plane", align_bytes=64)
-        w_one = keep.tile([P, P, PACK], BF16, name="w_one", align_bytes=64)
-        w_two = keep.tile([P, 2, P, PACK], BF16, name="w_two", align_bytes=64)
-        nc.scalar.copy(out=w_one[:, SPLIT:P, :], in_=w_src[:, 0, SPLIT:P, :])
-        nc.scalar.copy(
-            out=w_two[:].rearrange("p t m j -> p m t j"),
-            in_=w_src[:, 2:4].rearrange("p t m j -> p m t j"),
-        )
+        w_bf = keep.tile([P, 3 * P * PACK], BF16, name="w_bf", align_bytes=64)
 
         def quantise(first, count, source):
             cols = slice(first * P, (first + count) * P)
             nc.vector.quantize_mx(out=w_codes[:, cols].bitcast(FP8X4), scales=w_plane[:, cols], in_=source)
 
-        nc.vector.tensor_copy(out=w_one[:, 0:SPLIT, :], in_=w_src[:, 0, 0:SPLIT, :])
-        quantise(0, 1, w_one[:].rearrange("p m j -> p (m j)"))
-        nc.vector.tensor_copy(out=w_one[:], in_=w_src[:, 1])
-        quantise(1, 1, w_one[:].rearrange("p m j -> p (m j)"))
+        def slots(first, count):
+            return w_bf[:, first * P * PACK : (first + count) * P * PACK]
 
-        y_win = [keep.tile([P, 2 * T if t in WHOLE else T], F32, name="y_win%d" % t) for t in range(PACK)]
-        for t in WHOLE:
-            nc.gpsimd.memset(y_win[t][:, T : 2 * T], 0.0)
+        def round_pair(copy, h, part):
+            copy(
+                out=slots(1 - h, 2).rearrange("p (t m j) -> p m t j", t=2, j=PACK)[:, part],
+                in_=w_src[:, 2 * h : 2 * h + 2, part, :].rearrange("p t m j -> p m t j"),
+            )
+
+        round_pair(nc.vector.tensor_copy, 0, slice(0, SPLIT))
+        round_pair(nc.scalar.copy, 0, slice(SPLIT, P))
+        for t in range(2):
+            quantise(t, 1, slots(1 + t, 1))
+        round_pair(nc.vector.tensor_copy, 1, slice(0, P))
+        quantise(2, 2, slots(0, 2))
+
+        y_win = [keep.tile([P, T], F32, name="y_win%d" % t) for t in range(PACK)]
         y_own = keep.tile([P, PACK, T], F32, name="y_own")
-        half = T // 2
 
         def product(t, target, cols):
             nc.tensor.matmul_mx(
@@ -124,103 +115,108 @@ def tile_picked_whuber_none_lo_kernel(
             else:
                 nc.vector.tensor_copy(out=y_win[0][:, cols], in_=flat)
                 nc.scalar.copy(out=y_own[:, 0, cols], in_=flat)
-        quantise(2, 2, w_two[:].rearrange("p t m j -> p (t m j)"))
         for t in range(1, PACK):
             y_ps = bank(t, "y_ps%d" % t)
             flat = y_ps[:].rearrange("p a b -> p (a b)")
             product(t, flat, slice(0, T))
-            nc.scalar.copy(out=y_win[t][:, 0:T], in_=flat)
-            nc.sync.dma_start(out=y_own[:, t, :], in_=y_win[t][:, 0:T])
+            nc.scalar.copy(out=y_win[t][:], in_=flat)
+            nc.sync.dma_start(out=y_own[:, t, :], in_=y_win[t][:])
+
+        b_ps = bank(4, "b_ps")
+        nc.tensor.transpose(b_ps[:, 0, :], b_rows[:], ident[:])
+        b_cols = keep.tile([P, 4, 8], F32, name="b_cols")
+        b_hi, b_two, b_off, b_low = (b_cols[:, i, 0:blocks] for i in range(4))
+        for target, factor in ((b_hi, 1.0), (b_two, 2.0), (b_off, -float(D)), (b_low, -1.0)):
+            nc.scalar.activation(target, b_ps[:, 0, 0:blocks], ACT.Copy, scale=factor)
 
         def turn_into(target, source, start, stop):
             nc.tensor.matmul(target, lhsT=source, rhs=ident[:], start=start, stop=stop, is_transpose=True)
+
+        def col(cols, vb):
+            return cols[:, vb : vb + 1]
 
         o_codes = keep.tile([P, T], U32, name="o_codes", align_bytes=64)
         o_plane = keep.tile([P, T], U8, name="o_plane", align_bytes=64)
         out_rows = out_0.rearrange("(p t) v -> p t v", t=PACK)
         out_words = out_1[0].rearrange("p c r -> p (c r)").bitcast(I32)
 
-        ring = keep.tile([P, RING * 2 * P], F32, name="ring")
-        shared = keep.tile([P, 8 * P], F32, name="shared", align_bytes=64)
+        pairs = [(0, 0), (0, 2), (1, 0), (2, 0), (3, 0), (1, 2), (2, 2), (3, 2)]
+        last = len(pairs) - 1
+        strip = keep.tile([P, (LAG + 4 * last) * half], F32, name="strip")
+        last_raw = keep.tile([P, D * P], F32, name="last_raw", align_bytes=64)
+
+        def piece(first, count):
+            return strip[:, first * half : (first + count) * half]
+
+        def place(g):
+            return LAG + 4 * (last - 2) + 2 if g == D * last + D - 1 else g
+
         acc = {}
-        res = {vb: keep.tile([P, PACK, P], F32, name="res%d" % vb) for vb in range(blocks)}
-        turns = [0, 0]
 
-        def next_bank(name):
-            turns[1] = turns[1] + 1
-            return bank(4 + turns[1] % 4, name)
+        def gather(n):
+            t, vb = pairs[n]
+            banks = [bank(4 + (2 * n + e + 1) % 4, "pull%d_%d" % (n, e)) for e in range(2)]
+            for d in range(D):
+                picked = piece(place(D * n + d), 1)
+                nc.vector.tensor_tensor(
+                    picked,
+                    y_win[t][:].indirect(lists[d][:, vb * P // 16 : (vb + 2) * P // 16]),
+                    y_own[:, t, vb * P : (vb + 2) * P],
+                    ALU.subtract,
+                )
+                for e in range(2):
+                    turn_into(banks[e][:, d, :], picked[:, e * P : (e + 1) * P], True, True)
+            return banks
 
-        def next_slot(count):
-            slot = turns[0] % RING
-            turns[0] = turns[0] + (count + 1) // 2
-            first = slot * 2 * P + (P if count == 1 and slot % 2 == 0 else 0)
-            return slice(first, first + count * P)
+        def first_pass(raw, pulls, v):
+            nc.scalar.activation(raw, pulls, ACT.Relu, bias=col(b_hi, v), scale=-1.0)
 
-        def pick(target, t, vb, count, d, own):
-            nc.vector.tensor_tensor(
-                target,
-                y_win[t][:].indirect(lists[d][:, vb * P // 16 : (vb + count) * P // 16]),
-                own,
-                ALU.subtract,
-            )
-
-        def col(cols, vb):
-            return cols[:, vb : vb + 1]
-
-        def gather(t, vb, count, ds):
-            share = D // len(ds)
-            banks = [next_bank("pull%d_%d_%d_%d" % (t, vb, ds[0], i)) for i in range((count + share - 1) // share)]
-            places = {}
-            for e in range(count):
-                first = (e % share) * len(ds)
-                places[vb + e] = banks[e // share][:, first : first + len(ds), :]
-            for i, d in enumerate(ds):
-                picked = ring[:, next_slot(count)]
-                pick(picked, t, vb, count, d, y_own[:, t, vb * P : (vb + count) * P])
-                for e in range(count):
-                    turn_into(places[vb + e][:, i, :], picked[:, e * P : (e + 1) * P], True, True)
-            return places
-
-        def clip(t, ds, places, last):
-            raw = {}
-            done = {}
-            for v, place in places.items():
-                if last:
-                    raw[v] = shared[:, 3 * P : 7 * P].rearrange("p (d v) -> p d v", d=D)
-                else:
-                    raw[v] = keep.tile([P, len(ds), P], F32, name="raw%d_%d_%d" % (t, v, ds[0]))[:]
-                nc.scalar.activation(raw[v], place, ACT.Relu, bias=col(b_hi, v), scale=-1.0)
-            for v in places:
-                done[v] = keep.tile([P, len(ds), P], F32, name="clipped%d_%d_%d" % (t, v, ds[0]))
-                nc.scalar.activation(done[v][:], raw[v], ACT.Relu, bias=col(b_two, v), scale=-1.0)
-            return raw, done
-
-        def turned_rows(v):
-            return PACK - 1 if v == blocks - 1 else PACK
+        def second_pass(done, raw, v):
+            nc.scalar.activation(done, raw, ACT.Relu, bias=col(b_two, v), scale=-1.0)
 
         def open_sums(v):
             acc[v] = bank(v, "acc%d" % v)
-            for t in range(turned_rows(v)):
+            for t in range(PACK - 1 if v >= 2 else PACK):
                 turn_into(acc[v][:, t, :], col(b_off, v).to_broadcast([P, P]), t == 0, False)
 
-        def add_up(t, ds, done):
-            for v, tile in done.items():
-                for i, d in enumerate(ds):
-                    turn_into(acc[v][:, t, :], tile[:, i, :], False, t == turned_rows(v) - 1 and d == D - 1)
+        def add_up(t, v, done, ds):
+            for d in ds:
+                turn_into(acc[v][:, t, :], done[:, d, :], False, t == (PACK - 2 if v == 2 else PACK - 1) and d == D - 1)
 
-        def finish(vb, rows):
+        def clipped(n, e):
+            return keep.tile([P, D, P], F32, name="clipped%d_%d" % (n, e))
+
+        for n in range(last):
+            t, vb = pairs[n]
+            banks = gather(n)
+            raws = [piece(LAG + 4 * n + 2 * e, 2).rearrange("p (d v) -> p d v", d=D) for e in range(2)]
+            for e in range(2):
+                first_pass(raws[e], banks[e][:], vb + e)
+            if t == 0:
+                open_sums(vb)
+                open_sums(vb + 1)
+            for e in range(2):
+                done = clipped(n, e)
+                second_pass(done[:], raws[e], vb + e)
+                add_up(t, vb + e, done, range(D))
+
+        res = {
+            0: piece(D * last + 1, 2).rearrange("p (t v) -> p t v", t=PACK),
+            1: piece(place(D * last + 3), 2).rearrange("p (t v) -> p t v", t=PACK),
+            2: keep.tile([P, PACK, P], F32, name="res2")[:],
+            3: keep.tile([P, PACK, P], F32, name="res3")[:],
+        }
+
+        def finish(vb, rows, sums):
             cols = slice(vb * P, (vb + 1) * P)
-            nc.vector.scalar_tensor_tensor(
-                res[vb][:, rows, :], acc[vb][:, rows, :], 1.0 / D, y_own[:, rows, cols], ALU.mult, ALU.add
-            )
-
-        def store(vb):
-            nc.sync.dma_start(out=out_rows[:, :, vb * P : (vb + 1) * P], in_=res[vb][:])
+            nc.vector.scalar_tensor_tensor(res[vb][:, rows, :], sums, 1.0 / D, y_own[:, rows, cols], ALU.mult, ALU.add)
+            if rows.stop == PACK:
+                nc.sync.dma_start(out=out_rows[:, :, cols], in_=res[vb])
 
         def round_into(copy, target, vb):
             copy(
                 out=target.rearrange("p (c i) t -> p c t i", i=4),
-                in_=res[vb][:].rearrange("p t (c i) -> p c t i", i=4),
+                in_=res[vb].rearrange("p t (c i) -> p c t i", i=4),
             )
 
         def hand_on(vb, count, rounded):
@@ -231,58 +227,35 @@ def tile_picked_whuber_none_lo_kernel(
             cols = slice(h * half, (h + 1) * half)
             nc.sync.dma_start(out=out_words[:, cols], in_=o_codes[:, cols].bitcast(I32))
 
-        every = (0, 1, 2, 3)
-        units = [(0, 0, 2, every), (0, 2, 2, every), (1, 0, 4, (0, 1)), (1, 0, 4, (2, 3))] + [(2, 0, 2, every), (3, 0, 2, every), (2, 2, 1, every), (3, 2, 1, every), (2, 3, 1, every)]
-        raws = []
-        dones = []
-        for n, (t, vb, count, ds) in enumerate(units):
-            raw, done = clip(t, ds, gather(t, vb, count, ds), n == len(units) - 1)
-            raws.append(raw)
-            dones.append(done)
-            if n < 2:
-                open_sums(2 * n)
-                open_sums(2 * n + 1)
-            if n > 0:
-                add_up(units[n - 1][0], units[n - 1][3], dones[n - 1])
-
-        for v in range(2):
-            finish(v, slice(0, PACK))
-            store(v)
-
-        t, vb = PACK - 1, blocks - 1
-        cols = slice(vb * P, (vb + 1) * P)
-        base = keep.tile([P, P], F32, name="base")
-        nc.vector.tensor_tensor(base[:], y_own[:, t, cols], b_last[:], ALU.subtract)
-        lifted = [next_slot(1) for d in range(D)]
-        held = raws[-2][2]
-        sums = dones[-2][2]
-        add_up(units[-1][0], every, dones[-1])
-        for d in range(D):
-            pick(ring[:, lifted[d]], t, vb, 1, d, base[:])
-        finish(2, slice(0, PACK))
-        store(2)
-        finish(vb, slice(0, t))
-        top_two = top_last[:].unsqueeze(1).to_broadcast([P, 2, P])
-        for i in range(2):
-            nc.vector.scalar_tensor_tensor(
-                held[:, 2 * i : 2 * i + 2, :],
-                ring[:, lifted[2 * i].start : lifted[2 * i + 1].stop].rearrange("p (d v) -> p d v", d=2),
-                0.0, top_two, ALU.max, ALU.min,
-            )
-        nc.vector.tensor_tensor(sums[:, 0:2, :], held[:, 0:2, :], held[:, 2:4, :], ALU.add)
-        nc.vector.scalar_tensor_tensor(sums[:, 2, :], sums[:, 0, :], 1.0 / D, base[:], ALU.mult, ALU.add)
-        nc.vector.scalar_tensor_tensor(res[vb][:, t, :], sums[:, 1, :], 1.0 / D, sums[:, 2, :], ALU.mult, ALU.add)
-        store(vb)
-        first = shared[:, 3 * P : 7 * P].bitcast(BF16).rearrange("p (b v t) -> p b v t", b=2, t=PACK)
+        t, vb = pairs[last]
+        banks = gather(last)
+        raw = last_raw[:].rearrange("p (d v) -> p d v", d=D)
+        done = [clipped(last, e) for e in range(2)]
+        for ds in (slice(0, 2), slice(2, 4)):
+            first_pass(raw[:, ds, :], banks[0][:, ds, :], vb)
+        finish(0, slice(0, PACK), acc[0][:])
+        nc.vector.tensor_scalar(done[1][:], banks[1][:], col(b_hi, vb + 1), col(b_low, vb + 1), ALU.min, ALU.max)
+        add_up(t, vb + 1, done[1], range(D))
+        late = bank(5, "late")
+        turn_into(late[:, 0, :], col(b_off, vb).to_broadcast([P, P]), True, False)
+        for ds in (slice(0, 2), slice(2, 4)):
+            second_pass(done[0][:, ds, :], raw[:, ds, :], vb)
+            for d in range(ds.start, ds.stop):
+                turn_into(late[:, 0, :], done[0][:, d, :], False, d == D - 1)
+        finish(1, slice(0, PACK), acc[1][:])
+        finish(2, slice(0, t), acc[2][:, 0:t, :])
+        finish(3, slice(0, PACK), acc[3][:])
+        finish(2, slice(t, PACK), late[:, 0:1, :])
+        first = last_raw[:].bitcast(BF16).rearrange("p (b v t) -> p b v t", b=2, t=PACK)
         second = keep.tile([P, 2, P, PACK], BF16, name="second", align_bytes=64)
         round_into(nc.scalar.copy, first[:, 0], 0)
         round_into(nc.scalar.copy, first[:, 1], 1)
-        round_into(nc.scalar.copy, second[:, 0], 2)
-        round_into(nc.vector.tensor_copy, second[:, 1], 3)
+        round_into(nc.scalar.copy, second[:, 1], 3)
         hand_on(0, 2, first.rearrange("p b v t -> p (b v t)"))
         store_words(0)
-        for i in range(2):
-            hand_on(2 + i, 1, second[:, i].rearrange("p v t -> p (v t)"))
+        round_into(nc.vector.tensor_copy, second[:, 0], 2)
+        hand_on(3, 1, second[:, 1].rearrange("p v t -> p (v t)"))
+        hand_on(2, 1, second[:, 0].rearrange("p v t -> p (v t)"))
         store_words(1)
 
         for q in range(4):

@@ -1,14 +1,15 @@
 from contextlib import ExitStack
 
 import concourse.mybir as mybir
-from concourse.masks import make_identity
 
 K, T, N = 512, 512, 512
 D = 4
 P = 128
 PACK = 4
+QUAD = 32
 SPLIT = 88
-LAG = 11
+LAG = 9
+EARLY = 2
 FLOPS = 2 * K * T * N
 
 F32 = mybir.dt.float32
@@ -36,6 +37,11 @@ def tile_picked_whuber_none_lo_kernel(
         def bank(b, name):
             return psum.tile([P, 4, P], F32, name=name, tag="bank%d" % b)
 
+        b_rows = keep.tile([P, P], F32, name="b_rows")
+        nc.sync.dma_start(
+            out=b_rows[0:QUAD, :],
+            in_=bound[0 : QUAD // blocks, :].rearrange("o (c v) -> (o c) v", c=blocks),
+        )
         w_raw = keep.tile([P, PACK, N], F32, name="w_raw")
         nc.sync.dma_start(out=w_raw[:], in_=w1.rearrange("(p j) n -> p j n", j=PACK))
         x_codes = keep.tile([P, T], U32, name="x_codes", align_bytes=64)
@@ -47,7 +53,7 @@ def tile_picked_whuber_none_lo_kernel(
         nc.vector.memset(x_plane[:].bitcast(I32), 0)
         for q in range(4):
             nc.scalar.dma_start(
-                out=x_plane[32 * q : 32 * q + 4, :].bitcast(I32),
+                out=x_plane[QUAD * q : QUAD * q + 4, :].bitcast(I32),
                 in_=x_scales[0, 4 * q : 4 * q + 4, :].bitcast(I32),
             )
         lists = []
@@ -55,15 +61,44 @@ def tile_picked_whuber_none_lo_kernel(
             tile = keep.tile([P, T // 16], U16, name="list%d" % d)
             nc.sync.dma_start(tile[:], pos)
             lists.append(tile)
-        b_rows = keep.tile([P, P], F32, name="b_rows")
-        nc.gpsimd.memset(b_rows[:], 0.0)
-        nc.sync.dma_start(
-            out=b_rows[0:blocks, :],
-            in_=bound[0:1, :].rearrange("o (c v) -> (o c) v", c=blocks),
-        )
 
         ident = keep.tile([P, P], F32, name="ident")
-        make_identity(nc, ident[:])
+        ones = keep.tile([P, P], F32, name="ones")
+        along = keep.tile([P, P], F32, name="along", align_bytes=64)
+        across = keep.tile([P, P], F32, name="across", align_bytes=64)
+        nc.vector.memset(ones[:], 1.0)
+        nc.vector.memset(b_rows[QUAD : 2 * QUAD, :], 0.0)
+        nc.vector.tensor_tensor_scan(along[:], ones[:], ones[:], 0.0, ALU.mult, ALU.add)
+        nc.vector.memset(b_rows[2 * QUAD : P, :], 0.0)
+        nc.vector.transpose(across[:], along[:])
+        for q in range(P // QUAD):
+            rows = slice(QUAD * q, QUAD * (q + 1))
+            nc.vector.tensor_scalar(
+                ident[rows, :], along[rows, :], across[rows, QUAD * q : QUAD * q + 1], None, ALU.is_equal
+            )
+
+        def turn_into(target, source, start, stop):
+            nc.tensor.matmul(target, lhsT=source, rhs=ident[:], start=start, stop=stop, is_transpose=True)
+
+        def col(cols, vb):
+            return cols[:, vb : vb + 1]
+
+        b_ps = bank(7, "b_ps")
+        turn_into(b_ps[:, 0, :], b_rows[:], True, True)
+        b_cols = keep.tile([P, 4, 8], F32, name="b_cols")
+        b_off, b_hi, b_two, b_low = (b_cols[:, i, 0:blocks] for i in range(4))
+        for target, factor in ((b_off, -float(D)), (b_hi, 1.0), (b_two, 2.0), (b_low, -1.0)):
+            nc.scalar.activation(target, b_ps[:, 0, 0:blocks], ACT.Copy, scale=factor)
+
+        acc = {}
+
+        def open_sums(v):
+            acc[v] = bank(v, "acc%d" % v)
+            for t in range(PACK - 1 if v >= 2 else PACK):
+                turn_into(acc[v][:, t, :], col(b_off, v).to_broadcast([P, P]), t == 0, False)
+
+        for v in range(EARLY):
+            open_sums(v)
 
         w_src = w_raw[:].rearrange("p j (m t) -> p t m j", t=PACK)
         w_codes = keep.tile([P, N], U32, name="w_codes", align_bytes=64)
@@ -106,7 +141,7 @@ def tile_picked_whuber_none_lo_kernel(
 
         for h in range(2):
             cols = slice(h * half, (h + 1) * half)
-            y_ps = bank(4 * h, "y_half%d" % h)
+            y_ps = bank(2 + h, "y_half%d" % h)
             flat = y_ps[:].rearrange("p a b -> p (a b)")[:, 0:half]
             product(0, flat, cols)
             if h == 0:
@@ -116,32 +151,19 @@ def tile_picked_whuber_none_lo_kernel(
                 nc.vector.tensor_copy(out=y_win[0][:, cols], in_=flat)
                 nc.scalar.copy(out=y_own[:, 0, cols], in_=flat)
         for t in range(1, PACK):
-            y_ps = bank(t, "y_ps%d" % t)
+            y_ps = bank(3 + t, "y_ps%d" % t)
             flat = y_ps[:].rearrange("p a b -> p (a b)")
             product(t, flat, slice(0, T))
             nc.scalar.copy(out=y_win[t][:], in_=flat)
             nc.sync.dma_start(out=y_own[:, t, :], in_=y_win[t][:])
-
-        b_ps = bank(4, "b_ps")
-        nc.tensor.transpose(b_ps[:, 0, :], b_rows[:], ident[:])
-        b_cols = keep.tile([P, 4, 8], F32, name="b_cols")
-        b_hi, b_two, b_off, b_low = (b_cols[:, i, 0:blocks] for i in range(4))
-        for target, factor in ((b_hi, 1.0), (b_two, 2.0), (b_off, -float(D)), (b_low, -1.0)):
-            nc.scalar.activation(target, b_ps[:, 0, 0:blocks], ACT.Copy, scale=factor)
-
-        def turn_into(target, source, start, stop):
-            nc.tensor.matmul(target, lhsT=source, rhs=ident[:], start=start, stop=stop, is_transpose=True)
-
-        def col(cols, vb):
-            return cols[:, vb : vb + 1]
 
         o_codes = keep.tile([P, T], U32, name="o_codes", align_bytes=64)
         o_plane = keep.tile([P, T], U8, name="o_plane", align_bytes=64)
         out_rows = out_0.rearrange("(p t) v -> p t v", t=PACK)
         out_words = out_1[0].rearrange("p c r -> p (c r)").bitcast(I32)
 
-        pairs = [(0, 0), (0, 2), (1, 0), (2, 0), (3, 0), (1, 2), (2, 2), (3, 2)]
-        last = len(pairs) - 1
+        units = [(1, 0, 2), (2, 0, 2), (3, 0, 2), (1, 2, 2), (2, 2, 2)]
+        last = 7
         strip = keep.tile([P, (LAG + 4 * last) * half], F32, name="strip")
         last_raw = keep.tile([P, D * P], F32, name="last_raw", align_bytes=64)
 
@@ -149,22 +171,22 @@ def tile_picked_whuber_none_lo_kernel(
             return strip[:, first * half : (first + count) * half]
 
         def place(g):
-            return LAG + 4 * (last - 2) + 2 if g == D * last + D - 1 else g
+            return g
 
-        acc = {}
-
-        def gather(n):
-            t, vb = pairs[n]
-            banks = [bank(4 + (2 * n + e + 1) % 4, "pull%d_%d" % (n, e)) for e in range(2)]
+        def gather(step, t, vb, count):
+            banks = [bank(4 + (step + e + 3) % 4, "pull%d" % (step + e)) for e in range(count)]
             for d in range(D):
-                picked = piece(place(D * n + d), 1)
+                if count == 2:
+                    picked = piece(place(2 * step + d), 1)
+                else:
+                    picked = piece(2 * step, 2)[:, d * P : (d + 1) * P]
                 nc.vector.tensor_tensor(
                     picked,
-                    y_win[t][:].indirect(lists[d][:, vb * P // 16 : (vb + 2) * P // 16]),
-                    y_own[:, t, vb * P : (vb + 2) * P],
+                    y_win[t][:].indirect(lists[d][:, vb * P // 16 : (vb + count) * P // 16]),
+                    y_own[:, t, vb * P : (vb + count) * P],
                     ALU.subtract,
                 )
-                for e in range(2):
+                for e in range(count):
                     turn_into(banks[e][:, d, :], picked[:, e * P : (e + 1) * P], True, True)
             return banks
 
@@ -174,34 +196,52 @@ def tile_picked_whuber_none_lo_kernel(
         def second_pass(done, raw, v):
             nc.scalar.activation(done, raw, ACT.Relu, bias=col(b_two, v), scale=-1.0)
 
-        def open_sums(v):
-            acc[v] = bank(v, "acc%d" % v)
-            for t in range(PACK - 1 if v >= 2 else PACK):
-                turn_into(acc[v][:, t, :], col(b_off, v).to_broadcast([P, P]), t == 0, False)
-
         def add_up(t, v, done, ds):
             for d in ds:
                 turn_into(acc[v][:, t, :], done[:, d, :], False, t == (PACK - 2 if v == 2 else PACK - 1) and d == D - 1)
 
-        def clipped(n, e):
-            return keep.tile([P, D, P], F32, name="clipped%d_%d" % (n, e))
+        def clipped(step):
+            return keep.tile([P, D, P], F32, name="clipped%d" % step)
 
-        for n in range(last):
-            t, vb = pairs[n]
-            banks = gather(n)
-            raws = [piece(LAG + 4 * n + 2 * e, 2).rearrange("p (d v) -> p d v", d=D) for e in range(2)]
-            for e in range(2):
+        step = 0
+        for first_list in (0, 2):
+            for vb in (0, 2):
+                pulls = bank(4 + (step + 3) % 4, "pull%d" % step)
+                for i in range(2):
+                    picked = piece(2 * step + i, 1)
+                    nc.vector.tensor_tensor(
+                        picked,
+                        y_win[0][:].indirect(lists[first_list + i][:, vb * P // 16 : (vb + 2) * P // 16]),
+                        y_own[:, 0, vb * P : (vb + 2) * P],
+                        ALU.subtract,
+                    )
+                    for e in range(2):
+                        turn_into(pulls[:, 2 * e + i, :], picked[:, e * P : (e + 1) * P], True, True)
+                raw = piece(LAG + 2 * step, 2).rearrange("p (s v) -> p s v", s=D)
+                done = clipped(step)
+                for e in range(2):
+                    first_pass(raw[:, 2 * e : 2 * e + 2, :], pulls[:, 2 * e : 2 * e + 2, :], vb + e)
+                if step == 0:
+                    for v in range(EARLY, blocks):
+                        open_sums(v)
+                for e in range(2):
+                    second_pass(done[:, 2 * e : 2 * e + 2, :], raw[:, 2 * e : 2 * e + 2, :], vb + e)
+                    for i in range(2):
+                        turn_into(acc[vb + e][:, 0, :], done[:, 2 * e + i, :], False, False)
+                step = step + 1
+        for t, vb, count in units:
+            banks = gather(step, t, vb, count)
+            raws = [piece(LAG + 2 * (step + e), 2).rearrange("p (d v) -> p d v", d=D) for e in range(count)]
+            for e in range(count):
                 first_pass(raws[e], banks[e][:], vb + e)
-            if t == 0:
-                open_sums(vb)
-                open_sums(vb + 1)
-            for e in range(2):
-                done = clipped(n, e)
+            for e in range(count):
+                done = clipped(step + e)
                 second_pass(done[:], raws[e], vb + e)
                 add_up(t, vb + e, done, range(D))
+            step = step + count
 
         res = {
-            0: piece(D * last + 1, 2).rearrange("p (t v) -> p t v", t=PACK),
+            0: piece(place(D * last + 1), 2).rearrange("p (t v) -> p t v", t=PACK),
             1: piece(place(D * last + 3), 2).rearrange("p (t v) -> p t v", t=PACK),
             2: keep.tile([P, PACK, P], F32, name="res2")[:],
             3: keep.tile([P, PACK, P], F32, name="res3")[:],
@@ -227,16 +267,16 @@ def tile_picked_whuber_none_lo_kernel(
             cols = slice(h * half, (h + 1) * half)
             nc.sync.dma_start(out=out_words[:, cols], in_=o_codes[:, cols].bitcast(I32))
 
-        t, vb = pairs[last]
-        banks = gather(last)
+        t, vb = PACK - 1, 2
+        banks = gather(step, t, vb, 2)
         raw = last_raw[:].rearrange("p (d v) -> p d v", d=D)
-        done = [clipped(last, e) for e in range(2)]
+        done = [clipped(step + e) for e in range(2)]
         for ds in (slice(0, 2), slice(2, 4)):
             first_pass(raw[:, ds, :], banks[0][:, ds, :], vb)
         finish(0, slice(0, PACK), acc[0][:])
         nc.vector.tensor_scalar(done[1][:], banks[1][:], col(b_hi, vb + 1), col(b_low, vb + 1), ALU.min, ALU.max)
         add_up(t, vb + 1, done[1], range(D))
-        late = bank(5, "late")
+        late = bank(4 + (step + 1) % 4, "late")
         turn_into(late[:, 0, :], col(b_off, vb).to_broadcast([P, P]), True, False)
         for ds in (slice(0, 2), slice(2, 4)):
             second_pass(done[0][:, ds, :], raw[:, ds, :], vb)
@@ -262,5 +302,5 @@ def tile_picked_whuber_none_lo_kernel(
             queue = nc.sync if q % 2 == 0 else nc.scalar
             queue.dma_start(
                 out=out_2[0, 4 * q : 4 * q + 4, :].bitcast(I32),
-                in_=o_plane[32 * q : 32 * q + 4, :].bitcast(I32),
+                in_=o_plane[QUAD * q : QUAD * q + 4, :].bitcast(I32),
             )

@@ -37,6 +37,9 @@ def tile_picked_whuber_none_lo_kernel(
         def bank(b, name):
             return psum.tile([P, 4, P], F32, name=name, tag="bank%d" % b)
 
+        def pull_bank(step, name):
+            return bank(4 + (step + 3) % 4, name)
+
         b_rows = keep.tile([P, P], F32, name="b_rows")
         nc.sync.dma_start(
             out=b_rows[0:QUAD, :],
@@ -51,7 +54,7 @@ def tile_picked_whuber_none_lo_kernel(
         )
         x_plane = keep.tile([P, T], U8, name="x_plane", align_bytes=64)
         nc.vector.memset(x_plane[:].bitcast(I32), 0)
-        for q in range(4):
+        for q in range(P // QUAD):
             nc.scalar.dma_start(
                 out=x_plane[QUAD * q : QUAD * q + 4, :].bitcast(I32),
                 in_=x_scales[0, 4 * q : 4 * q + 4, :].bitcast(I32),
@@ -80,22 +83,28 @@ def tile_picked_whuber_none_lo_kernel(
         def turn_into(target, source, start, stop):
             nc.tensor.matmul(target, lhsT=source, rhs=ident[:], start=start, stop=stop, is_transpose=True)
 
-        def col(cols, vb):
-            return cols[:, vb : vb + 1]
+        def col(cols, v):
+            return cols[:, v : v + 1]
 
-        b_ps = bank(7, "b_ps")
+        b_ps = pull_bank(0, "b_ps")
         turn_into(b_ps[:, 0, :], b_rows[:], True, True)
         b_cols = keep.tile([P, 4, 8], F32, name="b_cols")
         b_off, b_hi, b_two, b_low = (b_cols[:, i, 0:blocks] for i in range(4))
         for target, factor in ((b_off, -float(D)), (b_hi, 1.0), (b_two, 2.0), (b_low, -1.0)):
             nc.scalar.activation(target, b_ps[:, 0, 0:blocks], ACT.Copy, scale=factor)
 
-        acc = {}
+        sums = {}
+
+        def rows_in_sums(v):
+            return PACK if v < 2 else PACK - 1
+
+        def offset_into(target, v, start):
+            turn_into(target, col(b_off, v).to_broadcast([P, P]), start, False)
 
         def open_sums(v):
-            acc[v] = bank(v, "acc%d" % v)
-            for t in range(PACK - 1 if v >= 2 else PACK):
-                turn_into(acc[v][:, t, :], col(b_off, v).to_broadcast([P, P]), t == 0, False)
+            sums[v] = bank(v, "sums%d" % v)
+            for t in range(rows_in_sums(v)):
+                offset_into(sums[v][:, t, :], v, t == 0)
 
         for v in range(EARLY):
             open_sums(v)
@@ -105,25 +114,25 @@ def tile_picked_whuber_none_lo_kernel(
         w_plane = keep.tile([P, N], U8, name="w_plane", align_bytes=64)
         w_bf = keep.tile([P, 3 * P * PACK], BF16, name="w_bf", align_bytes=64)
 
-        def quantise(first, count, source):
-            cols = slice(first * P, (first + count) * P)
-            nc.vector.quantize_mx(out=w_codes[:, cols].bitcast(FP8X4), scales=w_plane[:, cols], in_=source)
-
-        def slots(first, count):
+        def places(first, count):
             return w_bf[:, first * P * PACK : (first + count) * P * PACK]
 
         def round_pair(copy, h, part):
             copy(
-                out=slots(1 - h, 2).rearrange("p (t m j) -> p m t j", t=2, j=PACK)[:, part],
-                in_=w_src[:, 2 * h : 2 * h + 2, part, :].rearrange("p t m j -> p m t j"),
+                out=places(1 - h, 2).rearrange("p (t m j) -> p m j t", t=2, j=PACK)[:, part],
+                in_=w_src[:, 2 * h : 2 * h + 2, part, :].rearrange("p t m j -> p m j t"),
             )
+
+        def quantise(first, count, source):
+            cols = slice(first * P, (first + count) * P)
+            nc.vector.quantize_mx(out=w_codes[:, cols].bitcast(FP8X4), scales=w_plane[:, cols], in_=source)
 
         round_pair(nc.vector.tensor_copy, 0, slice(0, SPLIT))
         round_pair(nc.scalar.copy, 0, slice(SPLIT, P))
         for t in range(2):
-            quantise(t, 1, slots(1 + t, 1))
+            quantise(t, 1, places(1 + t, 1))
         round_pair(nc.vector.tensor_copy, 1, slice(0, P))
-        quantise(2, 2, slots(0, 2))
+        quantise(2, 2, places(0, 2))
 
         y_win = [keep.tile([P, T], F32, name="y_win%d" % t) for t in range(PACK)]
         y_own = keep.tile([P, PACK, T], F32, name="y_own")
@@ -139,20 +148,14 @@ def tile_picked_whuber_none_lo_kernel(
                 stop=True,
             )
 
-        for h in range(2):
+        for h, copy in enumerate((nc.scalar.copy, nc.vector.tensor_copy)):
             cols = slice(h * half, (h + 1) * half)
-            y_ps = bank(2 + h, "y_half%d" % h)
-            flat = y_ps[:].rearrange("p a b -> p (a b)")[:, 0:half]
+            flat = bank(EARLY + h, "y_half%d" % h)[:].rearrange("p a b -> p (a b)")[:, 0:half]
             product(0, flat, cols)
-            if h == 0:
-                nc.scalar.copy(out=y_win[0][:, cols], in_=flat)
-                nc.scalar.copy(out=y_own[:, 0, cols], in_=flat)
-            else:
-                nc.vector.tensor_copy(out=y_win[0][:, cols], in_=flat)
-                nc.scalar.copy(out=y_own[:, 0, cols], in_=flat)
+            copy(out=y_win[0][:, cols], in_=flat)
+            nc.scalar.copy(out=y_own[:, 0, cols], in_=flat)
         for t in range(1, PACK):
-            y_ps = bank(3 + t, "y_ps%d" % t)
-            flat = y_ps[:].rearrange("p a b -> p (a b)")
+            flat = pull_bank(t, "y_ps%d" % t)[:].rearrange("p a b -> p (a b)")
             product(t, flat, slice(0, T))
             nc.scalar.copy(out=y_win[t][:], in_=flat)
             nc.sync.dma_start(out=y_own[:, t, :], in_=y_win[t][:])
@@ -162,130 +165,112 @@ def tile_picked_whuber_none_lo_kernel(
         out_rows = out_0.rearrange("(p t) v -> p t v", t=PACK)
         out_words = out_1[0].rearrange("p c r -> p (c r)").bitcast(I32)
 
-        units = [(1, 0, 2), (2, 0, 2), (3, 0, 2), (1, 2, 2), (2, 2, 2)]
-        last = 7
-        strip = keep.tile([P, (LAG + 4 * last) * half], F32, name="strip")
+        every = tuple(range(D))
+        units = [(0, vb, ds) for ds in (every[:2], every[2:]) for vb in (0, 2)]
+        units = units + [(t, vb, every) for vb in (0, 2) for t in range(1, PACK)]
+        steps = PACK * blocks
+        gathers = 2 * steps
+
+        strip = keep.tile([P, (LAG + gathers - D) * half], F32, name="strip")
+        ends = keep.tile([P, D, D * P], F32, name="ends")
+        ends_step = (gathers - 1 - LAG) // 2
         last_raw = keep.tile([P, D * P], F32, name="last_raw", align_bytes=64)
 
         def piece(first, count):
             return strip[:, first * half : (first + count) * half]
 
-        def place(g):
-            return g
-
-        def gather(step, t, vb, count):
-            banks = [bank(4 + (step + e + 3) % 4, "pull%d" % (step + e)) for e in range(count)]
-            for d in range(D):
-                if count == 2:
-                    picked = piece(place(2 * step + d), 1)
-                else:
-                    picked = piece(2 * step, 2)[:, d * P : (d + 1) * P]
+        def gather(step, t, vb, ds):
+            banks = [pull_bank(step + i, "pull%d" % (step + i)) for i in range(2 * len(ds) // D)]
+            pulls = [banks[e * len(ds) // D][:, e * len(ds) % D : e * len(ds) % D + len(ds), :] for e in range(2)]
+            for i, d in enumerate(ds):
+                g = 2 * step + i
+                picked = ends[:, 0, 0:half] if g == gathers - 1 else piece(g, 1)
                 nc.vector.tensor_tensor(
                     picked,
-                    y_win[t][:].indirect(lists[d][:, vb * P // 16 : (vb + count) * P // 16]),
-                    y_own[:, t, vb * P : (vb + count) * P],
+                    y_win[t][:].indirect(lists[d][:, vb * P // 16 : (vb + 2) * P // 16]),
+                    y_own[:, t, vb * P : (vb + 2) * P],
                     ALU.subtract,
                 )
-                for e in range(count):
-                    turn_into(banks[e][:, d, :], picked[:, e * P : (e + 1) * P], True, True)
-            return banks
+                for e in range(2):
+                    turn_into(pulls[e][:, i, :], picked[:, e * P : (e + 1) * P], True, True)
+            return pulls
 
         def first_pass(raw, pulls, v):
             nc.scalar.activation(raw, pulls, ACT.Relu, bias=col(b_hi, v), scale=-1.0)
 
-        def second_pass(done, raw, v):
-            nc.scalar.activation(done, raw, ACT.Relu, bias=col(b_two, v), scale=-1.0)
-
-        def add_up(t, v, done, ds):
-            for d in ds:
-                turn_into(acc[v][:, t, :], done[:, d, :], False, t == (PACK - 2 if v == 2 else PACK - 1) and d == D - 1)
-
-        def clipped(step):
-            return keep.tile([P, D, P], F32, name="clipped%d" % step)
+        def second_pass(clipped, raw, v):
+            nc.scalar.activation(clipped, raw, ACT.Relu, bias=col(b_two, v), scale=-1.0)
 
         step = 0
-        for first_list in (0, 2):
-            for vb in (0, 2):
-                pulls = bank(4 + (step + 3) % 4, "pull%d" % step)
-                for i in range(2):
-                    picked = piece(2 * step + i, 1)
-                    nc.vector.tensor_tensor(
-                        picked,
-                        y_win[0][:].indirect(lists[first_list + i][:, vb * P // 16 : (vb + 2) * P // 16]),
-                        y_own[:, 0, vb * P : (vb + 2) * P],
-                        ALU.subtract,
-                    )
-                    for e in range(2):
-                        turn_into(pulls[:, 2 * e + i, :], picked[:, e * P : (e + 1) * P], True, True)
-                raw = piece(LAG + 2 * step, 2).rearrange("p (s v) -> p s v", s=D)
-                done = clipped(step)
-                for e in range(2):
-                    first_pass(raw[:, 2 * e : 2 * e + 2, :], pulls[:, 2 * e : 2 * e + 2, :], vb + e)
-                if step == 0:
-                    for v in range(EARLY, blocks):
-                        open_sums(v)
-                for e in range(2):
-                    second_pass(done[:, 2 * e : 2 * e + 2, :], raw[:, 2 * e : 2 * e + 2, :], vb + e)
-                    for i in range(2):
-                        turn_into(acc[vb + e][:, 0, :], done[:, 2 * e + i, :], False, False)
-                step = step + 1
-        for t, vb, count in units:
-            banks = gather(step, t, vb, count)
-            raws = [piece(LAG + 2 * (step + e), 2).rearrange("p (d v) -> p d v", d=D) for e in range(count)]
-            for e in range(count):
-                first_pass(raws[e], banks[e][:], vb + e)
-            for e in range(count):
-                done = clipped(step + e)
-                second_pass(done[:], raws[e], vb + e)
-                add_up(t, vb + e, done, range(D))
-            step = step + count
+        for t, vb, ds in units[:-1]:
+            pulls = gather(step, t, vb, ds)
+            raws = []
+            for e in range(2):
+                at = step + e * len(ds) // D
+                whole = ends[:, :, 0:P] if at == ends_step else piece(LAG + 2 * at, 2).rearrange("p (d m) -> p d m", d=D)
+                raws.append(whole[:, e * len(ds) % D : e * len(ds) % D + len(ds), :])
+                first_pass(raws[e], pulls[e], vb + e)
+            if step == 0:
+                for v in range(EARLY, blocks):
+                    open_sums(v)
+            for e in range(2):
+                clipped = keep.tile([P, len(ds), P], F32, name="clipped%d_%d" % (step, e))
+                second_pass(clipped[:], raws[e], vb + e)
+                for i, d in enumerate(ds):
+                    closes = t == rows_in_sums(vb + e) - 1 and d == D - 1
+                    turn_into(sums[vb + e][:, t, :], clipped[:, i, :], False, closes)
+            step = step + 2 * len(ds) // D
 
         res = {
-            0: piece(place(D * last + 1), 2).rearrange("p (t v) -> p t v", t=PACK),
-            1: piece(place(D * last + 3), 2).rearrange("p (t v) -> p t v", t=PACK),
+            0: ends[:, 1, :].rearrange("p (t v) -> p t v", t=PACK),
+            1: ends[:, 2, :].rearrange("p (t v) -> p t v", t=PACK),
             2: keep.tile([P, PACK, P], F32, name="res2")[:],
             3: keep.tile([P, PACK, P], F32, name="res3")[:],
         }
 
-        def finish(vb, rows, sums):
-            cols = slice(vb * P, (vb + 1) * P)
-            nc.vector.scalar_tensor_tensor(res[vb][:, rows, :], sums, 1.0 / D, y_own[:, rows, cols], ALU.mult, ALU.add)
+        def finish(v, rows, source):
+            cols = slice(v * P, (v + 1) * P)
+            nc.vector.scalar_tensor_tensor(res[v][:, rows, :], source, 1.0 / D, y_own[:, rows, cols], ALU.mult, ALU.add)
             if rows.stop == PACK:
-                nc.sync.dma_start(out=out_rows[:, :, cols], in_=res[vb])
+                nc.sync.dma_start(out=out_rows[:, :, cols], in_=res[v])
 
-        def round_into(copy, target, vb):
+        def round_into(copy, target, v):
             copy(
                 out=target.rearrange("p (c i) t -> p c t i", i=4),
-                in_=res[vb].rearrange("p t (c i) -> p c t i", i=4),
+                in_=res[v].rearrange("p t (c i) -> p c t i", i=4),
             )
 
-        def hand_on(vb, count, rounded):
-            cols = slice(vb * P, (vb + count) * P)
+        def hand_on(v, count, rounded):
+            cols = slice(v * P, (v + count) * P)
             nc.vector.quantize_mx(out=o_codes[:, cols].bitcast(FP8X4), scales=o_plane[:, cols], in_=rounded)
 
         def store_words(h):
             cols = slice(h * half, (h + 1) * half)
             nc.sync.dma_start(out=out_words[:, cols], in_=o_codes[:, cols].bitcast(I32))
 
-        t, vb = PACK - 1, 2
-        banks = gather(step, t, vb, 2)
-        raw = last_raw[:].rearrange("p (d v) -> p d v", d=D)
-        done = [clipped(step + e) for e in range(2)]
-        for ds in (slice(0, 2), slice(2, 4)):
-            first_pass(raw[:, ds, :], banks[0][:, ds, :], vb)
-        finish(0, slice(0, PACK), acc[0][:])
-        nc.vector.tensor_scalar(done[1][:], banks[1][:], col(b_hi, vb + 1), col(b_low, vb + 1), ALU.min, ALU.max)
-        add_up(t, vb + 1, done[1], range(D))
-        late = bank(4 + (step + 1) % 4, "late")
-        turn_into(late[:, 0, :], col(b_off, vb).to_broadcast([P, P]), True, False)
-        for ds in (slice(0, 2), slice(2, 4)):
-            second_pass(done[0][:, ds, :], raw[:, ds, :], vb)
-            for d in range(ds.start, ds.stop):
-                turn_into(late[:, 0, :], done[0][:, d, :], False, d == D - 1)
-        finish(1, slice(0, PACK), acc[1][:])
-        finish(2, slice(0, t), acc[2][:, 0:t, :])
-        finish(3, slice(0, PACK), acc[3][:])
-        finish(2, slice(t, PACK), late[:, 0:1, :])
+        t, vb, ds = units[-1]
+        pulls = gather(step, t, vb, ds)
+        raw = last_raw[:].rearrange("p (d m) -> p d m", d=D)
+        clipped = [keep.tile([P, D, P], F32, name="clipped_last%d" % e) for e in range(2)]
+        pairs = (slice(0, 2), slice(2, D))
+        for part in pairs:
+            first_pass(raw[:, part, :], pulls[0][:, part, :], vb)
+        for v in range(2):
+            finish(v, slice(0, PACK), sums[v][:])
+        nc.vector.tensor_scalar(clipped[1][:], pulls[1], col(b_hi, vb + 1), col(b_low, vb + 1), ALU.min, ALU.max)
+        late = [pull_bank(steps + e, "late%d" % e) for e in range(2)]
+        for d in ds:
+            turn_into(late[1][:, 0, :], clipped[1][:, d, :], d == 0, d == D - 1)
+        offset_into(late[0][:, 0, :], vb, True)
+        for part in pairs:
+            second_pass(clipped[0][:, part, :], raw[:, part, :], vb)
+            for d in ds[part]:
+                turn_into(late[0][:, 0, :], clipped[0][:, d, :], False, d == D - 1)
+        for v in (vb, vb + 1):
+            finish(v, slice(0, t), sums[v][:, 0:t, :])
+        for e in (1, 0):
+            finish(vb + e, slice(t, PACK), late[e][:, 0:1, :])
+
         first = last_raw[:].bitcast(BF16).rearrange("p (b v t) -> p b v t", b=2, t=PACK)
         second = keep.tile([P, 2, P, PACK], BF16, name="second", align_bytes=64)
         round_into(nc.scalar.copy, first[:, 0], 0)
@@ -298,7 +283,7 @@ def tile_picked_whuber_none_lo_kernel(
         hand_on(2, 1, second[:, 0].rearrange("p v t -> p (v t)"))
         store_words(1)
 
-        for q in range(4):
+        for q in range(P // QUAD):
             queue = nc.sync if q % 2 == 0 else nc.scalar
             queue.dma_start(
                 out=out_2[0, 4 * q : 4 * q + 4, :].bitcast(I32),

@@ -221,18 +221,17 @@ def tile_picked_whuber_none_lo_kernel(
                     turn_into(sums[vb + e][:, t, :], clipped[:, i, :], False, closes)
             step = step + 2 * len(ds) // D
 
+        res_late = keep.tile([P, PACK, half], F32, name="res_late")
         res = {
             0: ends[:, 1, :].rearrange("p (t v) -> p t v", t=PACK),
             1: ends[:, 2, :].rearrange("p (t v) -> p t v", t=PACK),
-            2: keep.tile([P, PACK, P], F32, name="res2")[:],
-            3: keep.tile([P, PACK, P], F32, name="res3")[:],
+            2: res_late[:, :, 0:P],
+            3: res_late[:, :, P:half],
         }
 
         def finish(v, rows, source):
             cols = slice(v * P, (v + 1) * P)
             nc.vector.scalar_tensor_tensor(res[v][:, rows, :], source, 1.0 / D, y_own[:, rows, cols], ALU.mult, ALU.add)
-            if rows.stop == PACK:
-                nc.sync.dma_start(out=out_rows[:, :, cols], in_=res[v])
 
         def round_into(copy, target, v):
             copy(
@@ -257,6 +256,7 @@ def tile_picked_whuber_none_lo_kernel(
             first_pass(raw[:, part, :], pulls[0][:, part, :], vb)
         for v in range(2):
             finish(v, slice(0, PACK), sums[v][:])
+            nc.sync.dma_start(out=out_rows[:, :, v * P : (v + 1) * P], in_=res[v])
         nc.vector.tensor_scalar(clipped[1][:], pulls[1], col(b_hi, vb + 1), col(b_low, vb + 1), ALU.min, ALU.max)
         late = [pull_bank(steps + e, "late%d" % e) for e in range(2)]
         for d in ds:
@@ -268,8 +268,10 @@ def tile_picked_whuber_none_lo_kernel(
                 turn_into(late[0][:, 0, :], clipped[0][:, d, :], False, d == D - 1)
         for v in (vb, vb + 1):
             finish(v, slice(0, t), sums[v][:, 0:t, :])
+        nc.sync.dma_start(out=out_rows[:, 0:t, half:T], in_=res_late[:, 0:t, :])
         for e in (1, 0):
             finish(vb + e, slice(t, PACK), late[e][:, 0:1, :])
+        nc.sync.dma_start(out=out_rows[:, t, half:T], in_=res_late[:, t, :])
 
         first = last_raw[:].bitcast(BF16).rearrange("p (b v t) -> p b v t", b=2, t=PACK)
         second = keep.tile([P, 2, P, PACK], BF16, name="second", align_bytes=64)

@@ -8,8 +8,6 @@ P = 128
 PACK = 4
 QUAD = 32
 SPLIT = 88
-LAG = 9
-EARLY = 2
 FLOPS = 2 * K * T * N
 
 F32 = mybir.dt.float32
@@ -34,11 +32,9 @@ def tile_picked_whuber_none_lo_kernel(
         keep = ctx.enter_context(tc.tile_pool(name="keep", bufs=1))
         psum = ctx.enter_context(tc.psum_pool(name="psum", bufs=1))
 
+
         def bank(b, name):
             return psum.tile([P, 4, P], F32, name=name, tag="bank%d" % b)
-
-        def pull_bank(step, name):
-            return bank(4 + (step + 3) % 4, name)
 
         b_rows = keep.tile([P, P], F32, name="b_rows")
         nc.sync.dma_start(
@@ -86,28 +82,13 @@ def tile_picked_whuber_none_lo_kernel(
         def col(cols, v):
             return cols[:, v : v + 1]
 
-        b_ps = pull_bank(0, "b_ps")
+
+        b_ps = bank(6, "b_ps")
         turn_into(b_ps[:, 0, :], b_rows[:], True, True)
-        b_cols = keep.tile([P, 4, 8], F32, name="b_cols")
-        b_off, b_hi, b_two, b_low = (b_cols[:, i, 0:blocks] for i in range(4))
-        for target, factor in ((b_off, -float(D)), (b_hi, 1.0), (b_two, 2.0), (b_low, -1.0)):
+        b_cols = keep.tile([P, 2, 8], F32, name="b_cols")
+        b_hi, b_low = (b_cols[:, i, 0:blocks] for i in range(2))
+        for target, factor in ((b_hi, 1.0), (b_low, -1.0)):
             nc.scalar.activation(target, b_ps[:, 0, 0:blocks], ACT.Copy, scale=factor)
-
-        sums = {}
-
-        def rows_in_sums(v):
-            return PACK if v < 2 else PACK - 1
-
-        def offset_into(target, v, start):
-            turn_into(target, col(b_off, v).to_broadcast([P, P]), start, False)
-
-        def open_sums(v):
-            sums[v] = bank(v, "sums%d" % v)
-            for t in range(rows_in_sums(v)):
-                offset_into(sums[v][:, t, :], v, t == 0)
-
-        for v in range(EARLY):
-            open_sums(v)
 
         w_src = w_raw[:].rearrange("p j (m t) -> p t m j", t=PACK)
         w_codes = keep.tile([P, N], U32, name="w_codes", align_bytes=64)
@@ -134,8 +115,9 @@ def tile_picked_whuber_none_lo_kernel(
         round_pair(nc.vector.tensor_copy, 1, slice(0, P))
         quantise(2, 2, places(0, 2))
 
+
         y_win = [keep.tile([P, T], F32, name="y_win%d" % t) for t in range(PACK)]
-        y_own = keep.tile([P, PACK, T], F32, name="y_own")
+        y_own = [keep.tile([P, half], F32, name="y_own%d" % t) for t in range(2)]
 
         def product(t, target, cols):
             nc.tensor.matmul_mx(
@@ -148,141 +130,179 @@ def tile_picked_whuber_none_lo_kernel(
                 stop=True,
             )
 
+        def flat(b, name):
+            return bank(b, name)[:].rearrange("p a b -> p (a b)")
+
+        halves = [flat(h, "y_half%d" % h)[:, 0:half] for h in range(2)]
         for h, copy in enumerate((nc.scalar.copy, nc.vector.tensor_copy)):
-            cols = slice(h * half, (h + 1) * half)
-            flat = bank(EARLY + h, "y_half%d" % h)[:].rearrange("p a b -> p (a b)")[:, 0:half]
-            product(0, flat, cols)
-            copy(out=y_win[0][:, cols], in_=flat)
-            nc.scalar.copy(out=y_own[:, 0, cols], in_=flat)
-        for t in range(1, PACK):
-            flat = pull_bank(t, "y_ps%d" % t)[:].rearrange("p a b -> p (a b)")
-            product(t, flat, slice(0, T))
-            nc.scalar.copy(out=y_win[t][:], in_=flat)
-            nc.sync.dma_start(out=y_own[:, t, :], in_=y_win[t][:])
+            product(0, halves[h], slice(h * half, (h + 1) * half))
+            copy(out=y_win[0][:, h * half : (h + 1) * half], in_=halves[h])
+        nc.vector.tensor_copy(out=y_own[0][:], in_=halves[1])
+        later = {}
+        for t, b in ((1, 6), (2, 7), (3, 0)):
+            later[t] = flat(b, "y_ps%d" % t)
+            product(t, later[t], slice(0, T))
 
         o_codes = keep.tile([P, T], U32, name="o_codes", align_bytes=64)
         o_plane = keep.tile([P, T], U8, name="o_plane", align_bytes=64)
         out_rows = out_0.rearrange("(p t) v -> p t v", t=PACK)
         out_words = out_1[0].rearrange("p c r -> p (c r)").bitcast(I32)
 
-        every = tuple(range(D))
-        units = [(0, vb, ds) for ds in (every[:2], every[2:]) for vb in (0, 2)]
-        units = units + [(t, vb, every) for vb in (0, 2) for t in range(1, PACK)]
-        steps = PACK * blocks
-        gathers = 2 * steps
+        units = [(0, 0, False), (0, 1, True), (1, 0, False), (2, 0, False), (1, 1, True), (3, 0, False), (2, 1, False), (3, 1, False)]
+        last = len(units) - 1
+        clipped = [keep.tile([P, 2 * D * P], F32, name="clipped%d" % n) for n in range(len(units))]
+        fresh = {n: keep.tile([P, D, half], F32, name="fresh%d" % n) for n in range(len(units)) if n != 4}
+        spent = (clipped[1][:, 0:half], clipped[1][:, 2 * half : 3 * half], clipped[2][:, 0:half], clipped[3][:, 0:half])
 
-        strip = keep.tile([P, (LAG + gathers - D) * half], F32, name="strip")
-        ends = keep.tile([P, D, D * P], F32, name="ends")
-        ends_step = (gathers - 1 - LAG) // 2
-        last_raw = keep.tile([P, D * P], F32, name="last_raw", align_bytes=64)
+        def piece(n, d, first, count):
+            whole = spent[d] if n == 4 else fresh[n][:, d, :]
+            return whole[:, first * P : (first + count) * P]
 
-        def piece(first, count):
-            return strip[:, first * half : (first + count) * half]
+        res = [keep.tile([P, PACK, half], F32, name="res%d" % h) for h in range(2)]
+        pulls = {}
+        sums = {}
 
-        def gather(step, t, vb, ds):
-            banks = [pull_bank(step + i, "pull%d" % (step + i)) for i in range(2 * len(ds) // D)]
-            pulls = [banks[e * len(ds) // D][:, e * len(ds) % D : e * len(ds) % D + len(ds), :] for e in range(2)]
-            for i, d in enumerate(ds):
-                g = 2 * step + i
-                picked = ends[:, 0, 0:half] if g == gathers - 1 else piece(g, 1)
-                nc.vector.tensor_tensor(
-                    picked,
-                    y_win[t][:].indirect(lists[d][:, vb * P // 16 : (vb + 2) * P // 16]),
-                    y_own[:, t, vb * P : (vb + 2) * P],
-                    ALU.subtract,
-                )
+        def open_unit(n):
+            t, h, by_vector = units[n]
+            pulls[n] = [bank(2 + (2 * n + e) % 6, "pull%d_%d" % (n, e)) for e in range(2)]
+            if not by_vector:
                 for e in range(2):
-                    turn_into(pulls[e][:, i, :], picked[:, e * P : (e + 1) * P], True, True)
-            return pulls
+                    v = 2 * h + e
+                    for d in range(D):
+                        turn_into(pulls[n][e][:, d, :], y_win[t][:, v * P : (v + 1) * P], d == 0, False)
 
-        def first_pass(raw, pulls, v):
-            nc.scalar.activation(raw, pulls, ACT.Relu, bias=col(b_hi, v), scale=-1.0)
+        def gather(n, d, first, count):
+            t, h, by_vector = units[n]
+            v = 2 * h + first
+            picked = piece(n, d, first, count)
+            window = y_win[t][:].indirect(lists[d][:, v * P // 16 : (v + count) * P // 16])
+            if by_vector:
+                nc.vector.tensor_tensor(picked, window, y_own[t][:], ALU.subtract)
+            else:
+                nc.scalar.activation(picked, window, ACT.Copy, scale=-1.0)
 
-        def second_pass(clipped, raw, v):
-            nc.scalar.activation(clipped, raw, ACT.Relu, bias=col(b_two, v), scale=-1.0)
+        def turn(n, d, e):
+            by_vector = units[n][2]
+            turn_into(pulls[n][e][:, d, :], piece(n, d, e, 1), by_vector, by_vector or d == D - 1)
 
-        step = 0
-        for t, vb, ds in units[:-1]:
-            pulls = gather(step, t, vb, ds)
-            raws = []
+        def clip(n, e, target, start, stop):
+            t, h, by_vector = units[n]
+            v = 2 * h + e
+            view = clipped[n][:, e * D * P : (e + 1) * D * P].rearrange("p (d m) -> p d m", d=D)
+            if by_vector:
+                nc.vector.tensor_scalar(view, pulls[n][e][:], col(b_hi, v), col(b_low, v), ALU.min, ALU.max)
+            else:
+                nc.vector.tensor_scalar(view, pulls[n][e][:], col(b_low, v), col(b_hi, v), ALU.max, ALU.min)
+            for d in range(D):
+                turn_into(target, view[:, d, :], start and d == 0, stop and d == D - 1)
+
+        def clips(n):
+            sums[n] = bank(n % 2, "sums%d" % n)
             for e in range(2):
-                at = step + e * len(ds) // D
-                whole = ends[:, :, 0:P] if at == ends_step else piece(LAG + 2 * at, 2).rearrange("p (d m) -> p d m", d=D)
-                raws.append(whole[:, e * len(ds) % D : e * len(ds) % D + len(ds), :])
-                first_pass(raws[e], pulls[e], vb + e)
-            if step == 0:
-                for v in range(EARLY, blocks):
-                    open_sums(v)
-            for e in range(2):
-                clipped = keep.tile([P, len(ds), P], F32, name="clipped%d_%d" % (step, e))
-                second_pass(clipped[:], raws[e], vb + e)
-                for i, d in enumerate(ds):
-                    closes = t == rows_in_sums(vb + e) - 1 and d == D - 1
-                    turn_into(sums[vb + e][:, t, :], clipped[:, i, :], False, closes)
-            step = step + 2 * len(ds) // D
+                clip(n, e, sums[n][:, e, :], e == 0, e == 1)
 
-        res_late = keep.tile([P, PACK, half], F32, name="res_late")
-        res = {
-            0: ends[:, 1, :].rearrange("p (t v) -> p t v", t=PACK),
-            1: ends[:, 2, :].rearrange("p (t v) -> p t v", t=PACK),
-            2: res_late[:, :, 0:P],
-            3: res_late[:, :, P:half],
-        }
-
-        def finish(v, rows, source):
-            cols = slice(v * P, (v + 1) * P)
-            nc.vector.scalar_tensor_tensor(res[v][:, rows, :], source, 1.0 / D, y_own[:, rows, cols], ALU.mult, ALU.add)
-
-        def round_into(copy, target, v):
-            copy(
-                out=target.rearrange("p (c i) t -> p c t i", i=4),
-                in_=res[v].rearrange("p t (c i) -> p c t i", i=4),
+        def finish(n, first, count, total):
+            t, h, by_vector = units[n]
+            v = 2 * h + first
+            nc.vector.scalar_tensor_tensor(
+                res[h][:, t, first * P : (first + count) * P],
+                total,
+                1.0 / D if by_vector else -1.0 / D,
+                y_win[t][:, v * P : (v + count) * P],
+                ALU.mult,
+                ALU.add,
             )
 
-        def hand_on(v, count, rounded):
+        def store(n):
+            t, h, by_vector = units[n]
+            nc.sync.dma_start(out=out_rows[:, t, h * half : (h + 1) * half], in_=res[h][:, t, :])
+
+        def finish_unit(n):
+            finish(n, 0, 2, sums[n][:, 0:2, :].rearrange("p a b -> p (a b)"))
+            store(n)
+
+        def scalar_unit(n):
+            open_unit(n)
+            for d in range(D):
+                gather(n, d, 0, 2)
+                for e in range(2):
+                    turn(n, d, e)
+
+        def turn_unit(n):
+            open_unit(n)
+            for e in range(2):
+                for d in range(D):
+                    turn(n, d, e)
+
+        rounded = keep.tile([P, blocks, P, PACK], BF16, name="rounded", align_bytes=64)
+
+        def round_into(copy, v, count):
+            h, first = divmod(v, 2)
+            copy(
+                out=rounded[:, v : v + count].rearrange("p b (c i) t -> p (b c) t i", i=4),
+                in_=res[h][:, :, first * P : (first + count) * P].rearrange("p t (c i) -> p c t i", i=4),
+            )
+
+        def hand_on(v, count):
             cols = slice(v * P, (v + count) * P)
-            nc.vector.quantize_mx(out=o_codes[:, cols].bitcast(FP8X4), scales=o_plane[:, cols], in_=rounded)
+            nc.vector.quantize_mx(
+                out=o_codes[:, cols].bitcast(FP8X4),
+                scales=o_plane[:, cols],
+                in_=rounded[:, v : v + count].rearrange("p b v t -> p (b v t)"),
+            )
 
         def store_words(h):
             cols = slice(h * half, (h + 1) * half)
             nc.sync.dma_start(out=out_words[:, cols], in_=o_codes[:, cols].bitcast(I32))
 
-        t, vb, ds = units[-1]
-        pulls = gather(step, t, vb, ds)
-        raw = last_raw[:].rearrange("p (d m) -> p d m", d=D)
-        clipped = [keep.tile([P, D, P], F32, name="clipped_last%d" % e) for e in range(2)]
-        pairs = (slice(0, 2), slice(2, D))
-        for part in pairs:
-            first_pass(raw[:, part, :], pulls[0][:, part, :], vb)
-        for v in range(2):
-            finish(v, slice(0, PACK), sums[v][:])
-            nc.sync.dma_start(out=out_rows[:, :, v * P : (v + 1) * P], in_=res[v])
-        nc.vector.tensor_scalar(clipped[1][:], pulls[1], col(b_hi, vb + 1), col(b_low, vb + 1), ALU.min, ALU.max)
-        late = [pull_bank(steps + e, "late%d" % e) for e in range(2)]
-        for d in ds:
-            turn_into(late[1][:, 0, :], clipped[1][:, d, :], d == 0, d == D - 1)
-        offset_into(late[0][:, 0, :], vb, True)
-        for part in pairs:
-            second_pass(clipped[0][:, part, :], raw[:, part, :], vb)
-            for d in ds[part]:
-                turn_into(late[0][:, 0, :], clipped[0][:, d, :], False, d == D - 1)
-        for v in (vb, vb + 1):
-            finish(v, slice(0, t), sums[v][:, 0:t, :])
-        nc.sync.dma_start(out=out_rows[:, 0:t, half:T], in_=res_late[:, 0:t, :])
-        for e in (1, 0):
-            finish(vb + e, slice(t, PACK), late[e][:, 0:1, :])
-        nc.sync.dma_start(out=out_rows[:, t, half:T], in_=res_late[:, t, :])
-
-        first = last_raw[:].bitcast(BF16).rearrange("p (b v t) -> p b v t", b=2, t=PACK)
-        second = keep.tile([P, 2, P, PACK], BF16, name="second", align_bytes=64)
-        round_into(nc.scalar.copy, first[:, 0], 0)
-        round_into(nc.scalar.copy, first[:, 1], 1)
-        round_into(nc.scalar.copy, second[:, 1], 3)
-        hand_on(0, 2, first.rearrange("p b v t -> p (b v t)"))
+        for d in range(D):
+            gather(1, d, 0, 2)
+        scalar_unit(0)
+        turn_unit(1)
+        for t in range(1, PACK):
+            nc.scalar.copy(out=y_win[t][:], in_=later[t])
+        clips(0)
+        scalar_unit(2)
+        clips(1)
+        nc.vector.tensor_copy(out=y_own[1][:], in_=y_win[1][:, half:T])
+        for d in range(2):
+            gather(4, d, 0, 2)
+        finish_unit(0)
+        scalar_unit(3)
+        finish_unit(1)
+        clips(2)
+        gather(4, 2, 0, 2)
+        finish_unit(2)
+        clips(3)
+        gather(4, 3, 0, 2)
+        turn_unit(4)
+        scalar_unit(5)
+        clips(4)
+        finish_unit(3)
+        scalar_unit(6)
+        clips(5)
+        finish_unit(4)
+        open_unit(last)
+        for e in range(2):
+            for d in range(D):
+                gather(last, d, e, 1)
+                turn(last, d, e)
+        finish_unit(5)
+        round_into(nc.vector.tensor_copy, 0, 2)
+        clips(6)
+        hand_on(0, 2)
         store_words(0)
-        round_into(nc.vector.tensor_copy, second[:, 0], 2)
-        hand_on(3, 1, second[:, 1].rearrange("p v t -> p (v t)"))
-        hand_on(2, 1, second[:, 0].rearrange("p v t -> p (v t)"))
+        ends = [bank(1, "end0"), bank(2, "end1")]
+        clip(last, 0, ends[0][:, 0, :], True, True)
+        finish_unit(6)
+        clip(last, 1, ends[1][:, 0, :], True, True)
+        for e in range(2):
+            finish(last, e, 1, ends[e][:, 0, :])
+        store(last)
+        round_into(nc.scalar.copy, 2, 1)
+        round_into(nc.vector.tensor_copy, 3, 1)
+        hand_on(2, 1)
+        hand_on(3, 1)
         store_words(1)
 
         for q in range(P // QUAD):

@@ -48,6 +48,8 @@ def tile_picked_whuber_none_lo_kernel(
             out=x_codes[:].bitcast(I32),
             in_=x_words[0].rearrange("p c r -> p (c r)").bitcast(I32),
         )
+        b_wide = keep.tile([P, half], F32, name="b_wide")
+        nc.sync.dma_start(out=b_wide[:], in_=bound[:, half:T])
         x_plane = keep.tile([P, T], U8, name="x_plane", align_bytes=64)
         nc.vector.memset(x_plane[:].bitcast(I32), 0)
         for q in range(P // QUAD):
@@ -83,7 +85,7 @@ def tile_picked_whuber_none_lo_kernel(
             return cols[:, v : v + 1]
 
 
-        b_ps = bank(6, "b_ps")
+        b_ps = bank(7, "b_ps")
         turn_into(b_ps[:, 0, :], b_rows[:], True, True)
         b_cols = keep.tile([P, 2, 8], F32, name="b_cols")
         b_hi, b_low = (b_cols[:, i, 0:blocks] for i in range(2))
@@ -113,11 +115,12 @@ def tile_picked_whuber_none_lo_kernel(
         for t in range(2):
             quantise(t, 1, places(1 + t, 1))
         round_pair(nc.vector.tensor_copy, 1, slice(0, P))
-        quantise(2, 2, places(0, 2))
 
 
         y_win = [keep.tile([P, T], F32, name="y_win%d" % t) for t in range(PACK)]
-        y_own = [keep.tile([P, half], F32, name="y_own%d" % t) for t in range(2)]
+        y_up = [keep.tile([P, half], F32, name="y_up%d" % t) for t in range(2)]
+        floor = keep.tile([P, half], F32, name="floor")
+        nc.scalar.activation(floor[:], b_wide[:], ACT.Copy, scale=-2.0)
 
         def product(t, target, cols):
             nc.tensor.matmul_mx(
@@ -137,102 +140,106 @@ def tile_picked_whuber_none_lo_kernel(
         for h, copy in enumerate((nc.scalar.copy, nc.vector.tensor_copy)):
             product(0, halves[h], slice(h * half, (h + 1) * half))
             copy(out=y_win[0][:, h * half : (h + 1) * half], in_=halves[h])
-        nc.vector.tensor_copy(out=y_own[0][:], in_=halves[1])
+        nc.vector.tensor_tensor(y_up[0][:], halves[1], b_wide[:], ALU.add)
         later = {}
-        for t, b in ((1, 6), (2, 7), (3, 0)):
+
+        def whole_product(t, b):
             later[t] = flat(b, "y_ps%d" % t)
             product(t, later[t], slice(0, T))
+
+        whole_product(1, 6)
 
         o_codes = keep.tile([P, T], U32, name="o_codes", align_bytes=64)
         o_plane = keep.tile([P, T], U8, name="o_plane", align_bytes=64)
         out_rows = out_0.rearrange("(p t) v -> p t v", t=PACK)
         out_words = out_1[0].rearrange("p c r -> p (c r)").bitcast(I32)
 
-        units = [(0, 0, False), (0, 1, True), (1, 0, False), (2, 0, False), (1, 1, True), (3, 0, False), (2, 1, False), (3, 1, False)]
+        units = [(0, 0), (1, 0), (2, 0), (3, 0), (2, 1), (3, 1)]
+        banks = ((2, 3), (4, 5), (6, 7), (2, 3), (4, 5), (6, 7))
         last = len(units) - 1
         clipped = [keep.tile([P, 2 * D * P], F32, name="clipped%d" % n) for n in range(len(units))]
-        fresh = {n: keep.tile([P, D, half], F32, name="fresh%d" % n) for n in range(len(units)) if n != 4}
-        spent = (clipped[1][:, 0:half], clipped[1][:, 2 * half : 3 * half], clipped[2][:, 0:half], clipped[3][:, 0:half])
-
-        def piece(n, d, first, count):
-            whole = spent[d] if n == 4 else fresh[n][:, d, :]
-            return whole[:, first * P : (first + count) * P]
-
+        picked = [keep.tile([P, D, half], F32, name="picked%d" % n) for n in range(len(units))]
         res = [keep.tile([P, PACK, half], F32, name="res%d" % h) for h in range(2)]
         pulls = {}
         sums = {}
 
+        def offsets(d, v, count):
+            return lists[d][:, v * P // 16 : (v + count) * P // 16]
+
         def open_unit(n):
-            t, h, by_vector = units[n]
-            pulls[n] = [bank(2 + (2 * n + e) % 6, "pull%d_%d" % (n, e)) for e in range(2)]
-            if not by_vector:
-                for e in range(2):
-                    v = 2 * h + e
-                    for d in range(D):
-                        turn_into(pulls[n][e][:, d, :], y_win[t][:, v * P : (v + 1) * P], d == 0, False)
+            t, h = units[n]
+            pulls[n] = [bank(banks[n][e], "pull%d_%d" % (n, e)) for e in range(2)]
+            for e in range(2):
+                v = 2 * h + e
+                for d in range(D):
+                    turn_into(pulls[n][e][:, d, :], y_win[t][:, v * P : (v + 1) * P], d == 0, False)
 
         def gather(n, d, first, count):
-            t, h, by_vector = units[n]
-            v = 2 * h + first
-            picked = piece(n, d, first, count)
-            window = y_win[t][:].indirect(lists[d][:, v * P // 16 : (v + count) * P // 16])
-            if by_vector:
-                nc.vector.tensor_tensor(picked, window, y_own[t][:], ALU.subtract)
-            else:
-                nc.scalar.activation(picked, window, ACT.Copy, scale=-1.0)
+            t, h = units[n]
+            target = picked[n][:, d, first * P : (first + count) * P]
+            nc.scalar.activation(target, y_win[t][:].indirect(offsets(d, 2 * h + first, count)), ACT.Copy, scale=-1.0)
+            for e in range(first, first + count):
+                turn_into(pulls[n][e][:, d, :], picked[n][:, d, e * P : (e + 1) * P], False, d == D - 1)
 
-        def turn(n, d, e):
-            by_vector = units[n][2]
-            turn_into(pulls[n][e][:, d, :], piece(n, d, e, 1), by_vector, by_vector or d == D - 1)
+        def scalar_unit(n):
+            for d in range(D):
+                gather(n, d, 0, 2)
 
         def clip(n, e, target, start, stop):
-            t, h, by_vector = units[n]
-            v = 2 * h + e
+            v = 2 * units[n][1] + e
             view = clipped[n][:, e * D * P : (e + 1) * D * P].rearrange("p (d m) -> p d m", d=D)
-            if by_vector:
-                nc.vector.tensor_scalar(view, pulls[n][e][:], col(b_hi, v), col(b_low, v), ALU.min, ALU.max)
-            else:
-                nc.vector.tensor_scalar(view, pulls[n][e][:], col(b_low, v), col(b_hi, v), ALU.max, ALU.min)
+            nc.vector.tensor_scalar(view, pulls[n][e][:], col(b_low, v), col(b_hi, v), ALU.max, ALU.min)
             for d in range(D):
                 turn_into(target, view[:, d, :], start and d == 0, stop and d == D - 1)
 
         def clips(n):
-            sums[n] = bank(n % 2, "sums%d" % n)
+            sums[n] = bank((n + 1) % 2, "sums%d" % n)
             for e in range(2):
                 clip(n, e, sums[n][:, e, :], e == 0, e == 1)
 
         def finish(n, first, count, total):
-            t, h, by_vector = units[n]
+            t, h = units[n]
             v = 2 * h + first
             nc.vector.scalar_tensor_tensor(
                 res[h][:, t, first * P : (first + count) * P],
                 total,
-                1.0 / D if by_vector else -1.0 / D,
+                -1.0 / D,
                 y_win[t][:, v * P : (v + count) * P],
                 ALU.mult,
                 ALU.add,
             )
 
-        def store(n):
-            t, h, by_vector = units[n]
+        def store(t, h):
             nc.sync.dma_start(out=out_rows[:, t, h * half : (h + 1) * half], in_=res[h][:, t, :])
 
         def finish_unit(n):
             finish(n, 0, 2, sums[n][:, 0:2, :].rearrange("p a b -> p (a b)"))
-            store(n)
+            store(*units[n])
 
-        def scalar_unit(n):
-            open_unit(n)
-            for d in range(D):
-                gather(n, d, 0, 2)
-                for e in range(2):
-                    turn(n, d, e)
+        own = keep.tile([P, D, half], F32, name="own")
+        below = [
+            [own[:, d, :] for d in range(D)],
+            [clipped[0][:, 0:half], clipped[0][:, 2 * half : 3 * half], clipped[1][:, 0:half], clipped[1][:, 2 * half : 3 * half]],
+        ]
+        held = [keep.tile([P, D, half], F32, name="held%d" % t) for t in range(2)]
+        pair = [keep.tile([P, 2, half], F32, name="pair%d" % t) for t in range(2)]
+        part = [keep.tile([P, half], F32, name="part%d" % t) for t in range(2)]
 
-        def turn_unit(n):
-            open_unit(n)
-            for e in range(2):
-                for d in range(D):
-                    turn(n, d, e)
+        def own_gather(t, d):
+            nc.vector.tensor_tensor(below[t][d], y_win[t][:].indirect(offsets(d, 2, 2)), y_up[t][:], ALU.subtract)
+
+        def own_clip(t, d):
+            nc.vector.scalar_tensor_tensor(held[t][:, d, :], below[t][d], 0.0, floor[:], ALU.min, ALU.max)
+
+        def own_pairs(t):
+            nc.vector.tensor_tensor(pair[t][:], held[t][:, 0:2, :], held[t][:, 2:D, :], ALU.add)
+
+        def own_part(t):
+            nc.vector.scalar_tensor_tensor(part[t][:], pair[t][:, 0, :], 1.0 / D, y_up[t][:], ALU.mult, ALU.add)
+
+        def own_finish(t):
+            nc.vector.scalar_tensor_tensor(res[1][:, t, :], pair[t][:, 1, :], 1.0 / D, part[t][:], ALU.mult, ALU.add)
+            store(t, 1)
 
         rounded = keep.tile([P, blocks, P, PACK], BF16, name="rounded", align_bytes=64)
 
@@ -255,50 +262,63 @@ def tile_picked_whuber_none_lo_kernel(
             cols = slice(h * half, (h + 1) * half)
             nc.sync.dma_start(out=out_words[:, cols], in_=o_codes[:, cols].bitcast(I32))
 
-        for d in range(D):
-            gather(1, d, 0, 2)
+        own_gather(0, 0)
+        quantise(2, 2, places(0, 2))
+        whole_product(2, 7)
+        whole_product(3, 0)
+        for d in range(1, D):
+            own_gather(0, d)
+        nc.scalar.copy(out=y_win[1][:], in_=later[1])
+        open_unit(0)
+        open_unit(1)
         scalar_unit(0)
-        turn_unit(1)
-        for t in range(1, PACK):
-            nc.scalar.copy(out=y_win[t][:], in_=later[t])
+        nc.scalar.copy(out=y_win[2][:], in_=later[2])
+        open_unit(2)
+        scalar_unit(1)
+        nc.scalar.copy(out=y_win[3][:], in_=later[3])
         clips(0)
+        for d in range(D):
+            own_clip(0, d)
+        own_pairs(0)
+        own_part(0)
+        nc.vector.tensor_tensor(y_up[1][:], y_win[1][:, half:T], b_wide[:], ALU.add)
+        own_finish(0)
+        open_unit(3)
         scalar_unit(2)
         clips(1)
-        nc.vector.tensor_copy(out=y_own[1][:], in_=y_win[1][:, half:T])
-        for d in range(2):
-            gather(4, d, 0, 2)
         finish_unit(0)
+        own_gather(1, 0)
+        own_gather(1, 1)
+        open_unit(4)
         scalar_unit(3)
-        finish_unit(1)
         clips(2)
-        gather(4, 2, 0, 2)
-        finish_unit(2)
-        clips(3)
-        gather(4, 3, 0, 2)
-        turn_unit(4)
-        scalar_unit(5)
-        clips(4)
-        finish_unit(3)
-        scalar_unit(6)
-        clips(5)
-        finish_unit(4)
+        finish_unit(1)
+        own_gather(1, 2)
+        own_gather(1, 3)
         open_unit(last)
+        scalar_unit(4)
+        clips(3)
+        finish_unit(2)
+        for d in range(D):
+            own_clip(1, d)
         for e in range(2):
             for d in range(D):
                 gather(last, d, e, 1)
-                turn(last, d, e)
-        finish_unit(5)
-        round_into(nc.vector.tensor_copy, 0, 2)
-        clips(6)
+        clips(4)
+        finish_unit(3)
+        round_into(nc.scalar.copy, 0, 2)
+        own_pairs(1)
+        ends = [bank(0, "end0"), bank(2, "end1")]
+        clip(last, 0, ends[0][:, 0, :], True, True)
+        finish_unit(4)
+        own_part(1)
+        clip(last, 1, ends[1][:, 0, :], True, True)
+        own_finish(1)
         hand_on(0, 2)
         store_words(0)
-        ends = [bank(1, "end0"), bank(2, "end1")]
-        clip(last, 0, ends[0][:, 0, :], True, True)
-        finish_unit(6)
-        clip(last, 1, ends[1][:, 0, :], True, True)
         for e in range(2):
             finish(last, e, 1, ends[e][:, 0, :])
-        store(last)
+        store(*units[last])
         round_into(nc.scalar.copy, 2, 1)
         round_into(nc.vector.tensor_copy, 3, 1)
         hand_on(2, 1)

@@ -176,10 +176,11 @@ def tile_picked_whuber_none_lo_kernel(
 
         def gather(n, d, first, count):
             t, h = units[n]
-            target = picked[n][:, d, first * P : (first + count) * P]
-            nc.scalar.activation(target, y_win[t][:].indirect(offsets(d, 2 * h + first, count)), ACT.Copy, scale=-1.0)
+            whole = res[1][:, (1, 4).index(n), :] if n in (1, 4) and d == D - 1 else picked[n][:, d, :]
+            window = y_win[t][:].indirect(offsets(d, 2 * h + first, count))
+            nc.scalar.activation(whole[:, first * P : (first + count) * P], window, ACT.Copy, scale=-1.0)
             for e in range(first, first + count):
-                turn_into(pulls[n][e][:, d, :], picked[n][:, d, e * P : (e + 1) * P], False, d == D - 1)
+                turn_into(pulls[n][e][:, d, :], whole[:, e * P : (e + 1) * P], False, d == D - 1)
 
         def scalar_unit(n):
             for d in range(D):
@@ -217,13 +218,10 @@ def tile_picked_whuber_none_lo_kernel(
             store(*units[n])
 
         own = keep.tile([P, D, half], F32, name="own")
-        below = [
-            [own[:, d, :] for d in range(D)],
-            [clipped[0][:, 0:half], clipped[0][:, 2 * half : 3 * half], clipped[1][:, 0:half], clipped[1][:, 2 * half : 3 * half]],
-        ]
         held = [keep.tile([P, D, half], F32, name="held%d" % t) for t in range(2)]
         pair = [keep.tile([P, 2, half], F32, name="pair%d" % t) for t in range(2)]
-        part = [keep.tile([P, half], F32, name="part%d" % t) for t in range(2)]
+        below = [[own[:, d, :] for d in range(D)], [clipped[n][:, e * 2 * half : (2 * e + 1) * half] for n in range(2) for e in range(2)]]
+        total = [own[:, 1, :], own[:, 0, :]]
 
         def own_gather(t, d):
             nc.vector.tensor_tensor(below[t][d], y_win[t][:].indirect(offsets(d, 2, 2)), y_up[t][:], ALU.subtract)
@@ -231,14 +229,14 @@ def tile_picked_whuber_none_lo_kernel(
         def own_clip(t, d):
             nc.vector.scalar_tensor_tensor(held[t][:, d, :], below[t][d], 0.0, floor[:], ALU.min, ALU.max)
 
-        def own_pairs(t):
-            nc.vector.tensor_tensor(pair[t][:], held[t][:, 0:2, :], held[t][:, 2:D, :], ALU.add)
+        def own_pair(t, i):
+            nc.gpsimd.tensor_tensor(pair[t][:, i, :], held[t][:, 2 * i, :], held[t][:, 2 * i + 1, :], ALU.add)
 
-        def own_part(t):
-            nc.vector.scalar_tensor_tensor(part[t][:], pair[t][:, 0, :], 1.0 / D, y_up[t][:], ALU.mult, ALU.add)
+        def own_total(t):
+            nc.gpsimd.tensor_tensor(total[t], pair[t][:, 0, :], pair[t][:, 1, :], ALU.add)
 
         def own_finish(t):
-            nc.vector.scalar_tensor_tensor(res[1][:, t, :], pair[t][:, 1, :], 1.0 / D, part[t][:], ALU.mult, ALU.add)
+            nc.vector.scalar_tensor_tensor(res[1][:, t, :], total[t], 1.0 / D, y_up[t][:], ALU.mult, ALU.add)
             store(t, 1)
 
         rounded = keep.tile([P, blocks, P, PACK], BF16, name="rounded", align_bytes=64)
@@ -275,54 +273,57 @@ def tile_picked_whuber_none_lo_kernel(
         nc.scalar.copy(out=y_win[2][:], in_=later[2])
         open_unit(2)
         scalar_unit(1)
-        nc.scalar.copy(out=y_win[3][:], in_=later[3])
-        clips(0)
+        nc.vector.tensor_tensor(y_up[1][:], y_win[1][:, half:T], b_wide[:], ALU.add)
         for d in range(D):
             own_clip(0, d)
-        own_pairs(0)
-        own_part(0)
-        nc.vector.tensor_tensor(y_up[1][:], y_win[1][:, half:T], b_wide[:], ALU.add)
-        own_finish(0)
+        nc.gpsimd.tensor_tensor(pair[0][:], held[0][:, 0:2, :], held[0][:, 2:D, :], ALU.add)
+        own_total(0)
+        nc.vector.tensor_copy(out=y_win[3][:], in_=later[3])
+        clips(0)
         open_unit(3)
         scalar_unit(2)
         clips(1)
         finish_unit(0)
+        own_finish(0)
         own_gather(1, 0)
         own_gather(1, 1)
+        own_clip(1, 0)
+        own_clip(1, 1)
+        own_pair(1, 0)
         open_unit(4)
         scalar_unit(3)
         clips(2)
         finish_unit(1)
         own_gather(1, 2)
         own_gather(1, 3)
+        own_clip(1, 2)
+        own_clip(1, 3)
+        own_pair(1, 1)
+        own_total(1)
         open_unit(last)
         scalar_unit(4)
         clips(3)
         finish_unit(2)
         for d in range(D):
-            own_clip(1, d)
-        for e in range(2):
-            for d in range(D):
-                gather(last, d, e, 1)
+            gather(last, d, 0, 1)
         clips(4)
+        for d in range(D):
+            gather(last, d, 1, 1)
         finish_unit(3)
         round_into(nc.scalar.copy, 0, 2)
-        own_pairs(1)
+        own_finish(1)
         ends = [bank(0, "end0"), bank(2, "end1")]
         clip(last, 0, ends[0][:, 0, :], True, True)
         finish_unit(4)
-        own_part(1)
         clip(last, 1, ends[1][:, 0, :], True, True)
-        own_finish(1)
+        finish(last, 0, 1, ends[0][:, 0, :])
+        round_into(nc.scalar.copy, 2, 1)
         hand_on(0, 2)
         store_words(0)
-        for e in range(2):
-            finish(last, e, 1, ends[e][:, 0, :])
+        finish(last, 1, 1, ends[1][:, 0, :])
         store(*units[last])
-        round_into(nc.scalar.copy, 2, 1)
         round_into(nc.vector.tensor_copy, 3, 1)
-        hand_on(2, 1)
-        hand_on(3, 1)
+        hand_on(2, 2)
         store_words(1)
 
         for q in range(P // QUAD):

@@ -118,7 +118,7 @@ def tile_picked_whuber_none_lo_kernel(
 
 
         y_win = [keep.tile([P, T], F32, name="y_win%d" % t) for t in range(PACK)]
-        y_up = [keep.tile([P, half], F32, name="y_up%d" % t) for t in range(2)]
+        y_up = {t: keep.tile([P, half], F32, name="y_up%d" % t) for t in (0, 1)}
         floor = keep.tile([P, half], F32, name="floor")
         nc.scalar.activation(floor[:], b_wide[:], ACT.Copy, scale=-2.0)
 
@@ -137,7 +137,7 @@ def tile_picked_whuber_none_lo_kernel(
             return bank(b, name)[:].rearrange("p a b -> p (a b)")
 
         halves = [flat(h, "y_half%d" % h)[:, 0:half] for h in range(2)]
-        for h, copy in enumerate((nc.scalar.copy, nc.vector.tensor_copy)):
+        for h, copy in ((1, nc.vector.tensor_copy), (0, nc.scalar.copy)):
             product(0, halves[h], slice(h * half, (h + 1) * half))
             copy(out=y_win[0][:, h * half : (h + 1) * half], in_=halves[h])
         nc.vector.tensor_tensor(y_up[0][:], halves[1], b_wide[:], ALU.add)
@@ -154,11 +154,21 @@ def tile_picked_whuber_none_lo_kernel(
         out_rows = out_0.rearrange("(p t) v -> p t v", t=PACK)
         out_words = out_1[0].rearrange("p c r -> p (c r)").bitcast(I32)
 
-        units = [(0, 0), (1, 0), (2, 0), (3, 0), (2, 1), (3, 1)]
+        units = [(0, 0), (1, 0), (2, 0), (2, 1), (3, 0), (3, 1)]
         banks = ((2, 3), (4, 5), (6, 7), (2, 3), (4, 5), (6, 7))
         last = len(units) - 1
         clipped = [keep.tile([P, 2 * D * P], F32, name="clipped%d" % n) for n in range(len(units))]
-        picked = [keep.tile([P, D, half], F32, name="picked%d" % n) for n in range(len(units))]
+        pieces = [keep.tile([P, (D + 1) * half], F32, name="pieces%d" % n) for n in range(len(units))]
+
+        def picked(n, d):
+            if n in (1, last - 1) and d == D - 1:
+                return res[1][:, min(n - 1, 1), :]
+            at = d * half + (P if d == D - 1 else 0)
+            return pieces[n][:, at : at + half]
+
+        def behind(n, i):
+            return pieces[n][:, (D - 1 + i) * half : (D + i) * half]
+
         res = [keep.tile([P, PACK, half], F32, name="res%d" % h) for h in range(2)]
         pulls = {}
         sums = {}
@@ -176,11 +186,23 @@ def tile_picked_whuber_none_lo_kernel(
 
         def gather(n, d, first, count):
             t, h = units[n]
-            whole = res[1][:, (1, 4).index(n), :] if n in (1, 4) and d == D - 1 else picked[n][:, d, :]
-            window = y_win[t][:].indirect(offsets(d, 2 * h + first, count))
-            nc.scalar.activation(whole[:, first * P : (first + count) * P], window, ACT.Copy, scale=-1.0)
+            target = picked(n, d)[:, first * P : (first + count) * P]
+            nc.scalar.activation(target, y_win[t][:].indirect(offsets(d, 2 * h + first, count)), ACT.Copy, scale=-1.0)
             for e in range(first, first + count):
-                turn_into(pulls[n][e][:, d, :], whole[:, e * P : (e + 1) * P], False, d == D - 1)
+                turn_into(pulls[n][e][:, d, :], picked(n, d)[:, e * P : (e + 1) * P], False, d == D - 1)
+
+        def last_gather(d, e, target, stop):
+            t, h = units[last]
+            part = picked(last, d)[:, e * P : (e + 1) * P]
+            nc.scalar.activation(part, y_win[t][:].indirect(offsets(d, 2 * h + e, 1)), ACT.Copy, scale=-1.0)
+            turn_into(target, part, False, stop)
+
+        def last_clip(e, ds, source, target, start, stop):
+            v = 2 * units[last][1] + e
+            view = clipped[last][:, (e * D + ds[0]) * P : (e * D + ds[-1] + 1) * P].rearrange("p (d m) -> p d m", d=len(ds))
+            nc.vector.tensor_scalar(view, source, col(b_low, v), col(b_hi, v), ALU.max, ALU.min)
+            for i in range(len(ds)):
+                turn_into(target, view[:, i, :], start and i == 0, stop and i == len(ds) - 1)
 
         def scalar_unit(n):
             for d in range(D):
@@ -218,19 +240,37 @@ def tile_picked_whuber_none_lo_kernel(
             store(*units[n])
 
         own = keep.tile([P, D, half], F32, name="own")
-        held = [keep.tile([P, D, half], F32, name="held%d" % t) for t in range(2)]
-        pair = [keep.tile([P, 2, half], F32, name="pair%d" % t) for t in range(2)]
-        below = [[own[:, d, :] for d in range(D)], [clipped[n][:, e * 2 * half : (2 * e + 1) * half] for n in range(2) for e in range(2)]]
-        total = [own[:, 1, :], own[:, 0, :]]
+        below = {
+            0: own[:].rearrange("p d v -> p (d v)"),
+            1: pieces[0][:, (D - 1) * half : (D + 1) * half],
+            2: clipped[0][:, 0 : 2 * half],
+        }
+        held = {0: keep.tile([P, D, half], F32, name="held0")[:], 1: clipped[1][:].rearrange("p (d v) -> p d v", d=D)}
+        pair = {t: keep.tile([P, 2, half], F32, name="pair%d" % t) for t in (0, 1)}
+        total = {0: own[:, 1, :], 1: own[:, 0, :]}
+
+        def lowered(t, first, count):
+            at = first if t == 0 else first % 2
+            return below[t + (first // 2 if t else 0)][:, at * half : (at + count) * half]
+
+        def lift(t):
+            nc.vector.tensor_tensor(y_up[t][:], y_win[t][:, half:T], b_wide[:], ALU.add)
 
         def own_gather(t, d):
-            nc.vector.tensor_tensor(below[t][d], y_win[t][:].indirect(offsets(d, 2, 2)), y_up[t][:], ALU.subtract)
+            nc.vector.tensor_tensor(lowered(t, d, 1), y_win[t][:].indirect(offsets(d, 2, 2)), y_up[t][:], ALU.subtract)
 
-        def own_clip(t, d):
-            nc.vector.scalar_tensor_tensor(held[t][:, d, :], below[t][d], 0.0, floor[:], ALU.min, ALU.max)
+        def own_clip(t, first, count):
+            nc.vector.scalar_tensor_tensor(
+                held[t][:, first : first + count, :],
+                lowered(t, first, count).rearrange("p (d v) -> p d v", d=count),
+                0.0,
+                floor[:].unsqueeze(1).to_broadcast([P, count, half]),
+                ALU.min,
+                ALU.max,
+            )
 
-        def own_pair(t, i):
-            nc.gpsimd.tensor_tensor(pair[t][:, i, :], held[t][:, 2 * i, :], held[t][:, 2 * i + 1, :], ALU.add)
+        def own_pairs(t):
+            nc.gpsimd.tensor_tensor(pair[t][:], held[t][:, 0:2, :], held[t][:, 2:D, :], ALU.add)
 
         def own_total(t):
             nc.gpsimd.tensor_tensor(total[t], pair[t][:, 0, :], pair[t][:, 1, :], ALU.add)
@@ -270,59 +310,64 @@ def tile_picked_whuber_none_lo_kernel(
         open_unit(0)
         open_unit(1)
         scalar_unit(0)
-        nc.scalar.copy(out=y_win[2][:], in_=later[2])
+        lift(1)
+        own_clip(0, 0, D)
+        nc.vector.tensor_copy(out=y_win[2][:], in_=later[2])
         open_unit(2)
         scalar_unit(1)
-        nc.vector.tensor_tensor(y_up[1][:], y_win[1][:, half:T], b_wide[:], ALU.add)
-        for d in range(D):
-            own_clip(0, d)
-        nc.gpsimd.tensor_tensor(pair[0][:], held[0][:, 0:2, :], held[0][:, 2:D, :], ALU.add)
+        own_pairs(0)
         own_total(0)
         nc.vector.tensor_copy(out=y_win[3][:], in_=later[3])
         clips(0)
+        own_gather(1, 0)
+        own_gather(1, 1)
         open_unit(3)
         scalar_unit(2)
         clips(1)
         finish_unit(0)
         own_finish(0)
-        own_gather(1, 0)
-        own_gather(1, 1)
-        own_clip(1, 0)
-        own_clip(1, 1)
-        own_pair(1, 0)
+        own_gather(1, 2)
+        own_gather(1, 3)
         open_unit(4)
         scalar_unit(3)
         clips(2)
         finish_unit(1)
-        own_gather(1, 2)
-        own_gather(1, 3)
-        own_clip(1, 2)
-        own_clip(1, 3)
-        own_pair(1, 1)
+        own_clip(1, 0, 2)
+        own_clip(1, 2, 2)
+        own_pairs(1)
         own_total(1)
-        open_unit(last)
+        parts = [(0, (0, 1, 2, 3), 6), (1, (0, 1, 2), 7), (1, (3,), 3)]
+        ends_in = []
+        for e, ds, b in parts[:2]:
+            ends_in.append(bank(b, "pull_end%d" % b)[:, 0 : len(ds), :])
+            for i in range(len(ds)):
+                turn_into(ends_in[-1][:, i, :], y_win[3][:, (2 + e) * P : (3 + e) * P], i == 0, False)
         scalar_unit(4)
         clips(3)
+        ends_in.append(bank(3, "pull_end3")[:, 0:1, :])
+        turn_into(ends_in[2][:, 0, :], y_win[3][:, 3 * P : T], True, False)
         finish_unit(2)
-        for d in range(D):
-            gather(last, d, 0, 1)
+        for i, d in enumerate(parts[0][1]):
+            last_gather(d, 0, ends_in[0][:, i, :], d == D - 1)
         clips(4)
-        for d in range(D):
-            gather(last, d, 1, 1)
+        for i, d in enumerate(parts[1][1]):
+            last_gather(d, 1, ends_in[1][:, i, :], d == D - 2)
+        last_gather(3, 1, ends_in[2][:, 0, :], True)
         finish_unit(3)
-        round_into(nc.scalar.copy, 0, 2)
-        own_finish(1)
         ends = [bank(0, "end0"), bank(2, "end1")]
-        clip(last, 0, ends[0][:, 0, :], True, True)
+        last_clip(0, parts[0][1], ends_in[0], ends[0][:, 0, :], True, True)
         finish_unit(4)
-        clip(last, 1, ends[1][:, 0, :], True, True)
+        own_finish(1)
+        round_into(nc.scalar.copy, 0, 2)
+        last_clip(1, parts[1][1], ends_in[1], ends[1][:, 0, :], True, False)
+        last_clip(1, parts[2][1], ends_in[2], ends[1][:, 0, :], False, True)
         finish(last, 0, 1, ends[0][:, 0, :])
-        round_into(nc.scalar.copy, 2, 1)
-        hand_on(0, 2)
-        store_words(0)
         finish(last, 1, 1, ends[1][:, 0, :])
         store(*units[last])
+        round_into(nc.vector.tensor_copy, 2, 1)
         round_into(nc.vector.tensor_copy, 3, 1)
+        hand_on(0, 2)
+        store_words(0)
         hand_on(2, 2)
         store_words(1)
 

@@ -36,13 +36,14 @@ def tile_picked_whuber_none_lo_kernel(
         def bank(b, name):
             return psum.tile([P, 4, P], F32, name=name, tag="bank%d" % b)
 
-        b_rows = keep.tile([P, P], F32, name="b_rows")
-        nc.sync.dma_start(
-            out=b_rows[0:QUAD, :],
-            in_=bound[0 : QUAD // blocks, :].rearrange("o (c v) -> (o c) v", c=blocks),
-        )
         w_raw = keep.tile([P, PACK, N], F32, name="w_raw")
         nc.sync.dma_start(out=w_raw[:], in_=w1.rearrange("(p j) n -> p j n", j=PACK))
+        lists = [keep.tile([P, T // 16], U16, name="list%d" % d) for d in range(D)]
+
+        def load_list(d):
+            nc.sync.dma_start(lists[d][:], (pos1, pos2, pos3, pos4)[d])
+
+        load_list(0)
         x_codes = keep.tile([P, T], U32, name="x_codes", align_bytes=64)
         nc.sync.dma_start(
             out=x_codes[:].bitcast(I32),
@@ -51,26 +52,25 @@ def tile_picked_whuber_none_lo_kernel(
         b_wide = keep.tile([P, half], F32, name="b_wide")
         nc.sync.dma_start(out=b_wide[:], in_=bound[:, half:T])
         x_plane = keep.tile([P, T], U8, name="x_plane", align_bytes=64)
-        nc.vector.memset(x_plane[:].bitcast(I32), 0)
         for q in range(P // QUAD):
             nc.scalar.dma_start(
-                out=x_plane[QUAD * q : QUAD * q + 4, :].bitcast(I32),
-                in_=x_scales[0, 4 * q : 4 * q + 4, :].bitcast(I32),
+                out=x_plane[QUAD * q : QUAD * (q + 1), :].bitcast(I32),
+                in_=x_scales[0:1, 4 * q : 4 * q + 4, :].bitcast(I32).to_broadcast([QUAD // 4, 4, T // 4]),
             )
-        lists = []
-        for d, pos in enumerate((pos1, pos2, pos3, pos4)):
-            tile = keep.tile([P, T // 16], U16, name="list%d" % d)
-            nc.sync.dma_start(tile[:], pos)
-            lists.append(tile)
+        for d in range(1, D):
+            load_list(d)
+        b_cols = keep.tile([P, 2, 8], F32, name="b_cols")
+        b_hi, b_low = (b_cols[:, i, 0:blocks] for i in range(2))
+        with nc.allow_non_contiguous_dma(reason="one bound a partition"):
+            nc.sync.dma_start(out=b_hi, in_=bound[0:1, :].rearrange("o (c p) -> p (o c)", p=P))
+        nc.gpsimd.tensor_scalar(b_low, b_hi, -1.0, 0.0, ALU.mult, ALU.add)
 
         ident = keep.tile([P, P], F32, name="ident")
         ones = keep.tile([P, P], F32, name="ones")
         along = keep.tile([P, P], F32, name="along", align_bytes=64)
         across = keep.tile([P, P], F32, name="across", align_bytes=64)
         nc.vector.memset(ones[:], 1.0)
-        nc.vector.memset(b_rows[QUAD : 2 * QUAD, :], 0.0)
         nc.vector.tensor_tensor_scan(along[:], ones[:], ones[:], 0.0, ALU.mult, ALU.add)
-        nc.vector.memset(b_rows[2 * QUAD : P, :], 0.0)
         nc.vector.transpose(across[:], along[:])
         for q in range(P // QUAD):
             rows = slice(QUAD * q, QUAD * (q + 1))
@@ -84,13 +84,6 @@ def tile_picked_whuber_none_lo_kernel(
         def col(cols, v):
             return cols[:, v : v + 1]
 
-
-        b_ps = bank(7, "b_ps")
-        turn_into(b_ps[:, 0, :], b_rows[:], True, True)
-        b_cols = keep.tile([P, 2, 8], F32, name="b_cols")
-        b_hi, b_low = (b_cols[:, i, 0:blocks] for i in range(2))
-        for target, factor in ((b_hi, 1.0), (b_low, -1.0)):
-            nc.scalar.activation(target, b_ps[:, 0, 0:blocks], ACT.Copy, scale=factor)
 
         w_src = w_raw[:].rearrange("p j (m t) -> p t m j", t=PACK)
         w_codes = keep.tile([P, N], U32, name="w_codes", align_bytes=64)

@@ -8,6 +8,8 @@ P = 128
 PACK = 4
 QUAD = 32
 SPLIT = 88
+SPARE = 16
+WHOLE = 3
 FLOPS = 2 * K * T * N
 
 F32 = mybir.dt.float32
@@ -63,7 +65,6 @@ def tile_picked_whuber_none_lo_kernel(
         b_hi, b_low = (b_cols[:, i, 0:blocks] for i in range(2))
         with nc.allow_non_contiguous_dma(reason="one bound a partition"):
             nc.sync.dma_start(out=b_hi, in_=bound[0:1, :].rearrange("o (c p) -> p (o c)", p=P))
-        nc.gpsimd.tensor_scalar(b_low, b_hi, -1.0, 0.0, ALU.mult, ALU.add)
 
         ident = keep.tile([P, P], F32, name="ident")
         ones = keep.tile([P, P], F32, name="ones")
@@ -107,11 +108,15 @@ def tile_picked_whuber_none_lo_kernel(
         round_pair(nc.scalar.copy, 0, slice(SPLIT, P))
         for t in range(2):
             quantise(t, 1, places(1 + t, 1))
-        round_pair(nc.vector.tensor_copy, 1, slice(0, P))
+        round_pair(nc.vector.tensor_copy, 1, slice(0, 64))
+        round_pair(nc.scalar.copy, 1, slice(64, P))
 
 
-        y_win = [keep.tile([P, T], F32, name="y_win%d" % t) for t in range(PACK)]
-        y_up = {t: keep.tile([P, half], F32, name="y_up%d" % t) for t in (0, 1)}
+        own = [keep.tile([P, 2, half], F32, name="own%d" % i) for i in range(2)]
+        y_win = {t: keep.tile([P, T], F32, name="y_win%d" % t) for t in range(2)}
+        y_win[3] = keep.tile([P, T], F32, name="y_win3")
+        nc.gpsimd.tensor_scalar(b_low, b_hi, -1.0, 0.0, ALU.mult, ALU.add)
+        y_up = [keep.tile([P, half], F32, name="y_up0")[:], own[1][:, 0, :]]
         floor = keep.tile([P, half], F32, name="floor")
         nc.scalar.activation(floor[:], b_wide[:], ACT.Copy, scale=-2.0)
 
@@ -133,14 +138,17 @@ def tile_picked_whuber_none_lo_kernel(
         for h, copy in ((1, nc.vector.tensor_copy), (0, nc.scalar.copy)):
             product(0, halves[h], slice(h * half, (h + 1) * half))
             copy(out=y_win[0][:, h * half : (h + 1) * half], in_=halves[h])
-        nc.vector.tensor_tensor(y_up[0][:], halves[1], b_wide[:], ALU.add)
+        nc.vector.tensor_tensor(y_up[0], halves[1], b_wide[:], ALU.add)
         later = {}
 
         def whole_product(t, b):
             later[t] = flat(b, "y_ps%d" % t)
             product(t, later[t], slice(0, T))
 
-        whole_product(1, 6)
+        nexts = [flat(6 + h, "y_next%d" % h)[:, 0:half] for h in range(2)]
+        for h in range(2):
+            product(1, nexts[h], slice(h * half, (h + 1) * half))
+        nc.scalar.copy(out=y_win[1][:, 0:half], in_=nexts[0])
 
         o_codes = keep.tile([P, T], U32, name="o_codes", align_bytes=64)
         o_plane = keep.tile([P, T], U8, name="o_plane", align_bytes=64)
@@ -151,16 +159,13 @@ def tile_picked_whuber_none_lo_kernel(
         banks = ((2, 3), (4, 5), (6, 7), (2, 3), (4, 5), (6, 7))
         last = len(units) - 1
         clipped = [keep.tile([P, 2 * D * P], F32, name="clipped%d" % n) for n in range(len(units))]
-        pieces = [keep.tile([P, (D + 1) * half], F32, name="pieces%d" % n) for n in range(len(units))]
+        pieces = [keep.tile([P, D, T], F32, name="pieces%d" % t) for t in range(PACK)]
 
         def picked(n, d):
-            if n in (1, last - 1) and d == D - 1:
-                return res[1][:, min(n - 1, 1), :]
-            at = d * half + (P if d == D - 1 else 0)
-            return pieces[n][:, at : at + half]
-
-        def behind(n, i):
-            return pieces[n][:, (D - 1 + i) * half : (D + i) * half]
+            t, h = units[n]
+            if (n, d) == (1, D - 1):
+                return res[1][:, 0, :]
+            return pieces[t][:, d, h * half : (h + 1) * half]
 
         res = [keep.tile([P, PACK, half], F32, name="res%d" % h) for h in range(2)]
         pulls = {}
@@ -169,24 +174,29 @@ def tile_picked_whuber_none_lo_kernel(
         def offsets(d, v, count):
             return lists[d][:, v * P // 16 : (v + count) * P // 16]
 
-        def open_unit(n):
+        def seed(n, e):
             t, h = units[n]
-            pulls[n] = [bank(banks[n][e], "pull%d_%d" % (n, e)) for e in range(2)]
-            for e in range(2):
-                v = 2 * h + e
-                for d in range(D):
-                    turn_into(pulls[n][e][:, d, :], y_win[t][:, v * P : (v + 1) * P], d == 0, False)
+            v = 2 * h + e
+            pulls[n, e] = bank(banks[n][e], "pull%d_%d" % (n, e))
+            for d in range(D):
+                turn_into(pulls[n, e][:, d, :], y_win[t][:, v * P : (v + 1) * P], d == 0, False)
 
-        def gather(n, d, first, count):
-            t, h = units[n]
-            target = picked(n, d)[:, first * P : (first + count) * P]
-            nc.scalar.activation(target, y_win[t][:].indirect(offsets(d, 2 * h + first, count)), ACT.Copy, scale=-1.0)
-            for e in range(first, first + count):
-                turn_into(pulls[n][e][:, d, :], picked(n, d)[:, e * P : (e + 1) * P], False, d == D - 1)
+        def open_unit(n):
+            for e in range(2):
+                seed(n, e)
+
+        def fetch(target, t, d, v, count):
+            nc.scalar.activation(target, y_win[t][:].indirect(offsets(d, v, count)), ACT.Copy, scale=-1.0)
+
+        def turn(n, d):
+            for e in range(2):
+                turn_into(pulls[n, e][:, d, :], picked(n, d)[:, e * P : (e + 1) * P], False, d == D - 1)
 
         def last_gather(d, e, target, stop):
             t, h = units[last]
-            part = picked(last, d)[:, e * P : (e + 1) * P]
+            part = limited(last - 2, d // 2)[:, d, :] if e else picked(last, d)[:, 0:P]
+            if (e, d) == (0, D - 1):
+                part = res[1][:, 1, 0:P]
             nc.scalar.activation(part, y_win[t][:].indirect(offsets(d, 2 * h + e, 1)), ACT.Copy, scale=-1.0)
             turn_into(target, part, False, stop)
 
@@ -197,21 +207,24 @@ def tile_picked_whuber_none_lo_kernel(
             for i in range(len(ds)):
                 turn_into(target, view[:, i, :], start and i == 0, stop and i == len(ds) - 1)
 
-        def scalar_unit(n):
-            for d in range(D):
-                gather(n, d, 0, 2)
+        def scalar_unit(n, ds=range(D)):
+            for d in ds:
+                fetch(picked(n, d), units[n][0], d, 2 * units[n][1], 2)
+                turn(n, d)
 
-        def clip(n, e, target, start, stop):
-            v = 2 * units[n][1] + e
-            view = clipped[n][:, e * D * P : (e + 1) * D * P].rearrange("p (d m) -> p d m", d=D)
-            nc.vector.tensor_scalar(view, pulls[n][e][:], col(b_low, v), col(b_hi, v), ALU.max, ALU.min)
-            for d in range(D):
-                turn_into(target, view[:, d, :], start and d == 0, stop and d == D - 1)
+        def limited(n, e):
+            return clipped[n][:, e * D * P : (e + 1) * D * P].rearrange("p (d m) -> p d m", d=D)
 
         def clips(n):
-            sums[n] = bank((n + 1) % 2, "sums%d" % n)
             for e in range(2):
-                clip(n, e, sums[n][:, e, :], e == 0, e == 1)
+                v = 2 * units[n][1] + e
+                nc.vector.tensor_scalar(limited(n, e), pulls[n, e][:], col(b_low, v), col(b_hi, v), ALU.max, ALU.min)
+
+        def add_up(n, e):
+            if e == 0:
+                sums[n] = bank((n + 1) % 2, "sums%d" % n)
+            for d in range(D):
+                turn_into(sums[n][:, e, :], limited(n, e)[:, d, :], (e, d) == (0, 0), (e, d) == (1, D - 1))
 
         def finish(n, first, count, total):
             t, h = units[n]
@@ -232,29 +245,32 @@ def tile_picked_whuber_none_lo_kernel(
             finish(n, 0, 2, sums[n][:, 0:2, :].rearrange("p a b -> p (a b)"))
             store(*units[n])
 
-        own = keep.tile([P, D, half], F32, name="own")
         below = {
-            0: own[:].rearrange("p d v -> p (d v)"),
-            1: pieces[0][:, (D - 1) * half : (D + 1) * half],
-            2: clipped[0][:, 0 : 2 * half],
+            0: [own[i][:].rearrange("p d v -> p (d v)") for i in range(2)],
+            1: [clipped[0][:, 0:T], clipped[0][:, T : 2 * T]],
         }
-        held = {0: keep.tile([P, D, half], F32, name="held0")[:], 1: clipped[1][:].rearrange("p (d v) -> p d v", d=D)}
+        held = {
+            0: [keep.tile([P, 2, half], F32, name="held%d" % i)[:] for i in range(2)],
+            1: [pieces[2][:, 0, :].rearrange("p (d v) -> p d v", d=2), pieces[2][:, 1, :].rearrange("p (d v) -> p d v", d=2)],
+        }
         pair = {t: keep.tile([P, 2, half], F32, name="pair%d" % t) for t in (0, 1)}
-        total = {0: own[:, 1, :], 1: own[:, 0, :]}
+        total = {t: keep.tile([P, half], F32, name="total%d" % t)[:] for t in (0, 1)}
 
         def lowered(t, first, count):
-            at = first if t == 0 else first % 2
-            return below[t + (first // 2 if t else 0)][:, at * half : (at + count) * half]
+            return below[t][first // 2][:, first % 2 * half : (first % 2 + count) * half]
+
+        def bring_out(t):
+            nc.vector.tensor_copy(out=y_win[t][:, 0:T], in_=later[t])
 
         def lift(t):
-            nc.vector.tensor_tensor(y_up[t][:], y_win[t][:, half:T], b_wide[:], ALU.add)
+            nc.gpsimd.tensor_tensor(y_up[t], y_win[t][:, half:T], b_wide[:], ALU.add)
 
         def own_gather(t, d):
-            nc.vector.tensor_tensor(lowered(t, d, 1), y_win[t][:].indirect(offsets(d, 2, 2)), y_up[t][:], ALU.subtract)
+            nc.vector.tensor_tensor(lowered(t, d, 1), y_win[t][:].indirect(offsets(d, 2, 2)), y_up[t], ALU.subtract)
 
         def own_clip(t, first, count):
             nc.vector.scalar_tensor_tensor(
-                held[t][:, first : first + count, :],
+                held[t][first // 2],
                 lowered(t, first, count).rearrange("p (d v) -> p d v", d=count),
                 0.0,
                 floor[:].unsqueeze(1).to_broadcast([P, count, half]),
@@ -263,13 +279,13 @@ def tile_picked_whuber_none_lo_kernel(
             )
 
         def own_pairs(t):
-            nc.gpsimd.tensor_tensor(pair[t][:], held[t][:, 0:2, :], held[t][:, 2:D, :], ALU.add)
+            nc.gpsimd.tensor_tensor(pair[t][:], held[t][0], held[t][1], ALU.add)
 
         def own_total(t):
             nc.gpsimd.tensor_tensor(total[t], pair[t][:, 0, :], pair[t][:, 1, :], ALU.add)
 
         def own_finish(t):
-            nc.vector.scalar_tensor_tensor(res[1][:, t, :], total[t], 1.0 / D, y_up[t][:], ALU.mult, ALU.add)
+            nc.vector.scalar_tensor_tensor(res[1][:, t, :], total[t], 1.0 / D, y_up[t], ALU.mult, ALU.add)
             store(t, 1)
 
         rounded = keep.tile([P, blocks, P, PACK], BF16, name="rounded", align_bytes=64)
@@ -281,6 +297,9 @@ def tile_picked_whuber_none_lo_kernel(
                 in_=res[h][:, :, first * P : (first + count) * P].rearrange("p t (c i) -> p c t i", i=4),
             )
 
+        def scaled_copy(out, in_):
+            nc.gpsimd.tensor_scalar(out, in_, 1.0, 0.0, ALU.mult, ALU.add)
+
         def hand_on(v, count):
             cols = slice(v * P, (v + count) * P)
             nc.vector.quantize_mx(
@@ -288,81 +307,109 @@ def tile_picked_whuber_none_lo_kernel(
                 scales=o_plane[:, cols],
                 in_=rounded[:, v : v + count].rearrange("p b v t -> p (b v t)"),
             )
-
-        def store_words(h):
-            cols = slice(h * half, (h + 1) * half)
             nc.sync.dma_start(out=out_words[:, cols], in_=o_codes[:, cols].bitcast(I32))
 
-        own_gather(0, 0)
         quantise(2, 2, places(0, 2))
-        whole_product(2, 7)
-        whole_product(3, 0)
-        for d in range(1, D):
-            own_gather(0, d)
-        nc.scalar.copy(out=y_win[1][:], in_=later[1])
+        own_gather(0, 0)
+        own_gather(0, 1)
+        nc.vector.tensor_copy(out=y_win[1][:, half:T], in_=nexts[1])
+        own_gather(0, 2)
+        own_gather(0, 3)
         open_unit(0)
+        scalar_unit(0, (0, 1))
+        whole_product(2, 7)
+        scalar_unit(0, (2,))
         open_unit(1)
-        scalar_unit(0)
-        lift(1)
-        own_clip(0, 0, D)
-        nc.vector.tensor_copy(out=y_win[2][:], in_=later[2])
-        open_unit(2)
-        scalar_unit(1)
+        scalar_unit(0, (3,))
+        own_clip(0, 0, 2)
+        y_win[2] = keep.tile([P, T + SPARE], F32, name="y_win2", tag="own0")
+        nc.gpsimd.memset(y_win[2][:, T : T + SPARE], 0.0)
+        own_clip(0, 2, 2)
         own_pairs(0)
+        lift(1)
         own_total(0)
-        nc.vector.tensor_copy(out=y_win[3][:], in_=later[3])
+        bring_out(2)
+        scalar_unit(1, (0,))
+        whole_product(3, 0)
+        scalar_unit(1, (1, 2))
+        seed(2, 0)
+        scalar_unit(1, (3,))
         clips(0)
-        own_gather(1, 0)
-        own_gather(1, 1)
-        open_unit(3)
-        scalar_unit(2)
+        add_up(0, 0)
+        add_up(0, 1)
+        seed(2, 1)
+        bring_out(3)
         clips(1)
         finish_unit(0)
-        own_finish(0)
-        own_gather(1, 2)
-        own_gather(1, 3)
-        open_unit(4)
-        scalar_unit(3)
-        clips(2)
+        for d in range(2):
+            fetch(pieces[2][:, d, :], 2, d, 0, blocks)
+            turn(2, d)
+            seed(3, d)
+        add_up(1, 0)
+        add_up(1, 1)
+        for d in range(D):
+            own_gather(1, d)
         finish_unit(1)
+        own_finish(0)
+        for d in range(2, WHOLE):
+            fetch(pieces[2][:, d, :], 2, d, 0, blocks)
+            turn(2, d)
+        scalar_unit(2, range(WHOLE, D))
+        for d in range(2):
+            turn(3, d)
+        for d in range(2, D):
+            seed(4, d - 2)
+            if d < WHOLE:
+                turn(3, d)
+            else:
+                scalar_unit(3, (d,))
+        clips(2)
+        add_up(2, 0)
         own_clip(1, 0, 2)
         own_clip(1, 2, 2)
         own_pairs(1)
         own_total(1)
         parts = [(0, (0, 1, 2, 3), 6), (1, (0, 1, 2), 7), (1, (3,), 3)]
         ends_in = []
+        scalar_unit(4, (0,))
+        add_up(2, 1)
         for e, ds, b in parts[:2]:
             ends_in.append(bank(b, "pull_end%d" % b)[:, 0 : len(ds), :])
             for i in range(len(ds)):
                 turn_into(ends_in[-1][:, i, :], y_win[3][:, (2 + e) * P : (3 + e) * P], i == 0, False)
-        scalar_unit(4)
+            scalar_unit(4, (1 + e,))
         clips(3)
+        finish_unit(2)
+        scalar_unit(4, (3,))
+        add_up(3, 0)
+        add_up(3, 1)
         ends_in.append(bank(3, "pull_end3")[:, 0:1, :])
         turn_into(ends_in[2][:, 0, :], y_win[3][:, 3 * P : T], True, False)
-        finish_unit(2)
-        for i, d in enumerate(parts[0][1]):
-            last_gather(d, 0, ends_in[0][:, i, :], d == D - 1)
         clips(4)
-        for i, d in enumerate(parts[1][1]):
-            last_gather(d, 1, ends_in[1][:, i, :], d == D - 2)
+        for d in range(D):
+            last_gather(d, 0, ends_in[0][:, d, :], d == D - 1)
+        add_up(4, 0)
+        add_up(4, 1)
+        last_gather(0, 1, ends_in[1][:, 0, :], False)
+        last_gather(1, 1, ends_in[1][:, 1, :], False)
+        last_gather(2, 1, ends_in[1][:, 2, :], True)
         last_gather(3, 1, ends_in[2][:, 0, :], True)
-        finish_unit(3)
         ends = [bank(0, "end0"), bank(2, "end1")]
+        finish_unit(3)
         last_clip(0, parts[0][1], ends_in[0], ends[0][:, 0, :], True, True)
         finish_unit(4)
-        own_finish(1)
-        round_into(nc.scalar.copy, 0, 2)
+        round_into(scaled_copy, 0, 1)
+        round_into(nc.scalar.copy, 1, 1)
         last_clip(1, parts[1][1], ends_in[1], ends[1][:, 0, :], True, False)
         last_clip(1, parts[2][1], ends_in[2], ends[1][:, 0, :], False, True)
+        own_finish(1)
         finish(last, 0, 1, ends[0][:, 0, :])
+        round_into(nc.scalar.copy, 2, 1)
         finish(last, 1, 1, ends[1][:, 0, :])
         store(*units[last])
-        round_into(nc.vector.tensor_copy, 2, 1)
         round_into(nc.vector.tensor_copy, 3, 1)
-        hand_on(0, 2)
-        store_words(0)
-        hand_on(2, 2)
-        store_words(1)
+        hand_on(0, 3)
+        hand_on(3, 1)
 
         for q in range(P // QUAD):
             queue = nc.sync if q % 2 == 0 else nc.scalar

@@ -165,6 +165,8 @@ def tile_picked_whuber_none_lo_kernel(
             t, h = units[n]
             if (n, d) == (1, D - 1):
                 return res[1][:, 0, :]
+            if (n, d) == (0, D - 1):
+                return pieces[0][:, d, P : P + half]
             return pieces[t][:, d, h * half : (h + 1) * half]
 
         res = [keep.tile([P, PACK, half], F32, name="res%d" % h) for h in range(2)]
@@ -212,6 +214,10 @@ def tile_picked_whuber_none_lo_kernel(
                 fetch(picked(n, d), units[n][0], d, 2 * units[n][1], 2)
                 turn(n, d)
 
+        def whole_list(d):
+            fetch(pieces[2][:, d, :], 2, d, 0, blocks)
+            turn(2, d)
+
         def limited(n, e):
             return clipped[n][:, e * D * P : (e + 1) * D * P].rearrange("p (d m) -> p d m", d=D)
 
@@ -247,14 +253,14 @@ def tile_picked_whuber_none_lo_kernel(
 
         below = {
             0: [own[i][:].rearrange("p d v -> p (d v)") for i in range(2)],
-            1: [clipped[0][:, 0:T], clipped[0][:, T : 2 * T]],
+            1: [pieces[0][:, D - 1, :], clipped[0][:, 0:T]],
         }
         held = {
             0: [keep.tile([P, 2, half], F32, name="held%d" % i)[:] for i in range(2)],
-            1: [pieces[2][:, 0, :].rearrange("p (d v) -> p d v", d=2), pieces[2][:, 1, :].rearrange("p (d v) -> p d v", d=2)],
+            1: [keep.tile([P, 2, half], F32, name="held2")[:], pieces[2][:, 2, :].rearrange("p (a v) -> p a v", a=2)],
         }
         pair = {t: keep.tile([P, 2, half], F32, name="pair%d" % t) for t in (0, 1)}
-        total = {t: keep.tile([P, half], F32, name="total%d" % t)[:] for t in (0, 1)}
+        total = {0: clipped[0][:, 2 * T - half : 2 * T], 1: keep.tile([P, half], F32, name="total1")[:]}
 
         def lowered(t, first, count):
             return below[t][first // 2][:, first % 2 * half : (first % 2 + count) * half]
@@ -280,6 +286,9 @@ def tile_picked_whuber_none_lo_kernel(
 
         def own_pairs(t):
             nc.gpsimd.tensor_tensor(pair[t][:], held[t][0], held[t][1], ALU.add)
+
+        def own_pair(t, i):
+            nc.gpsimd.tensor_tensor(pair[t][:, i, :], held[t][i][:, 0, :], held[t][i][:, 1, :], ALU.add)
 
         def own_total(t):
             nc.gpsimd.tensor_tensor(total[t], pair[t][:, 0, :], pair[t][:, 1, :], ALU.add)
@@ -316,71 +325,73 @@ def tile_picked_whuber_none_lo_kernel(
         own_gather(0, 2)
         own_gather(0, 3)
         open_unit(0)
-        scalar_unit(0, (0, 1))
+        scalar_unit(0, (0,))
+        seed(1, 0)
+        scalar_unit(0, (1,))
         whole_product(2, 7)
         scalar_unit(0, (2,))
-        open_unit(1)
+        seed(1, 1)
         scalar_unit(0, (3,))
         own_clip(0, 0, 2)
         y_win[2] = keep.tile([P, T + SPARE], F32, name="y_win2", tag="own0")
         nc.gpsimd.memset(y_win[2][:, T : T + SPARE], 0.0)
         own_clip(0, 2, 2)
-        own_pairs(0)
         lift(1)
-        own_total(0)
+        own_pairs(0)
         bring_out(2)
         scalar_unit(1, (0,))
         whole_product(3, 0)
         scalar_unit(1, (1, 2))
         seed(2, 0)
         scalar_unit(1, (3,))
-        clips(0)
-        add_up(0, 0)
-        add_up(0, 1)
         seed(2, 1)
+        clips(0)
         bring_out(3)
+        own_gather(1, 0)
+        own_gather(1, 1)
         clips(1)
+        add_up(0, 0)
+        whole_list(0)
+        add_up(0, 1)
+        own_total(0)
         finish_unit(0)
-        for d in range(2):
-            fetch(pieces[2][:, d, :], 2, d, 0, blocks)
-            turn(2, d)
-            seed(3, d)
+        seed(3, 0)
+        whole_list(1)
+        seed(3, 1)
+        turn(3, 0)
+        turn(3, 1)
         add_up(1, 0)
-        add_up(1, 1)
-        for d in range(D):
-            own_gather(1, d)
-        finish_unit(1)
+        own_gather(1, 2)
+        own_gather(1, 3)
+        own_clip(1, 0, 2)
         own_finish(0)
-        for d in range(2, WHOLE):
-            fetch(pieces[2][:, d, :], 2, d, 0, blocks)
-            turn(2, d)
-        scalar_unit(2, range(WHOLE, D))
-        for d in range(2):
-            turn(3, d)
-        for d in range(2, D):
-            seed(4, d - 2)
-            if d < WHOLE:
-                turn(3, d)
-            else:
-                scalar_unit(3, (d,))
+        whole_list(2)
+        add_up(1, 1)
+        finish_unit(1)
+        scalar_unit(2, (3,))
+        turn(3, 2)
+        scalar_unit(3, (3,))
+        open_unit(4)
+        scalar_unit(4, (0,))
         clips(2)
         add_up(2, 0)
-        own_clip(1, 0, 2)
+        own_pair(1, 0)
         own_clip(1, 2, 2)
-        own_pairs(1)
+        own_pair(1, 1)
         own_total(1)
         parts = [(0, (0, 1, 2, 3), 6), (1, (0, 1, 2), 7), (1, (3,), 3)]
         ends_in = []
-        scalar_unit(4, (0,))
+        scalar_unit(4, (1,))
         add_up(2, 1)
+        scalar_unit(4, (2,))
         for e, ds, b in parts[:2]:
             ends_in.append(bank(b, "pull_end%d" % b)[:, 0 : len(ds), :])
             for i in range(len(ds)):
                 turn_into(ends_in[-1][:, i, :], y_win[3][:, (2 + e) * P : (3 + e) * P], i == 0, False)
-            scalar_unit(4, (1 + e,))
+            if e == 0:
+                scalar_unit(4, (3,))
         clips(3)
         finish_unit(2)
-        scalar_unit(4, (3,))
         add_up(3, 0)
         add_up(3, 1)
         ends_in.append(bank(3, "pull_end3")[:, 0:1, :])

@@ -161,12 +161,16 @@ def tile_picked_whuber_none_lo_kernel(
         clipped = [keep.tile([P, 2 * D * P], F32, name="clipped%d" % n) for n in range(len(units))]
         pieces = [keep.tile([P, D, T], F32, name="pieces%d" % t) for t in range(PACK)]
 
+        strip = keep.tile([P, 3 * half], F32, name="strip")
+
         def picked(n, d):
             t, h = units[n]
             if (n, d) == (1, D - 1):
                 return res[1][:, 0, :]
             if (n, d) == (0, D - 1):
-                return pieces[0][:, d, P : P + half]
+                return strip[:, P : P + half]
+            if (n, d) == (1, D - 2):
+                return strip[:, T : T + half]
             return pieces[t][:, d, h * half : (h + 1) * half]
 
         res = [keep.tile([P, PACK, half], F32, name="res%d" % h) for h in range(2)]
@@ -221,8 +225,8 @@ def tile_picked_whuber_none_lo_kernel(
         def limited(n, e):
             return clipped[n][:, e * D * P : (e + 1) * D * P].rearrange("p (d m) -> p d m", d=D)
 
-        def clips(n):
-            for e in range(2):
+        def clips(n, es=range(2)):
+            for e in es:
                 v = 2 * units[n][1] + e
                 nc.vector.tensor_scalar(limited(n, e), pulls[n, e][:], col(b_low, v), col(b_hi, v), ALU.max, ALU.min)
 
@@ -253,14 +257,14 @@ def tile_picked_whuber_none_lo_kernel(
 
         below = {
             0: [own[i][:].rearrange("p d v -> p (d v)") for i in range(2)],
-            1: [pieces[0][:, D - 1, :], clipped[0][:, 0:T]],
+            1: [strip[:, 0:T], strip[:, half : half + T]],
         }
         held = {
             0: [keep.tile([P, 2, half], F32, name="held%d" % i)[:] for i in range(2)],
             1: [keep.tile([P, 2, half], F32, name="held2")[:], pieces[2][:, 2, :].rearrange("p (a v) -> p a v", a=2)],
         }
-        pair = {t: keep.tile([P, 2, half], F32, name="pair%d" % t) for t in (0, 1)}
-        total = {0: clipped[0][:, 2 * T - half : 2 * T], 1: keep.tile([P, half], F32, name="total1")[:]}
+        pair = keep.tile([P, 3, half], F32, name="pair")
+        total = {0: strip[:, 0:half], 1: keep.tile([P, half], F32, name="total1")[:]}
 
         def lowered(t, first, count):
             return below[t][first // 2][:, first % 2 * half : (first % 2 + count) * half]
@@ -285,13 +289,13 @@ def tile_picked_whuber_none_lo_kernel(
             )
 
         def own_pairs(t):
-            nc.gpsimd.tensor_tensor(pair[t][:], held[t][0], held[t][1], ALU.add)
+            nc.gpsimd.tensor_tensor(pair[:, 0:2, :], held[t][0], held[t][1], ALU.add)
 
         def own_pair(t, i):
-            nc.gpsimd.tensor_tensor(pair[t][:, i, :], held[t][i][:, 0, :], held[t][i][:, 1, :], ALU.add)
+            nc.gpsimd.tensor_tensor((total[0], pair[:, 2, :])[i], held[t][i][:, 0, :], held[t][i][:, 1, :], ALU.add)
 
         def own_total(t):
-            nc.gpsimd.tensor_tensor(total[t], pair[t][:, 0, :], pair[t][:, 1, :], ALU.add)
+            nc.gpsimd.tensor_tensor(total[t], (pair[:, 0, :], total[0])[t], pair[:, 1 + t, :], ALU.add)
 
         def own_finish(t):
             nc.vector.scalar_tensor_tensor(res[1][:, t, :], total[t], 1.0 / D, y_up[t], ALU.mult, ALU.add)
@@ -325,13 +329,10 @@ def tile_picked_whuber_none_lo_kernel(
         own_gather(0, 2)
         own_gather(0, 3)
         open_unit(0)
-        scalar_unit(0, (0,))
-        seed(1, 0)
-        scalar_unit(0, (1,))
         whole_product(2, 7)
-        scalar_unit(0, (2,))
-        seed(1, 1)
-        scalar_unit(0, (3,))
+        whole_product(3, 0)
+        open_unit(1)
+        scalar_unit(0)
         own_clip(0, 0, 2)
         y_win[2] = keep.tile([P, T + SPARE], F32, name="y_win2", tag="own0")
         nc.gpsimd.memset(y_win[2][:, T : T + SPARE], 0.0)
@@ -339,57 +340,49 @@ def tile_picked_whuber_none_lo_kernel(
         lift(1)
         own_pairs(0)
         bring_out(2)
-        scalar_unit(1, (0,))
-        whole_product(3, 0)
-        scalar_unit(1, (1, 2))
-        seed(2, 0)
-        scalar_unit(1, (3,))
-        seed(2, 1)
-        clips(0)
         bring_out(3)
+        open_unit(2)
+        scalar_unit(1)
+        clips(0)
+        add_up(0, 0)
+        add_up(0, 1)
         own_gather(1, 0)
         own_gather(1, 1)
-        clips(1)
-        add_up(0, 0)
-        whole_list(0)
-        add_up(0, 1)
-        own_total(0)
-        finish_unit(0)
-        seed(3, 0)
-        whole_list(1)
-        seed(3, 1)
-        turn(3, 0)
-        turn(3, 1)
-        add_up(1, 0)
-        own_gather(1, 2)
         own_gather(1, 3)
+        clips(1, (0,))
         own_clip(1, 0, 2)
-        own_finish(0)
-        whole_list(2)
+        own_total(0)
+        clips(1, (1,))
+        finish_unit(0)
+        open_unit(3)
+        for d in range(2):
+            whole_list(d)
+            turn(3, d)
+        add_up(1, 0)
         add_up(1, 1)
+        own_gather(1, 2)
+        own_finish(0)
         finish_unit(1)
+        whole_list(2)
         scalar_unit(2, (3,))
         turn(3, 2)
-        scalar_unit(3, (3,))
         open_unit(4)
-        scalar_unit(4, (0,))
+        scalar_unit(3, (3,))
+        scalar_unit(4, (0, 1))
         clips(2)
         add_up(2, 0)
+        add_up(2, 1)
         own_pair(1, 0)
         own_clip(1, 2, 2)
         own_pair(1, 1)
         own_total(1)
         parts = [(0, (0, 1, 2, 3), 6), (1, (0, 1, 2), 7), (1, (3,), 3)]
         ends_in = []
-        scalar_unit(4, (1,))
-        add_up(2, 1)
-        scalar_unit(4, (2,))
         for e, ds, b in parts[:2]:
             ends_in.append(bank(b, "pull_end%d" % b)[:, 0 : len(ds), :])
             for i in range(len(ds)):
                 turn_into(ends_in[-1][:, i, :], y_win[3][:, (2 + e) * P : (3 + e) * P], i == 0, False)
-            if e == 0:
-                scalar_unit(4, (3,))
+        scalar_unit(4, (2, 3))
         clips(3)
         finish_unit(2)
         add_up(3, 0)

@@ -157,6 +157,7 @@ def tile_picked_whuber_none_lo_kernel(
 
         units = [(0, 0), (1, 0), (2, 0), (2, 1), (3, 0), (3, 1)]
         banks = ((2, 3), (4, 5), (6, 7), (2, 3), (4, 5), (6, 7))
+        sum_banks = (1, 0, 0, 6, 0)
         last = len(units) - 1
         clipped = [keep.tile([P, 2 * D * P], F32, name="clipped%d" % n) for n in range(len(units))]
         pieces = [keep.tile([P, D, T], F32, name="pieces%d" % t) for t in range(PACK)]
@@ -232,7 +233,7 @@ def tile_picked_whuber_none_lo_kernel(
 
         def add_up(n, e):
             if e == 0:
-                sums[n] = bank((n + 1) % 2, "sums%d" % n)
+                sums[n] = bank(sum_banks[n], "sums%d" % n)
             for d in range(D):
                 turn_into(sums[n][:, e, :], limited(n, e)[:, d, :], (e, d) == (0, 0), (e, d) == (1, D - 1))
 
@@ -261,7 +262,7 @@ def tile_picked_whuber_none_lo_kernel(
         }
         held = {
             0: [keep.tile([P, 2, half], F32, name="held%d" % i)[:] for i in range(2)],
-            1: [keep.tile([P, 2, half], F32, name="held2")[:], pieces[2][:, 2, :].rearrange("p (a v) -> p a v", a=2)],
+            1: [keep.tile([P, 2, half], F32, name="held2")[:], pieces[2][:, 3, :].rearrange("p (a v) -> p a v", a=2)],
         }
         pair = keep.tile([P, 3, half], F32, name="pair")
         total = {0: strip[:, 0:half], 1: keep.tile([P, half], F32, name="total1")[:]}
@@ -359,15 +360,25 @@ def tile_picked_whuber_none_lo_kernel(
             whole_list(d)
             turn(3, d)
         add_up(1, 0)
+        whole_list(2)
+        turn(3, 2)
         add_up(1, 1)
         own_gather(1, 2)
         own_finish(0)
         finish_unit(1)
-        whole_list(2)
         scalar_unit(2, (3,))
-        turn(3, 2)
         open_unit(4)
         scalar_unit(3, (3,))
+        parts = [(0, (0, 1, 2, 3), 1), (1, (0, 1, 2), 7), (1, (3,), 3)]
+        ends_in = []
+
+        def open_end(i):
+            e, ds, b = parts[i]
+            ends_in.append(bank(b, "pull_end%d" % b)[:, 0 : len(ds), :])
+            for j in range(len(ds)):
+                turn_into(ends_in[i][:, j, :], y_win[3][:, (2 + e) * P : (3 + e) * P], j == 0, False)
+
+        open_end(0)
         scalar_unit(4, (0, 1))
         clips(2)
         add_up(2, 0)
@@ -376,19 +387,13 @@ def tile_picked_whuber_none_lo_kernel(
         own_clip(1, 2, 2)
         own_pair(1, 1)
         own_total(1)
-        parts = [(0, (0, 1, 2, 3), 6), (1, (0, 1, 2), 7), (1, (3,), 3)]
-        ends_in = []
-        for e, ds, b in parts[:2]:
-            ends_in.append(bank(b, "pull_end%d" % b)[:, 0 : len(ds), :])
-            for i in range(len(ds)):
-                turn_into(ends_in[-1][:, i, :], y_win[3][:, (2 + e) * P : (3 + e) * P], i == 0, False)
+        open_end(1)
         scalar_unit(4, (2, 3))
         clips(3)
         finish_unit(2)
         add_up(3, 0)
         add_up(3, 1)
-        ends_in.append(bank(3, "pull_end3")[:, 0:1, :])
-        turn_into(ends_in[2][:, 0, :], y_win[3][:, 3 * P : T], True, False)
+        open_end(2)
         clips(4)
         for d in range(D):
             last_gather(d, 0, ends_in[0][:, d, :], d == D - 1)
@@ -398,7 +403,7 @@ def tile_picked_whuber_none_lo_kernel(
         last_gather(1, 1, ends_in[1][:, 1, :], False)
         last_gather(2, 1, ends_in[1][:, 2, :], True)
         last_gather(3, 1, ends_in[2][:, 0, :], True)
-        ends = [bank(0, "end0"), bank(2, "end1")]
+        ends = [bank(4, "end0"), bank(2, "end1")]
         finish_unit(3)
         last_clip(0, parts[0][1], ends_in[0], ends[0][:, 0, :], True, True)
         finish_unit(4)

from contextlib import ExitStack

import concourse.mybir as mybir

K, T, N = 512, 512, 512
D = 4
P = 128
PACK = 4
QUAD = 32
SPLIT = 88
SPARE = 16
WHOLE = 3
FLOPS = 2 * K * T * N

F32 = mybir.dt.float32
BF16 = mybir.dt.bfloat16
I32 = mybir.dt.int32
U32 = mybir.dt.uint32
U16 = mybir.dt.uint16
U8 = mybir.dt.uint8
FP8X4 = mybir.dt.float8_e4m3fn_x4
ALU = mybir.AluOpType
ACT = mybir.ActivationFunctionType


def tile_picked_whuber_none_lo_kernel(
    tc, x_words, x_scales, w1, bound, pos1, pos2, pos3, pos4, out_0, out_1, out_2
):
    nc = tc.nc
    blocks = T // P
    half = T // 2

    with ExitStack() as ctx:
        keep = ctx.enter_context(tc.tile_pool(name="keep", bufs=1))
        psum = ctx.enter_context(tc.psum_pool(name="psum", bufs=1))


        def bank(b, name):
            return psum.tile([P, 4, P], F32, name=name, tag="bank%d" % b)

        w_raw = keep.tile([P, PACK, N], F32, name="w_raw")
        nc.sync.dma_start(out=w_raw[:], in_=w1.rearrange("(p j) n -> p j n", j=PACK))
        lists = [keep.tile([P, T // 16], U16, name="list%d" % d) for d in range(D)]

        def load_list(d):
            nc.sync.dma_start(lists[d][:], (pos1, pos2, pos3, pos4)[d])

        load_list(0)
        x_codes = keep.tile([P, T], U32, name="x_codes", align_bytes=64)
        nc.sync.dma_start(
            out=x_codes[:].bitcast(I32),
            in_=x_words[0].rearrange("p c r -> p (c r)").bitcast(I32),
        )
        b_wide = keep.tile([P, half], F32, name="b_wide")
        nc.sync.dma_start(out=b_wide[:], in_=bound[:, half:T])
        x_plane = keep.tile([P, T], U8, name="x_plane", align_bytes=64)
        for q in range(P // QUAD):
            nc.scalar.dma_start(
                out=x_plane[QUAD * q : QUAD * (q + 1), :].bitcast(I32),
                in_=x_scales[0:1, 4 * q : 4 * q + 4, :].bitcast(I32).to_broadcast([QUAD // 4, 4, T // 4]),
            )
        for d in range(1, D):
            load_list(d)
        b_cols = keep.tile([P, 2, 8], F32, name="b_cols")
        b_hi, b_low = (b_cols[:, i, 0:blocks] for i in range(2))
        with nc.allow_non_contiguous_dma(reason="one bound a partition"):
            nc.sync.dma_start(out=b_hi, in_=bound[0:1, :].rearrange("o (c p) -> p (o c)", p=P))

        ident = keep.tile([P, P], F32, name="ident")
        ones = keep.tile([P, P], F32, name="ones")
        along = keep.tile([P, P], F32, name="along", align_bytes=64)
        across = keep.tile([P, P], F32, name="across", align_bytes=64)
        nc.vector.memset(ones[:], 1.0)
        nc.vector.tensor_tensor_scan(along[:], ones[:], ones[:], 0.0, ALU.mult, ALU.add)
        nc.vector.transpose(across[:], along[:])
        for q in range(P // QUAD):
            rows = slice(QUAD * q, QUAD * (q + 1))
            nc.vector.tensor_scalar(
                ident[rows, :], along[rows, :], across[rows, QUAD * q : QUAD * q + 1], None, ALU.is_equal
            )

        def turn_into(target, source, start, stop):
            nc.tensor.matmul(target, lhsT=source, rhs=ident[:], start=start, stop=stop, is_transpose=True)

        def col(cols, v):
            return cols[:, v : v + 1]


        w_src = w_raw[:].rearrange("p j (m t) -> p t m j", t=PACK)
        w_codes = keep.tile([P, N], U32, name="w_codes", align_bytes=64)
        w_plane = keep.tile([P, N], U8, name="w_plane", align_bytes=64)
        w_bf = keep.tile([P, 3 * P * PACK], BF16, name="w_bf", align_bytes=64)

        def places(first, count):
            return w_bf[:, first * P * PACK : (first + count) * P * PACK]

        def round_pair(copy, h, part):
            copy(
                out=places(1 - h, 2).rearrange("p (t m j) -> p m j t", t=2, j=PACK)[:, part],
                in_=w_src[:, 2 * h : 2 * h + 2, part, :].rearrange("p t m j -> p m j t"),
            )

        def quantise(first, count, source):
            cols = slice(first * P, (first + count) * P)
            nc.vector.quantize_mx(out=w_codes[:, cols].bitcast(FP8X4), scales=w_plane[:, cols], in_=source)

        round_pair(nc.vector.tensor_copy, 0, slice(0, SPLIT))
        round_pair(nc.scalar.copy, 0, slice(SPLIT, P))
        for t in range(2):
            quantise(t, 1, places(1 + t, 1))
        round_pair(nc.vector.tensor_copy, 1, slice(0, 64))
        round_pair(nc.scalar.copy, 1, slice(64, P))


        own = [keep.tile([P, 2, half], F32, name="own%d" % i) for i in range(2)]
        y_win = {t: keep.tile([P, T], F32, name="y_win%d" % t) for t in range(2)}
        y_win[3] = keep.tile([P, T], F32, name="y_win3")
        nc.gpsimd.tensor_scalar(b_low, b_hi, -1.0, 0.0, ALU.mult, ALU.add)
        y_up = [keep.tile([P, half], F32, name="y_up0")[:], own[1][:, 0, :]]
        floor = keep.tile([P, half], F32, name="floor")
        nc.scalar.activation(floor[:], b_wide[:], ACT.Copy, scale=-2.0)

        def product(t, target, cols):
            nc.tensor.matmul_mx(
                out=target,
                lhsT=w_codes[:, t * P : (t + 1) * P].bitcast(FP8X4),
                lhsT_scale=w_plane[:, t * P : (t + 1) * P],
                rhs=x_codes[:, cols].bitcast(FP8X4),
                rhs_scale=x_plane[:, cols],
                start=True,
                stop=True,
            )

        def flat(b, name):
            return bank(b, name)[:].rearrange("p a b -> p (a b)")

        halves = [flat(h, "y_half%d" % h)[:, 0:half] for h in range(2)]
        for h, copy in ((1, nc.vector.tensor_copy), (0, nc.scalar.copy)):
            product(0, halves[h], slice(h * half, (h + 1) * half))
            copy(out=y_win[0][:, h * half : (h + 1) * half], in_=halves[h])
        nc.vector.tensor_tensor(y_up[0], halves[1], b_wide[:], ALU.add)
        later = {}

        def whole_product(t, b):
            later[t] = flat(b, "y_ps%d" % t)
            product(t, later[t], slice(0, T))

        nexts = [flat(6 + h, "y_next%d" % h)[:, 0:half] for h in range(2)]
        for h in range(2):
            product(1, nexts[h], slice(h * half, (h + 1) * half))
        nc.scalar.copy(out=y_win[1][:, 0:half], in_=nexts[0])

        o_codes = keep.tile([P, T], U32, name="o_codes", align_bytes=64)
        o_plane = keep.tile([P, T], U8, name="o_plane", align_bytes=64)
        out_rows = out_0.rearrange("(p t) v -> p t v", t=PACK)
        out_words = out_1[0].rearrange("p c r -> p (c r)").bitcast(I32)

        units = [(0, 0), (1, 0), (2, 0), (2, 1), (3, 0), (3, 1)]
        banks = ((2, 3), (4, 5), (6, 7), (2, 3), (4, 5), (6, 7))
        sum_banks = (1, 0, 0, 6, 0)
        last = len(units) - 1
        clipped = [keep.tile([P, 2 * D * P], F32, name="clipped%d" % n) for n in range(len(units))]
        pieces = [keep.tile([P, D, T], F32, name="pieces%d" % t) for t in range(PACK)]

        strip = keep.tile([P, 3 * half], F32, name="strip")

        def picked(n, d):
            t, h = units[n]
            if (n, d) == (1, D - 1):
                return res[1][:, 0, :]
            if (n, d) == (0, D - 1):
                return strip[:, P : P + half]
            if (n, d) == (1, D - 2):
                return strip[:, T : T + half]
            return pieces[t][:, d, h * half : (h + 1) * half]

        res = [keep.tile([P, PACK, half], F32, name="res%d" % h) for h in range(2)]
        pulls = {}
        sums = {}

        def offsets(d, v, count):
            return lists[d][:, v * P // 16 : (v + count) * P // 16]

        def seed(n, e):
            t, h = units[n]
            v = 2 * h + e
            pulls[n, e] = bank(banks[n][e], "pull%d_%d" % (n, e))
            for d in range(D):
                turn_into(pulls[n, e][:, d, :], y_win[t][:, v * P : (v + 1) * P], d == 0, False)

        def open_unit(n):
            for e in range(2):
                seed(n, e)

        def fetch(target, t, d, v, count):
            nc.scalar.activation(target, y_win[t][:].indirect(offsets(d, v, count)), ACT.Copy, scale=-1.0)

        def turn(n, d):
            for e in range(2):
                turn_into(pulls[n, e][:, d, :], picked(n, d)[:, e * P : (e + 1) * P], False, d == D - 1)

        def last_gather(d, e, target, stop):
            t, h = units[last]
            part = limited(last - 2, d // 2)[:, d, :] if e else picked(last, d)[:, 0:P]
            if (e, d) == (0, D - 1):
                part = res[1][:, 1, 0:P]
            nc.scalar.activation(part, y_win[t][:].indirect(offsets(d, 2 * h + e, 1)), ACT.Copy, scale=-1.0)
            turn_into(target, part, False, stop)

        def last_clip(e, ds, source, target, start, stop):
            v = 2 * units[last][1] + e
            view = clipped[last][:, (e * D + ds[0]) * P : (e * D + ds[-1] + 1) * P].rearrange("p (d m) -> p d m", d=len(ds))
            nc.vector.tensor_scalar(view, source, col(b_low, v), col(b_hi, v), ALU.max, ALU.min)
            for i in range(len(ds)):
                turn_into(target, view[:, i, :], start and i == 0, stop and i == len(ds) - 1)

        def scalar_unit(n, ds=range(D)):
            for d in ds:
                fetch(picked(n, d), units[n][0], d, 2 * units[n][1], 2)
                turn(n, d)

        def whole_list(d):
            fetch(pieces[2][:, d, :], 2, d, 0, blocks)
            turn(2, d)

        def limited(n, e):
            return clipped[n][:, e * D * P : (e + 1) * D * P].rearrange("p (d m) -> p d m", d=D)

        def clips(n, es=range(2)):
            for e in es:
                v = 2 * units[n][1] + e
                nc.vector.tensor_scalar(limited(n, e), pulls[n, e][:], col(b_low, v), col(b_hi, v), ALU.max, ALU.min)

        def add_up(n, e):
            if e == 0:
                sums[n] = bank(sum_banks[n], "sums%d" % n)
            for d in range(D):
                turn_into(sums[n][:, e, :], limited(n, e)[:, d, :], (e, d) == (0, 0), (e, d) == (1, D - 1))

        def finish(n, first, count, total):
            t, h = units[n]
            v = 2 * h + first
            nc.vector.scalar_tensor_tensor(
                res[h][:, t, first * P : (first + count) * P],
                total,
                -1.0 / D,
                y_win[t][:, v * P : (v + count) * P],
                ALU.mult,
                ALU.add,
            )

        def store(t, h):
            nc.sync.dma_start(out=out_rows[:, t, h * half : (h + 1) * half], in_=res[h][:, t, :])

        def finish_unit(n):
            finish(n, 0, 2, sums[n][:, 0:2, :].rearrange("p a b -> p (a b)"))
            store(*units[n])

        below = {
            0: [own[i][:].rearrange("p d v -> p (d v)") for i in range(2)],
            1: [strip[:, 0:T], strip[:, half : half + T]],
        }
        held = {
            0: [keep.tile([P, 2, half], F32, name="held%d" % i)[:] for i in range(2)],
            1: [keep.tile([P, 2, half], F32, name="held2")[:], pieces[2][:, 3, :].rearrange("p (a v) -> p a v", a=2)],
        }
        pair = keep.tile([P, 3, half], F32, name="pair")
        total = {0: strip[:, 0:half], 1: keep.tile([P, half], F32, name="total1")[:]}

        def lowered(t, first, count):
            return below[t][first // 2][:, first % 2 * half : (first % 2 + count) * half]

        def bring_out(t):
            nc.vector.tensor_copy(out=y_win[t][:, 0:T], in_=later[t])

        def lift(t):
            nc.gpsimd.tensor_tensor(y_up[t], y_win[t][:, half:T], b_wide[:], ALU.add)

        def own_gather(t, d):
            nc.vector.tensor_tensor(lowered(t, d, 1), y_win[t][:].indirect(offsets(d, 2, 2)), y_up[t], ALU.subtract)

        def own_clip(t, first, count):
            nc.vector.scalar_tensor_tensor(
                held[t][first // 2],
                lowered(t, first, count).rearrange("p (d v) -> p d v", d=count),
                0.0,
                floor[:].unsqueeze(1).to_broadcast([P, count, half]),
                ALU.min,
                ALU.max,
            )

        def own_pairs(t):
            nc.gpsimd.tensor_tensor(pair[:, 0:2, :], held[t][0], held[t][1], ALU.add)

        def own_pair(t, i):
            nc.gpsimd.tensor_tensor((total[0], pair[:, 2, :])[i], held[t][i][:, 0, :], held[t][i][:, 1, :], ALU.add)

        def own_total(t):
            nc.gpsimd.tensor_tensor(total[t], (pair[:, 0, :], total[0])[t], pair[:, 1 + t, :], ALU.add)

        def own_finish(t):
            nc.vector.scalar_tensor_tensor(res[1][:, t, :], total[t], 1.0 / D, y_up[t], ALU.mult, ALU.add)
            store(t, 1)

        rounded = keep.tile([P, blocks, P, PACK], BF16, name="rounded", align_bytes=64)

        def round_into(copy, v, count):
            h, first = divmod(v, 2)
            copy(
                out=rounded[:, v : v + count].rearrange("p b (c i) t -> p (b c) t i", i=4),
                in_=res[h][:, :, first * P : (first + count) * P].rearrange("p t (c i) -> p c t i", i=4),
            )

        def scaled_copy(out, in_):
            nc.gpsimd.tensor_scalar(out, in_, 1.0, 0.0, ALU.mult, ALU.add)

        def hand_on(v, count):
            cols = slice(v * P, (v + count) * P)
            nc.vector.quantize_mx(
                out=o_codes[:, cols].bitcast(FP8X4),
                scales=o_plane[:, cols],
                in_=rounded[:, v : v + count].rearrange("p b v t -> p (b v t)"),
            )
            nc.sync.dma_start(out=out_words[:, cols], in_=o_codes[:, cols].bitcast(I32))

        quantise(2, 2, places(0, 2))
        own_gather(0, 0)
        own_gather(0, 1)
        nc.vector.tensor_copy(out=y_win[1][:, half:T], in_=nexts[1])
        own_gather(0, 2)
        own_gather(0, 3)
        open_unit(0)
        whole_product(2, 7)
        whole_product(3, 0)
        open_unit(1)
        scalar_unit(0)
        own_clip(0, 0, 2)
        y_win[2] = keep.tile([P, T + SPARE], F32, name="y_win2", tag="own0")
        nc.gpsimd.memset(y_win[2][:, T : T + SPARE], 0.0)
        own_clip(0, 2, 2)
        lift(1)
        own_pairs(0)
        bring_out(2)
        bring_out(3)
        open_unit(2)
        scalar_unit(1)
        clips(0)
        add_up(0, 0)
        add_up(0, 1)
        own_gather(1, 0)
        own_gather(1, 1)
        own_gather(1, 3)
        clips(1, (0,))
        own_clip(1, 0, 2)
        own_total(0)
        clips(1, (1,))
        finish_unit(0)
        open_unit(3)
        for d in range(2):
            whole_list(d)
            turn(3, d)
        add_up(1, 0)
        whole_list(2)
        turn(3, 2)
        add_up(1, 1)
        own_gather(1, 2)
        own_finish(0)
        finish_unit(1)
        scalar_unit(2, (3,))
        open_unit(4)
        scalar_unit(3, (3,))
        parts = [(0, (0, 1, 2, 3), 1), (1, (0, 1, 2), 7), (1, (3,), 3)]
        ends_in = []

        def open_end(i):
            e, ds, b = parts[i]
            ends_in.append(bank(b, "pull_end%d" % b)[:, 0 : len(ds), :])
            for j in range(len(ds)):
                turn_into(ends_in[i][:, j, :], y_win[3][:, (2 + e) * P : (3 + e) * P], j == 0, False)

        open_end(0)
        scalar_unit(4, (0, 1))
        clips(2)
        add_up(2, 0)
        add_up(2, 1)
        own_pair(1, 0)
        own_clip(1, 2, 2)
        own_pair(1, 1)
        own_total(1)
        open_end(1)
        scalar_unit(4, (2, 3))
        clips(3)
        finish_unit(2)
        add_up(3, 0)
        add_up(3, 1)
        open_end(2)
        clips(4)
        for d in range(D):
            last_gather(d, 0, ends_in[0][:, d, :], d == D - 1)
        add_up(4, 0)
        add_up(4, 1)
        last_gather(0, 1, ends_in[1][:, 0, :], False)
        last_gather(1, 1, ends_in[1][:, 1, :], False)
        last_gather(2, 1, ends_in[1][:, 2, :], True)
        last_gather(3, 1, ends_in[2][:, 0, :], True)
        ends = [bank(4, "end0"), bank(2, "end1")]
        finish_unit(3)
        last_clip(0, parts[0][1], ends_in[0], ends[0][:, 0, :], True, True)
        finish_unit(4)
        round_into(scaled_copy, 0, 1)
        round_into(nc.scalar.copy, 1, 1)
        last_clip(1, parts[1][1], ends_in[1], ends[1][:, 0, :], True, False)
        last_clip(1, parts[2][1], ends_in[2], ends[1][:, 0, :], False, True)
        own_finish(1)
        finish(last, 0, 1, ends[0][:, 0, :])
        round_into(nc.scalar.copy, 2, 1)
        finish(last, 1, 1, ends[1][:, 0, :])
        store(*units[last])
        round_into(nc.vector.tensor_copy, 3, 1)
        hand_on(0, 3)
        hand_on(3, 1)

        for q in range(P // QUAD):
            queue = nc.sync if q % 2 == 0 else nc.scalar
            queue.dma_start(
                out=out_2[0, 4 * q : 4 * q + 4, :].bitcast(I32),
                in_=o_plane[QUAD * q : QUAD * q + 4, :].bitcast(I32),
            )
